import numpy as np
import ml_dtypes


def mxq(x, axis, fmt="e4m3"):
    dtype, down = {"e4m3": (ml_dtypes.float8_e4m3fn, 7), "e5m2": (ml_dtypes.float8_e5m2, 14)}[fmt]
    v = np.moveaxis(np.asarray(x, np.float32).astype(ml_dtypes.bfloat16).astype(np.float64), axis, -1)
    blocks = v.reshape(v.shape[:-1] + (-1, 32))
    amax = np.abs(blocks).max(-1, keepdims=True)
    byte = np.maximum(np.where(amax > 0, np.frexp(amax)[1] - 1 + 127, 0) - down, 1)
    scale = np.exp2(byte - 127.0)
    codes = (blocks / scale).astype(np.float32).astype(dtype).astype(np.float64)
    return np.moveaxis((codes * scale).reshape(v.shape), -1, axis)


WIDE = False


def mx_kscale(k):
    if not WIDE:
        return np.ones(k)
    levels = np.array([10, -10, 5, -5, 0])
    if k % 512:
        return np.exp2(np.random.permutation(np.resize(levels, k // 32))).repeat(32)
    a = np.empty((k // 512, 16))
    for p in range(k // 512):
        a[p, :8] = np.random.permutation(np.resize(levels, 8))
        for g in range(8):
            far = levels[np.abs(levels - a[p, g]) >= 10]
            a[p, g + 8] = far[np.random.randint(len(far))]
    return np.exp2(a.ravel()).repeat(32)


def f64(x):
    return np.asarray(x).astype(np.float64)


def striped(idx):
    return np.tile(idx.reshape(-1, 16).T, (8, 1)).astype(np.uint16)


def unstriped(offs):
    return offs[:16].T.reshape(-1).astype(np.int64)


E2M1 = np.array([0.0, 0.5, 1.0, 1.5, 2.0, 3.0, 4.0, 6.0, -0.0, -0.5, -1.0, -1.5, -2.0, -3.0, -4.0, -6.0])


def pack_weight(w, fmt):
    k, n = w.shape
    w = f64(np.asarray(w, np.float32).astype(ml_dtypes.bfloat16)).reshape(k // 32, 32, n)
    amax = np.abs(w).max(1)
    if fmt == "e4m3":
        byte = np.frexp(amax)[1] - 1 + 127 - 7
    else:
        mant, ex = np.frexp(amax / 6.0)
        byte = np.where(mant > 0.5, ex, ex - 1) + 127
    byte = np.clip(np.where(amax > 0, byte, 1), 1, 254)
    scaled = (w * np.exp2(127.0 - byte)[:, None, :]).reshape(k, n).astype(np.float32)
    by_word = np.ascontiguousarray(scaled.reshape(k // 512, 128, 4, n).transpose(0, 1, 3, 2))
    if fmt == "e4m3":
        words = by_word.astype(ml_dtypes.float8_e4m3fn).view(np.uint8)
    else:
        c = by_word.astype(ml_dtypes.float4_e2m1fn).view(np.uint8) & 0xF
        words = (c[..., 0::2] | (c[..., 1::2] << 4)).reshape(k // 512, 128, 2 * n)
    return np.ascontiguousarray(words), np.ascontiguousarray(byte.astype(np.uint8).reshape(k // 512, 16, n))


def unpack_weight(words, scales, fmt):
    g, _, n = scales.shape
    words = np.ascontiguousarray(words).reshape(g, 128, n, -1)
    if fmt == "e4m3":
        vals = words.view(ml_dtypes.float8_e4m3fn).astype(np.float64)
    else:
        nib = np.empty((g, 128, n, 4), np.uint8)
        nib[..., 0::2] = words & 0xF
        nib[..., 1::2] = words >> 4
        vals = E2M1[nib]
    vals = vals * np.repeat(np.exp2(scales.astype(np.float64) - 127.0), 8, axis=1)[..., None]
    return vals.transpose(0, 1, 3, 2).reshape(g * 512, n)


K, T, E, C, N = 512, 1024, 8, 256, 512


def by_expert(wq, xq):
    return np.concatenate([wq[e].T @ xq[:, e * C:(e + 1) * C] for e in range(E)], axis=1)


def setup_inputs():
    n = np.random.standard_normal
    s = mx_kscale(N)[:, None]
    first = np.random.permutation(np.repeat(np.arange(E), T // E))
    second = (first + 1 + np.random.permutation(np.repeat(np.arange(E - 1), -(-T // (E - 1)))[:T])) % E
    while np.bincount(second, minlength=E).max() != T // E:
        load = np.bincount(second, minlength=E); hi, lo = int(load.argmax()), int(load.argmin())
        t = np.flatnonzero((second == hi) & (first != lo))[0]; second[t] = lo
    slot_token = np.empty(E * C, np.int64); pos = np.empty((2, T), np.int64); fill = np.zeros(E, np.int64)
    place = np.stack([np.random.permutation(C) for _ in range(E)])
    for r, deal in enumerate((first, second)):
        for t in np.random.permutation(T):
            e = deal[t]; j = e * C + place[e, fill[e]]; fill[e] += 1; slot_token[j] = t; pos[r, t] = j
    g = np.random.uniform(0.2, 0.8, T)
    w_slot = np.empty(E * C); w_slot[pos[0]] = g; w_slot[pos[1]] = 1.0 - g
    w = [pack_weight(m, "e2m1") for m in n((E + 1, N, K)) / np.sqrt(N) / s[None]]
    return {
        "dyT": (n((N, T)) * s).astype(np.float32),
        "w_words": np.stack([m[0] for m in w]),
        "w_scales": np.stack([m[1] for m in w]),
        "gate": np.tile(w_slot, (N, 1)).astype(np.float32),
        "offs": striped(slot_token),
        "pos1": striped(pos[0]),
        "pos2": striped(pos[1]),
    }


def reference(dyT, w_words, w_scales, gate, offs, pos1, pos2):
    idx = unstriped(offs)
    w = np.stack([unpack_weight(w_words[e], w_scales[e], "e2m1") for e in range(E + 1)])
    gq = mxq(f64(gate) * f64(dyT)[:, idx], 0, "e4m3")
    wq = w
    ds = wq[E].T @ mxq(f64(dyT), 0, "e4m3")
    dx = by_expert(wq, gq)
    return ds + dx[:, unstriped(pos1)] + dx[:, unstriped(pos2)]

@@ -1,0 +1,242 @@
+from contextlib import ExitStack
+
+import concourse.mybir as mybir
+from concourse.masks import make_identity
+
+K, T, E, C, N = 512, 1024, 8, 256, 512
+S = E * C
+
+F32 = mybir.dt.float32
+BF16 = mybir.dt.bfloat16
+I32 = mybir.dt.int32
+U32 = mybir.dt.uint32
+U16 = mybir.dt.uint16
+U8 = mybir.dt.uint8
+FP8X4 = mybir.dt.float8_e4m3fn_x4
+FP4X4 = mybir.dt.float4_e2m1fn_x4
+MULT = mybir.AluOpType.mult
+ADD = mybir.AluOpType.add
+
+P = 128
+PACK = 4
+BANK = 512
+PER_COL = 16
+
+FLOPS = 2 * N * K * (S + T)
+BYTES = 4 * N * T + (E + 1) * (N * K // 2 + N * K // 32) + 4 * S + 2 * (S + 2 * T) + 4 * K * T
+
+CHUNKS = [(0, 512), (512, 512), (1024, 512), (1536, 384), (1920, 128)]
+SHARED_PIECE = 256
+
+
+def interleave(nc, dst, src):
+    nc.scalar.copy(
+        out=dst.rearrange("p (c i) t -> p c t i", i=4),
+        in_=src.rearrange("p t (c i) -> p c t i", i=4),
+    )
+
+
+def quantize(nc, codes, scales, grouped, width):
+    done = 0
+    for part in (512, 256, 128):
+        if width - done >= part:
+            nc.vector.quantize_mx(
+                out=codes[:, done : done + part].bitcast(FP8X4),
+                scales=scales[:, done : done + part],
+                in_=grouped[:, done : done + part, :].rearrange("p w t -> p (w t)"),
+            )
+            done += part
+    assert done == width
+
+
+def tile_moe_bds_lin_none_kernel(
+    tc, dyT, w_words, w_scales, gate, offs, pos1, pos2, out
+):
+    nc = tc.nc
+    with ExitStack() as ctx:
+        keep = ctx.enter_context(tc.tile_pool(name="keep", bufs=1))
+        ring = ctx.enter_context(tc.tile_pool(name="ring", bufs=2))
+        psum = ctx.enter_context(tc.psum_pool(name="psum", bufs=2))
+
+        offs_sb = keep.tile([P, S // PER_COL], U16, name="offs_sb")
+        pos1_sb = keep.tile([P, T // PER_COL], U16, name="pos1_sb")
+        pos2_sb = keep.tile([P, T // PER_COL], U16, name="pos2_sb")
+        planes = [keep.tile([P, T], F32, name=f"plane{t}") for t in range(PACK)]
+        gates = [keep.tile([P, w], F32, name=f"gate{c}") for c, (s0, w) in enumerate(CHUNKS)]
+        n_shared = T // SHARED_PIECE
+        dy_rows = [keep.tile([P, PACK, SHARED_PIECE], F32, name=f"dy_rows{q}") for q in range(n_shared)]
+        w_sb = [keep.tile([P, 2 * K], U8, name=f"w_sb{e}", align_bytes=64) for e in range(E + 1)]
+        w_sc = keep.tile([P, E + 1, K], U8, name="w_sc", align_bytes=64)
+        ident = keep.tile([P, P], F32, name="ident")
+        dx = [keep.tile([P, S], F32, name=f"dx{m}") for m in range(K // P)]
+        ds_t = [keep.tile([P, K], F32, name=f"ds_t{b}") for b in range(T // P)]
+
+        nc.vector.memset(w_sc[:].bitcast(I32), 0)
+        make_identity(nc, ident[:])
+
+        dy_view = dyT.rearrange("(p t) x -> p t x", t=PACK)
+
+        def load_gate(c):
+            s0, w = CHUNKS[c]
+            nc.sync.dma_start(gates[c][:], gate[0:P, s0 : s0 + w])
+
+        def load_rows(q):
+            nc.sync.dma_start(dy_rows[q][:], dy_view[:, :, q * SHARED_PIECE : (q + 1) * SHARED_PIECE])
+
+        def load_words(e):
+            nc.sync.dma_start(w_sb[e][:].bitcast(I32), w_words[e, 0].bitcast(I32))
+
+        nc.sync.dma_start(offs_sb[:], offs)
+        nc.sync.dma_start(planes[0][:], dy_view[:, 0, :])
+        load_gate(0)
+        for t in range(1, PACK):
+            nc.sync.dma_start(planes[t][:], dy_view[:, t, :])
+        load_gate(1)
+        load_rows(0)
+        load_rows(1)
+        for q in range(4):
+            nc.sync.dma_start(
+                w_sc[32 * q : 32 * q + 4, :, :].bitcast(I32),
+                w_scales[:, 0, 4 * q : 4 * q + 4, :].rearrange("e f k -> f e k").bitcast(I32),
+            )
+        load_words(0)
+        load_words(1)
+        load_gate(2)
+        load_rows(2)
+        load_rows(3)
+        for e in range(2, E + 1):
+            load_words(e)
+        load_gate(3)
+        load_gate(4)
+        nc.sync.dma_start(pos1_sb[:], pos1)
+        nc.sync.dma_start(pos2_sb[:], pos2)
+
+        grouped = {}
+        g_codes = [keep.tile([P, w], U32, name=f"g_codes{c}", align_bytes=64) for c, (s0, w) in enumerate(CHUNKS)]
+        g_scales = [keep.tile([P, w], U8, name=f"g_scales{c}", align_bytes=64) for c, (s0, w) in enumerate(CHUNKS)]
+        y_grouped = [
+            keep.tile([P, SHARED_PIECE, PACK], BF16, name=f"y_grouped{q}", align_bytes=64) for q in range(n_shared)
+        ]
+        y_codes = [keep.tile([P, SHARED_PIECE], U32, name=f"y_codes{q}", align_bytes=64) for q in range(n_shared)]
+        y_scales = [keep.tile([P, SHARED_PIECE], U8, name=f"y_scales{q}", align_bytes=64) for q in range(n_shared)]
+
+        def gather_slots(c):
+            s0, w = CHUNKS[c]
+            g_rows = ring.tile([P, PACK, w], F32, name="g_rows")
+            for t in range(PACK):
+                nc.vector.tensor_tensor(
+                    g_rows[:, t, :],
+                    planes[t][:].indirect(offs_sb[:, s0 // PER_COL : (s0 + w) // PER_COL]),
+                    gates[c][:],
+                    MULT,
+                )
+            grouped[c] = ring.tile([P, w, PACK], BF16, name="g_grouped", align_bytes=64, bufs=3)
+            interleave(nc, grouped[c][:], g_rows[:])
+
+        def expert_products(c, m):
+            s0, w = CHUNKS[c]
+            acc = psum.tile([P, BANK], F32, name="acc", bufs=4)
+            j = s0
+            while j < s0 + w:
+                e = j // C
+                n = min((e + 1) * C, s0 + w) - j
+                nc.tensor.matmul_mx(
+                    out=acc[:, j - s0 : j - s0 + n],
+                    lhsT=w_sb[e][:, 2 * P * m : 2 * P * (m + 1)].bitcast(FP4X4),
+                    lhsT_scale=w_sc[:, e, P * m : P * (m + 1)],
+                    rhs=g_codes[c][:, j - s0 : j - s0 + n].bitcast(FP8X4),
+                    rhs_scale=g_scales[c][:, j - s0 : j - s0 + n],
+                    start=True,
+                    stop=True,
+                )
+                j += n
+            nc.scalar.copy(out=dx[m][:, s0 : s0 + w], in_=acc[:, 0:w])
+
+        def shared_product(b):
+            q, r = divmod(b * P, SHARED_PIECE)
+            acc = psum.tile([P, BANK], F32, name="acc", bufs=4)
+            nc.tensor.matmul_mx(
+                out=acc[:],
+                lhsT=y_codes[q][:, r : r + P].bitcast(FP8X4),
+                lhsT_scale=y_scales[q][:, r : r + P],
+                rhs=w_sb[E][:].bitcast(FP4X4),
+                rhs_scale=w_sc[:, E, :],
+                start=True,
+                stop=True,
+            )
+            nc.scalar.copy(out=ds_t[b][:], in_=acc[:])
+
+        def gather_results(m, t0, w):
+            cols = slice(t0 // PER_COL, (t0 + w) // PER_COL)
+            first = ring.tile([P, w], F32, name="first")
+            nc.vector.tensor_copy(first[:], dx[m][:].indirect(pos1_sb[:, cols]))
+            second = ring.tile([P, w], F32, name="second")
+            nc.vector.tensor_copy(second[:], dx[m][:].indirect(pos2_sb[:, cols]))
+            return first, second
+
+        def add_turned(acc, a, b):
+            nc.tensor.matmul(acc, a, ident[:], start=True, stop=False, is_transpose=True)
+            nc.tensor.matmul(acc, b, ident[:], start=False, stop=True, is_transpose=True)
+
+        def combine_on_tensor(m, t0, w, first, second):
+            for u0 in range(0, w, BANK):
+                uw = min(BANK, w - u0)
+                pair_ps = psum.tile([P, BANK], F32, name="pair_ps")
+                for j in range(0, uw, P):
+                    blk = slice(u0 + j, u0 + j + P)
+                    add_turned(pair_ps[:, j : j + P], first[:, blk], second[:, blk])
+                pair = ring.tile([P, BANK], F32, name="pair", bufs=4)
+                nc.scalar.copy(out=pair[:, 0:uw], in_=pair_ps[:, 0:uw])
+                sum_ps = psum.tile([P, BANK], F32, name="sum_ps")
+                for j in range(0, uw, P):
+                    b = (t0 + u0 + j) // P
+                    add_turned(sum_ps[:, j : j + P], pair[:, j : j + P], ds_t[b][:, P * m : P * (m + 1)])
+                result = ring.tile([P, BANK], F32, name="result", bufs=4)
+                nc.scalar.copy(out=result[:, 0:uw], in_=sum_ps[:, 0:uw])
+                nc.sync.dma_start(out[P * m : P * (m + 1), t0 + u0 : t0 + u0 + uw], result[:, 0:uw])
+
+        last = len(CHUNKS) - 1
+        for c in range(len(CHUNKS)):
+            gather_slots(c)
+            if c > 0:
+                quantize(nc, g_codes[c - 1], g_scales[c - 1], grouped[c - 1], CHUNKS[c - 1][1])
+                expert_products(c - 1, 0)
+        quantize(nc, g_codes[last], g_scales[last], grouped[last], CHUNKS[last][1])
+        expert_products(last, 0)
+        for q in range(n_shared):
+            interleave(nc, y_grouped[q][:], dy_rows[q][:])
+            quantize(nc, y_codes[q], y_scales[q], y_grouped[q], SHARED_PIECE)
+
+        for c in range(len(CHUNKS)):
+            expert_products(c, 1)
+        for b in range(T // P):
+            shared_product(b)
+        for m in range(K // P - 1):
+            first, second = gather_results(m, 0, T)
+            if m + 2 < K // P:
+                for c in range(len(CHUNKS)):
+                    expert_products(c, m + 2)
+            combine_on_tensor(m, 0, T, first, second)
+
+        m = K // P - 1
+        for t0, w in ((0, 512), (512, 256)):
+            first, second = gather_results(m, t0, w)
+            combine_on_tensor(m, t0, w, first, second)
+
+        t0, w = T - SHARED_PIECE, SHARED_PIECE
+        acc = psum.tile([P, BANK], F32, name="acc", bufs=4)
+        nc.tensor.matmul_mx(
+            out=acc[:, 0:w],
+            lhsT=w_sb[E][:, 2 * P * m : 2 * P * (m + 1)].bitcast(FP4X4),
+            lhsT_scale=w_sc[:, E, P * m : P * (m + 1)],
+            rhs=y_codes[n_shared - 1][:].bitcast(FP8X4),
+            rhs_scale=y_scales[n_shared - 1][:],
+            start=True,
+            stop=True,
+        )
+        first, second = gather_results(m, t0, w)
+        partial = keep.tile([P, w], F32, name="partial")
+        nc.vector.tensor_tensor(partial[:], first[:], acc[:, 0:w], ADD)
+        total = keep.tile([P, w], F32, name="total")
+        nc.vector.tensor_tensor(total[:], partial[:], second[:], ADD)
+        nc.sync.dma_start(out[P * m : P * (m + 1), t0 : t0 + w], total[:])

@@ -1,7 +1,6 @@
 from contextlib import ExitStack
 
 import concourse.mybir as mybir
-from concourse.masks import make_identity
 
 K, T, E, C, N = 512, 1024, 8, 256, 512
 S = E * C
@@ -67,12 +66,10 @@ def tile_moe_bds_lin_none_kernel(
         dy_rows = [keep.tile([P, PACK, SHARED_PIECE], F32, name=f"dy_rows{q}") for q in range(n_shared)]
         w_sb = [keep.tile([P, 2 * K], U8, name=f"w_sb{e}", align_bytes=64) for e in range(E + 1)]
         w_sc = keep.tile([P, E + 1, K], U8, name="w_sc", align_bytes=64)
-        ident = keep.tile([P, P], F32, name="ident")
         dx = [keep.tile([P, S], F32, name=f"dx{m}") for m in range(K // P)]
-        ds_t = [keep.tile([P, K], F32, name=f"ds_t{b}") for b in range(T // P)]
+        ds = [keep.tile([P, T], F32, name=f"ds{m}") for m in range(K // P)]
 
         nc.vector.memset(w_sc[:].bitcast(I32), 0)
-        make_identity(nc, ident[:])
 
         dy_view = dyT.rearrange("(p t) x -> p t x", t=PACK)
 
@@ -104,10 +101,12 @@ def tile_moe_bds_lin_none_kernel(
         load_gate(2)
         load_rows(2)
         load_rows(3)
-        for e in range(2, E + 1):
-            load_words(e)
+        load_words(2)
+        load_words(3)
         load_gate(3)
         load_gate(4)
+        for e in range(4, E + 1):
+            load_words(e)
         nc.sync.dma_start(pos1_sb[:], pos1)
         nc.sync.dma_start(pos2_sb[:], pos2)
 
@@ -117,8 +116,8 @@ def tile_moe_bds_lin_none_kernel(
         y_grouped = [
             keep.tile([P, SHARED_PIECE, PACK], BF16, name=f"y_grouped{q}", align_bytes=64) for q in range(n_shared)
         ]
-        y_codes = [keep.tile([P, SHARED_PIECE], U32, name=f"y_codes{q}", align_bytes=64) for q in range(n_shared)]
-        y_scales = [keep.tile([P, SHARED_PIECE], U8, name=f"y_scales{q}", align_bytes=64) for q in range(n_shared)]
+        y_codes = keep.tile([P, T], U32, name="y_codes", align_bytes=64)
+        y_scales = keep.tile([P, T], U8, name="y_scales", align_bytes=64)
 
         def gather_slots(c):
             s0, w = CHUNKS[c]
@@ -133,9 +132,9 @@ def tile_moe_bds_lin_none_kernel(
             grouped[c] = ring.tile([P, w, PACK], BF16, name="g_grouped", align_bytes=64, bufs=3)
             interleave(nc, grouped[c][:], g_rows[:])
 
-        def expert_products(c, m):
+        def expert_matmuls(c, m):
             s0, w = CHUNKS[c]
-            acc = psum.tile([P, BANK], F32, name="acc", bufs=4)
+            acc = psum.tile([P, BANK], F32, name="acc", bufs=8)
             j = s0
             while j < s0 + w:
                 e = j // C
@@ -150,93 +149,90 @@ def tile_moe_bds_lin_none_kernel(
                     stop=True,
                 )
                 j += n
-            nc.scalar.copy(out=dx[m][:, s0 : s0 + w], in_=acc[:, 0:w])
+            return dx[m][:, s0 : s0 + w], acc[:, 0:w]
 
-        def shared_product(b):
-            q, r = divmod(b * P, SHARED_PIECE)
-            acc = psum.tile([P, BANK], F32, name="acc", bufs=4)
+        def shared_matmul(m, t0, w):
+            acc = psum.tile([P, BANK], F32, name="acc", bufs=8)
             nc.tensor.matmul_mx(
-                out=acc[:],
-                lhsT=y_codes[q][:, r : r + P].bitcast(FP8X4),
-                lhsT_scale=y_scales[q][:, r : r + P],
-                rhs=w_sb[E][:].bitcast(FP4X4),
-                rhs_scale=w_sc[:, E, :],
+                out=acc[:, 0:w],
+                lhsT=w_sb[E][:, 2 * P * m : 2 * P * (m + 1)].bitcast(FP4X4),
+                lhsT_scale=w_sc[:, E, P * m : P * (m + 1)],
+                rhs=y_codes[:, t0 : t0 + w].bitcast(FP8X4),
+                rhs_scale=y_scales[:, t0 : t0 + w],
                 start=True,
                 stop=True,
             )
-            nc.scalar.copy(out=ds_t[b][:], in_=acc[:])
+            return ds[m][:, t0 : t0 + w], acc[:, 0:w]
+
+        def empty(jobs):
+            for dst, src in jobs:
+                nc.scalar.copy(out=dst, in_=src)
 
         def gather_results(m, t0, w):
             cols = slice(t0 // PER_COL, (t0 + w) // PER_COL)
-            first = ring.tile([P, w], F32, name="first")
+            first = ring.tile([P, w], F32, name="first", bufs=3)
             nc.vector.tensor_copy(first[:], dx[m][:].indirect(pos1_sb[:, cols]))
-            second = ring.tile([P, w], F32, name="second")
+            second = ring.tile([P, w], F32, name="second", bufs=3)
             nc.vector.tensor_copy(second[:], dx[m][:].indirect(pos2_sb[:, cols]))
             return first, second
 
-        def add_turned(acc, a, b):
-            nc.tensor.matmul(acc, a, ident[:], start=True, stop=False, is_transpose=True)
-            nc.tensor.matmul(acc, b, ident[:], start=False, stop=True, is_transpose=True)
+        def store(m, t0, w, result):
+            nc.sync.dma_start(out[P * m : P * (m + 1), t0 : t0 + w], result)
 
-        def combine_on_tensor(m, t0, w, first, second):
-            for u0 in range(0, w, BANK):
-                uw = min(BANK, w - u0)
-                pair_ps = psum.tile([P, BANK], F32, name="pair_ps")
-                for j in range(0, uw, P):
-                    blk = slice(u0 + j, u0 + j + P)
-                    add_turned(pair_ps[:, j : j + P], first[:, blk], second[:, blk])
-                pair = ring.tile([P, BANK], F32, name="pair", bufs=4)
-                nc.scalar.copy(out=pair[:, 0:uw], in_=pair_ps[:, 0:uw])
-                sum_ps = psum.tile([P, BANK], F32, name="sum_ps")
-                for j in range(0, uw, P):
-                    b = (t0 + u0 + j) // P
-                    add_turned(sum_ps[:, j : j + P], pair[:, j : j + P], ds_t[b][:, P * m : P * (m + 1)])
-                result = ring.tile([P, BANK], F32, name="result", bufs=4)
-                nc.scalar.copy(out=result[:, 0:uw], in_=sum_ps[:, 0:uw])
-                nc.sync.dma_start(out[P * m : P * (m + 1), t0 + u0 : t0 + u0 + uw], result[:, 0:uw])
+        def quantize_chunk(c):
+            quantize(nc, g_codes[c], g_scales[c], grouped[c], CHUNKS[c][1])
 
-        last = len(CHUNKS) - 1
-        for c in range(len(CHUNKS)):
-            gather_slots(c)
-            if c > 0:
-                quantize(nc, g_codes[c - 1], g_scales[c - 1], grouped[c - 1], CHUNKS[c - 1][1])
-                expert_products(c - 1, 0)
-        quantize(nc, g_codes[last], g_scales[last], grouped[last], CHUNKS[last][1])
-        expert_products(last, 0)
-        for q in range(n_shared):
+        def interleave_tokens(q):
             interleave(nc, y_grouped[q][:], dy_rows[q][:])
-            quantize(nc, y_codes[q], y_scales[q], y_grouped[q], SHARED_PIECE)
 
-        for c in range(len(CHUNKS)):
-            expert_products(c, 1)
-        for b in range(T // P):
-            shared_product(b)
-        for m in range(K // P - 1):
-            first, second = gather_results(m, 0, T)
-            if m + 2 < K // P:
-                for c in range(len(CHUNKS)):
-                    expert_products(c, m + 2)
-            combine_on_tensor(m, 0, T, first, second)
+        def quantize_tokens(q):
+            cols = slice(q * SHARED_PIECE, (q + 1) * SHARED_PIECE)
+            quantize(nc, y_codes[:, cols], y_scales[:, cols], y_grouped[q], SHARED_PIECE)
 
-        m = K // P - 1
-        for t0, w in ((0, 512), (512, 256)):
+        def products(pairs):
+            empty([expert_matmuls(c, m) for c, m in pairs])
+
+        gather_slots(0)
+        interleave_tokens(0)
+        interleave_tokens(1)
+        gather_slots(1)
+        quantize_chunk(0)
+        products([(0, 0), (0, 1), (0, 2), (0, 3)])
+        interleave_tokens(2)
+        gather_slots(2)
+        quantize_chunk(1)
+        products([(1, 0)])
+        interleave_tokens(3)
+        products([(1, 1)])
+        gather_slots(3)
+        quantize_chunk(2)
+        products([(2, 0)])
+        gather_slots(4)
+        quantize_chunk(3)
+        products([(2, 1), (3, 0)])
+        quantize_tokens(0)
+        quantize_tokens(1)
+        quantize_chunk(4)
+        products([(4, 0)])
+        quantize_tokens(2)
+        quantize_tokens(3)
+
+        def combine(engine, m, t0, w, shared):
             first, second = gather_results(m, t0, w)
-            combine_on_tensor(m, t0, w, first, second)
+            partial = ring.tile([P, w], F32, name="partial", bufs=3)
+            engine.tensor_tensor(partial[:], first[:], shared, ADD)
+            total = ring.tile([P, w], F32, name="total", bufs=4)
+            engine.tensor_tensor(total[:], partial[:], second[:], ADD)
+            store(m, t0, w, total[:])
 
-        t0, w = T - SHARED_PIECE, SHARED_PIECE
-        acc = psum.tile([P, BANK], F32, name="acc", bufs=4)
-        nc.tensor.matmul_mx(
-            out=acc[:, 0:w],
-            lhsT=w_sb[E][:, 2 * P * m : 2 * P * (m + 1)].bitcast(FP4X4),
-            lhsT_scale=w_sc[:, E, P * m : P * (m + 1)],
-            rhs=y_codes[n_shared - 1][:].bitcast(FP8X4),
-            rhs_scale=y_scales[n_shared - 1][:],
-            start=True,
-            stop=True,
-        )
-        first, second = gather_results(m, t0, w)
-        partial = keep.tile([P, w], F32, name="partial")
-        nc.vector.tensor_tensor(partial[:], first[:], acc[:, 0:w], ADD)
-        total = keep.tile([P, w], F32, name="total")
-        nc.vector.tensor_tensor(total[:], partial[:], second[:], ADD)
-        nc.sync.dma_start(out[P * m : P * (m + 1), t0 : t0 + w], total[:])
+        empty([shared_matmul(0, 0, BANK), shared_matmul(0, BANK, BANK)])
+        products([(3, 1), (4, 1)])
+        empty([shared_matmul(1, 0, BANK), shared_matmul(1, BANK, BANK)])
+        products([(1, 2), (2, 2), (3, 2), (4, 2)])
+        empty([shared_matmul(2, 0, BANK), shared_matmul(2, BANK, BANK)])
+        products([(1, 3), (2, 3), (3, 3), (4, 3)])
+        empty([shared_matmul(3, 0, BANK)])
+        direct = shared_matmul(3, 512, 512)[1]
+        for m, t0, w in ((0,0,T),(1,0,T),(2,0,T),(3,0,512)):
+            combine(nc.gpsimd, m, t0, w, ds[m][:, t0 : t0 + w])
+        combine(nc.vector, 3, 512, 512, direct)

@@ -61,10 +61,10 @@ def tile_moe_bds_lin_none_kernel(
         pos1_sb = keep.tile([P, T // PER_COL], U16, name="pos1_sb")
         pos2_sb = keep.tile([P, T // PER_COL], U16, name="pos2_sb")
         planes = [keep.tile([P, T], F32, name=f"plane{t}") for t in range(PACK)]
-        gates = [keep.tile([P, w], F32, name=f"gate{c}") for c, (s0, w) in enumerate(CHUNKS)]
+        gate_sb = keep.tile([P, S], F32, name="gate_sb")
         n_shared = T // SHARED_PIECE
         dy_rows = [keep.tile([P, PACK, SHARED_PIECE], F32, name=f"dy_rows{q}") for q in range(n_shared)]
-        w_sb = [keep.tile([P, 2 * K], U8, name=f"w_sb{e}", align_bytes=64) for e in range(E + 1)]
+        w_sb = keep.tile([P, E + 1, 2 * K], U8, name="w_sb", align_bytes=64)
         w_sc = keep.tile([P, E + 1, K], U8, name="w_sc", align_bytes=64)
         dx = [keep.tile([P, S], F32, name=f"dx{m}") for m in range(K // P)]
         ds = [keep.tile([P, T], F32, name=f"ds{m}") for m in range(K // P)]
@@ -73,40 +73,35 @@ def tile_moe_bds_lin_none_kernel(
 
         dy_view = dyT.rearrange("(p t) x -> p t x", t=PACK)
 
-        def load_gate(c):
-            s0, w = CHUNKS[c]
-            nc.sync.dma_start(gates[c][:], gate[0:P, s0 : s0 + w])
+        def load_gate(s0, s1):
+            nc.sync.dma_start(gate_sb[:, s0:s1], gate[0:P, s0:s1])
 
         def load_rows(q):
             nc.sync.dma_start(dy_rows[q][:], dy_view[:, :, q * SHARED_PIECE : (q + 1) * SHARED_PIECE])
 
-        def load_words(e):
-            nc.sync.dma_start(w_sb[e][:].bitcast(I32), w_words[e, 0].bitcast(I32))
+        def load_words(e0, e1):
+            nc.sync.dma_start(
+                w_sb[:, e0:e1, :].bitcast(I32), w_words[e0:e1].rearrange("e a p b -> p (e a) b").bitcast(I32)
+            )
 
         nc.sync.dma_start(offs_sb[:], offs)
         nc.sync.dma_start(planes[0][:], dy_view[:, 0, :])
-        load_gate(0)
+        load_gate(0, 512)
         for t in range(1, PACK):
             nc.sync.dma_start(planes[t][:], dy_view[:, t, :])
-        load_gate(1)
+        load_gate(512, 1024)
         load_rows(0)
+        load_gate(1024, S)
         load_rows(1)
+        load_rows(2)
+        load_rows(3)
         for q in range(4):
             nc.sync.dma_start(
                 w_sc[32 * q : 32 * q + 4, :, :].bitcast(I32),
                 w_scales[:, 0, 4 * q : 4 * q + 4, :].rearrange("e f k -> f e k").bitcast(I32),
             )
-        load_words(0)
-        load_words(1)
-        load_gate(2)
-        load_rows(2)
-        load_rows(3)
-        load_words(2)
-        load_words(3)
-        load_gate(3)
-        load_gate(4)
-        for e in range(4, E + 1):
-            load_words(e)
+        load_words(0, 4)
+        load_words(4, E + 1)
         nc.sync.dma_start(pos1_sb[:], pos1)
         nc.sync.dma_start(pos2_sb[:], pos2)
 
@@ -126,7 +121,7 @@ def tile_moe_bds_lin_none_kernel(
                 nc.vector.tensor_tensor(
                     g_rows[:, t, :],
                     planes[t][:].indirect(offs_sb[:, s0 // PER_COL : (s0 + w) // PER_COL]),
-                    gates[c][:],
+                    gate_sb[:, s0 : s0 + w],
                     MULT,
                 )
             grouped[c] = ring.tile([P, w, PACK], BF16, name="g_grouped", align_bytes=64, bufs=3)
@@ -141,7 +136,7 @@ def tile_moe_bds_lin_none_kernel(
                 n = min((e + 1) * C, s0 + w) - j
                 nc.tensor.matmul_mx(
                     out=acc[:, j - s0 : j - s0 + n],
-                    lhsT=w_sb[e][:, 2 * P * m : 2 * P * (m + 1)].bitcast(FP4X4),
+                    lhsT=w_sb[:, e, 2 * P * m : 2 * P * (m + 1)].bitcast(FP4X4),
                     lhsT_scale=w_sc[:, e, P * m : P * (m + 1)],
                     rhs=g_codes[c][:, j - s0 : j - s0 + n].bitcast(FP8X4),
                     rhs_scale=g_scales[c][:, j - s0 : j - s0 + n],
@@ -155,7 +150,7 @@ def tile_moe_bds_lin_none_kernel(
             acc = psum.tile([P, BANK], F32, name="acc", bufs=8)
             nc.tensor.matmul_mx(
                 out=acc[:, 0:w],
-                lhsT=w_sb[E][:, 2 * P * m : 2 * P * (m + 1)].bitcast(FP4X4),
+                lhsT=w_sb[:, E, 2 * P * m : 2 * P * (m + 1)].bitcast(FP4X4),
                 lhsT_scale=w_sc[:, E, P * m : P * (m + 1)],
                 rhs=y_codes[:, t0 : t0 + w].bitcast(FP8X4),
                 rhs_scale=y_scales[:, t0 : t0 + w],
@@ -172,7 +167,7 @@ def tile_moe_bds_lin_none_kernel(
             cols = slice(t0 // PER_COL, (t0 + w) // PER_COL)
             first = ring.tile([P, w], F32, name="first", bufs=3)
             nc.vector.tensor_copy(first[:], dx[m][:].indirect(pos1_sb[:, cols]))
-            second = ring.tile([P, w], F32, name="second", bufs=3)
+            second = ring.tile([P, w], F32, name="second", bufs=4)
             nc.vector.tensor_copy(second[:], dx[m][:].indirect(pos2_sb[:, cols]))
             return first, second
 
@@ -197,23 +192,20 @@ def tile_moe_bds_lin_none_kernel(
         interleave_tokens(1)
         gather_slots(1)
         quantize_chunk(0)
-        products([(0, 0), (0, 1), (0, 2), (0, 3)])
         interleave_tokens(2)
+        interleave_tokens(3)
         gather_slots(2)
         quantize_chunk(1)
-        products([(1, 0)])
-        interleave_tokens(3)
-        products([(1, 1)])
+        products([(0, 0), (1, 0)])
         gather_slots(3)
         quantize_chunk(2)
-        products([(2, 0)])
         gather_slots(4)
-        quantize_chunk(3)
-        products([(2, 1), (3, 0)])
         quantize_tokens(0)
+        quantize_chunk(3)
+        products([(2, 0)])
         quantize_tokens(1)
         quantize_chunk(4)
-        products([(4, 0)])
+        products([(3, 0), (4, 0)])
         quantize_tokens(2)
         quantize_tokens(3)
 
@@ -221,18 +213,33 @@ def tile_moe_bds_lin_none_kernel(
             first, second = gather_results(m, t0, w)
             partial = ring.tile([P, w], F32, name="partial", bufs=3)
             engine.tensor_tensor(partial[:], first[:], shared, ADD)
-            total = ring.tile([P, w], F32, name="total", bufs=4)
+            total = ring.tile([P, w], F32, name="total", bufs=5)
             engine.tensor_tensor(total[:], partial[:], second[:], ADD)
             store(m, t0, w, total[:])
 
-        empty([shared_matmul(0, 0, BANK), shared_matmul(0, BANK, BANK)])
-        products([(3, 1), (4, 1)])
-        empty([shared_matmul(1, 0, BANK), shared_matmul(1, BANK, BANK)])
-        products([(1, 2), (2, 2), (3, 2), (4, 2)])
-        empty([shared_matmul(2, 0, BANK), shared_matmul(2, BANK, BANK)])
-        products([(1, 3), (2, 3), (3, 3), (4, 3)])
-        empty([shared_matmul(3, 0, BANK)])
+        for m in range(K // P):
+            halves = [shared_matmul(m, 0, BANK)]
+            if m + 1 < K // P:
+                halves.append(shared_matmul(m, BANK, BANK))
+            empty(halves)
+            if m + 1 < K // P:
+                products([(c, m + 1) for c in range(len(CHUNKS))])
         direct = shared_matmul(3, 512, 512)[1]
         for m, t0, w in ((0,0,T),(1,0,T),(2,0,T),(3,0,512)):
             combine(nc.gpsimd, m, t0, w, ds[m][:, t0 : t0 + w])
-        combine(nc.vector, 3, 512, 512, direct)
+        m, t0, half = 3, 512, 256
+        first = ring.tile([P, BANK], F32, name="first", bufs=3)
+        nc.vector.tensor_copy(first[:], dx[m][:].indirect(pos1_sb[:, t0 // PER_COL : T // PER_COL]))
+        partial = ring.tile([P, BANK], F32, name="partial", bufs=3)
+        seconds = []
+        for u in (0, half):
+            second = ring.tile([P, half], F32, name="second", bufs=4)
+            cols = slice((t0 + u) // PER_COL, (t0 + u + half) // PER_COL)
+            nc.vector.tensor_copy(second[:], dx[m][:].indirect(pos2_sb[:, cols]))
+            seconds.append(second)
+            if u == 0:
+                nc.vector.tensor_tensor(partial[:], first[:], direct, ADD)
+        for u, second in zip((0, half), seconds):
+            total = ring.tile([P, half], F32, name="total", bufs=5)
+            nc.vector.tensor_tensor(total[:], partial[:, u : u + half], second[:], ADD)
+            store(m, t0 + u, half, total[:])

@@ -1,6 +1,7 @@
 from contextlib import ExitStack
 
 import concourse.mybir as mybir
+from concourse.masks import make_identity
 
 K, T, E, C, N = 512, 1024, 8, 256, 512
 S = E * C
@@ -69,7 +70,9 @@ def tile_moe_bds_lin_none_kernel(
         dx = [keep.tile([P, S], F32, name=f"dx{m}") for m in range(K // P)]
         ds = [keep.tile([P, T], F32, name=f"ds{m}") for m in range(K // P)]
 
+        ident = keep.tile([P, P], F32, name="ident")
         nc.vector.memset(w_sc[:].bitcast(I32), 0)
+        make_identity(nc, ident[:])
 
         dy_view = dyT.rearrange("(p t) x -> p t x", t=PACK)
 
@@ -129,7 +132,7 @@ def tile_moe_bds_lin_none_kernel(
 
         def expert_matmuls(c, m):
             s0, w = CHUNKS[c]
-            acc = psum.tile([P, BANK], F32, name="acc", bufs=8)
+            acc = psum.tile([P, BANK], F32, name="acc", bufs=6)
             j = s0
             while j < s0 + w:
                 e = j // C
@@ -147,7 +150,7 @@ def tile_moe_bds_lin_none_kernel(
             return dx[m][:, s0 : s0 + w], acc[:, 0:w]
 
         def shared_matmul(m, t0, w):
-            acc = psum.tile([P, BANK], F32, name="acc", bufs=8)
+            acc = psum.tile([P, BANK], F32, name="acc", bufs=6)
             nc.tensor.matmul_mx(
                 out=acc[:, 0:w],
                 lhsT=w_sb[:, E, 2 * P * m : 2 * P * (m + 1)].bitcast(FP4X4),
@@ -217,6 +220,24 @@ def tile_moe_bds_lin_none_kernel(
             engine.tensor_tensor(total[:], partial[:], second[:], ADD)
             store(m, t0, w, total[:])
 
+        def combine_on_tensor(m, t0):
+            first, second = gather_results(m, t0, BANK)
+            turned_ps = psum.tile([P, BANK], F32, name="turned_ps", bufs=1)
+            for j in range(0, BANK, P):
+                terms = (ds[m][:, t0 + j : t0 + j + P], first[:, j : j + P], second[:, j : j + P])
+                for r, term in enumerate(terms):
+                    nc.tensor.matmul(
+                        turned_ps[:, j : j + P], term, ident[:], start=(r == 0), stop=(r == 2), is_transpose=True
+                    )
+            turned = ring.tile([P, BANK], F32, name="turned")
+            nc.scalar.copy(out=turned[:], in_=turned_ps[:])
+            back_ps = psum.tile([P, BANK], F32, name="back_ps", bufs=1)
+            for j in range(0, BANK, P):
+                nc.tensor.transpose(back_ps[:, j : j + P], turned[:, j : j + P], ident[:])
+            back = ring.tile([P, BANK], F32, name="back")
+            nc.scalar.copy(out=back[:], in_=back_ps[:])
+            store(m, t0, BANK, back[:])
+
         for m in range(K // P):
             halves = [shared_matmul(m, 0, BANK)]
             if m + 1 < K // P:
@@ -224,9 +245,12 @@ def tile_moe_bds_lin_none_kernel(
             empty(halves)
             if m + 1 < K // P:
                 products([(c, m + 1) for c in range(len(CHUNKS))])
-        direct = shared_matmul(3, 512, 512)[1]
-        for m, t0, w in ((0,0,T),(1,0,T),(2,0,T),(3,0,512)):
-            combine(nc.gpsimd, m, t0, w, ds[m][:, t0 : t0 + w])
+        direct = shared_matmul(3, T - 512, 512)[1]
+        for m, t0, w, on_tensor in [(0,0,T,0),(1,0,T,0),(2,0,512,0),(2,512,512,1),(3,0,512,0)]:
+            if on_tensor:
+                combine_on_tensor(m, t0)
+            else:
+                combine(nc.gpsimd, m, t0, w, ds[m][:, t0 : t0 + w])
         m, t0, half = 3, 512, 256
         first = ring.tile([P, BANK], F32, name="first", bufs=3)
         nc.vector.tensor_copy(first[:], dx[m][:].indirect(pos1_sb[:, t0 // PER_COL : T // PER_COL]))

@@ -1,7 +1,6 @@
 from contextlib import ExitStack
 
 import concourse.mybir as mybir
-from concourse.masks import make_identity
 
 K, T, E, C, N = 512, 1024, 8, 256, 512
 S = E * C
@@ -25,7 +24,9 @@ PER_COL = 16
 FLOPS = 2 * N * K * (S + T)
 BYTES = 4 * N * T + (E + 1) * (N * K // 2 + N * K // 32) + 4 * S + 2 * (S + 2 * T) + 4 * K * T
 
-CHUNKS = [(0, 512), (512, 512), (1024, 512), (1536, 384), (1920, 128)]
+CHUNKS = [(0, 896), (896, 640), (1536, 384), (1920, 128)]
+FIRST_GATE = 256
+LATE = CHUNKS[2][0]
 SHARED_PIECE = 256
 
 
@@ -36,19 +37,6 @@ def interleave(nc, dst, src):
     )
 
 
-def quantize(nc, codes, scales, grouped, width):
-    done = 0
-    for part in (512, 256, 128):
-        if width - done >= part:
-            nc.vector.quantize_mx(
-                out=codes[:, done : done + part].bitcast(FP8X4),
-                scales=scales[:, done : done + part],
-                in_=grouped[:, done : done + part, :].rearrange("p w t -> p (w t)"),
-            )
-            done += part
-    assert done == width
-
-
 def tile_moe_bds_lin_none_kernel(
     tc, dyT, w_words, w_scales, gate, offs, pos1, pos2, out
 ):
@@ -56,7 +44,7 @@ def tile_moe_bds_lin_none_kernel(
     with ExitStack() as ctx:
         keep = ctx.enter_context(tc.tile_pool(name="keep", bufs=1))
         ring = ctx.enter_context(tc.tile_pool(name="ring", bufs=2))
-        psum = ctx.enter_context(tc.psum_pool(name="psum", bufs=2))
+        psum = ctx.enter_context(tc.psum_pool(name="psum", bufs=1))
 
         offs_sb = keep.tile([P, S // PER_COL], U16, name="offs_sb")
         pos1_sb = keep.tile([P, T // PER_COL], U16, name="pos1_sb")
@@ -64,15 +52,25 @@ def tile_moe_bds_lin_none_kernel(
         planes = [keep.tile([P, T], F32, name=f"plane{t}") for t in range(PACK)]
         gate_sb = keep.tile([P, S], F32, name="gate_sb")
         n_shared = T // SHARED_PIECE
-        dy_rows = [keep.tile([P, PACK, SHARED_PIECE], F32, name=f"dy_rows{q}") for q in range(n_shared)]
+        dy_rows = [
+            keep.tile([P, PACK, SHARED_PIECE], F32, name=f"dy_rows{q}", tag=f"dy_rows{q}", align_bytes=64)
+            for q in range(n_shared)
+        ]
         w_sb = keep.tile([P, E + 1, 2 * K], U8, name="w_sb", align_bytes=64)
         w_sc = keep.tile([P, E + 1, K], U8, name="w_sc", align_bytes=64)
         dx = [keep.tile([P, S], F32, name=f"dx{m}") for m in range(K // P)]
         ds = [keep.tile([P, T], F32, name=f"ds{m}") for m in range(K // P)]
+        g_rows = {}
+        w_first = keep.tile([P, 3, 2 * P], U8, name="w_first", tag="held", align_bytes=64)
+        late = {}
+        banks = [psum.tile([P, BANK], F32, name=f"bank{b}") for b in range(8)]
+        g_codes = keep.tile([P, S], U32, name="g_codes", align_bytes=64)
+        g_scales = keep.tile([P, S], U8, name="g_scales", align_bytes=64)
+        y_grouped = keep.tile([P, T * PACK], BF16, name="y_grouped", align_bytes=64)
+        y_codes = {}
+        y_scales = keep.tile([P, T], U8, name="y_scales", align_bytes=64)
 
-        ident = keep.tile([P, P], F32, name="ident")
         nc.vector.memset(w_sc[:].bitcast(I32), 0)
-        make_identity(nc, ident[:])
 
         dy_view = dyT.rearrange("(p t) x -> p t x", t=PACK)
 
@@ -89,181 +87,169 @@ def tile_moe_bds_lin_none_kernel(
 
         nc.sync.dma_start(offs_sb[:], offs)
         nc.sync.dma_start(planes[0][:], dy_view[:, 0, :])
-        load_gate(0, 512)
-        for t in range(1, PACK):
-            nc.sync.dma_start(planes[t][:], dy_view[:, t, :])
-        load_gate(512, 1024)
+        load_gate(0, FIRST_GATE)
+        load_gate(FIRST_GATE, CHUNKS[0][1])
+        nc.sync.dma_start(planes[1][:], dy_view[:, 1, :])
         load_rows(0)
-        load_gate(1024, S)
+        nc.sync.dma_start(planes[2][:], dy_view[:, 2, :])
+        nc.sync.dma_start(planes[3][:], dy_view[:, 3, :])
         load_rows(1)
         load_rows(2)
+        load_gate(CHUNKS[1][0], CHUNKS[2][0])
         load_rows(3)
+        load_gate(CHUNKS[2][0], S)
         for q in range(4):
             nc.sync.dma_start(
                 w_sc[32 * q : 32 * q + 4, :, :].bitcast(I32),
                 w_scales[:, 0, 4 * q : 4 * q + 4, :].rearrange("e f k -> f e k").bitcast(I32),
             )
-        load_words(0, 4)
-        load_words(4, E + 1)
+        words = w_words.rearrange("e a p b -> p (e a) b")
+        load_words(3, E + 1)
+        nc.sync.dma_start(w_first[:].bitcast(I32), words[:, 0:3, 0 : 2 * P].bitcast(I32))
+        nc.sync.dma_start(w_sb[:, 0:3, 2 * P :].bitcast(I32), words[:, 0:3, 2 * P :].bitcast(I32))
         nc.sync.dma_start(pos1_sb[:], pos1)
         nc.sync.dma_start(pos2_sb[:], pos2)
 
-        grouped = {}
-        g_codes = [keep.tile([P, w], U32, name=f"g_codes{c}", align_bytes=64) for c, (s0, w) in enumerate(CHUNKS)]
-        g_scales = [keep.tile([P, w], U8, name=f"g_scales{c}", align_bytes=64) for c, (s0, w) in enumerate(CHUNKS)]
-        y_grouped = [
-            keep.tile([P, SHARED_PIECE, PACK], BF16, name=f"y_grouped{q}", align_bytes=64) for q in range(n_shared)
-        ]
-        y_codes = keep.tile([P, T], U32, name="y_codes", align_bytes=64)
-        y_scales = keep.tile([P, T], U8, name="y_scales", align_bytes=64)
+        def gather_plane(c, t, a, b):
+            s0 = CHUNKS[c][0]
+            nc.vector.tensor_tensor(
+                g_rows[c][:, t, a:b],
+                planes[t][:].indirect(offs_sb[:, (s0 + a) // PER_COL : (s0 + b) // PER_COL]),
+                gate_sb[:, s0 + a : s0 + b],
+                MULT,
+            )
 
         def gather_slots(c):
             s0, w = CHUNKS[c]
-            g_rows = ring.tile([P, PACK, w], F32, name="g_rows")
+            g_rows[c] = ring.tile([P, PACK, w], F32, name="g_rows")
             for t in range(PACK):
-                nc.vector.tensor_tensor(
-                    g_rows[:, t, :],
-                    planes[t][:].indirect(offs_sb[:, s0 // PER_COL : (s0 + w) // PER_COL]),
-                    gate_sb[:, s0 : s0 + w],
-                    MULT,
-                )
-            grouped[c] = ring.tile([P, w, PACK], BF16, name="g_grouped", align_bytes=64, bufs=3)
-            interleave(nc, grouped[c][:], g_rows[:])
+                if c == 0 and t == 0:
+                    gather_plane(c, t, 0, FIRST_GATE)
+                    gather_plane(c, t, FIRST_GATE, w)
+                else:
+                    gather_plane(c, t, 0, w)
 
-        def expert_matmuls(c, m):
-            s0, w = CHUNKS[c]
-            acc = psum.tile([P, BANK], F32, name="acc", bufs=6)
+        def grouped(s0, w):
+            if s0 < LATE:
+                return late["early"][:, PACK * s0 : PACK * (s0 + w)]
+            return late["grouped"][:, PACK * (s0 - LATE) : PACK * (s0 - LATE + w)]
+
+        def interleave_slots(c):
+            interleave(nc, grouped(*CHUNKS[c]).rearrange("p (w t) -> p w t", t=PACK), g_rows[c][:])
+
+        def interleave_tokens(q):
+            t0 = q * SHARED_PIECE
+            dst = y_grouped[:, PACK * t0 : PACK * (t0 + SHARED_PIECE)].rearrange("p (w t) -> p w t", t=PACK)
+            interleave(nc, dst, dy_rows[q][:])
+
+        def quantize_slots(s0, w):
+            nc.vector.quantize_mx(
+                out=g_codes[:, s0 : s0 + w].bitcast(FP8X4),
+                scales=g_scales[:, s0 : s0 + w],
+                in_=grouped(s0, w),
+            )
+
+        def quantize_tokens(t0, w, tag):
+            y_codes[t0] = keep.tile([P, w], U32, name=f"y_codes{t0}", tag=tag, align_bytes=64)
+            nc.vector.quantize_mx(
+                out=y_codes[t0][:].bitcast(FP8X4),
+                scales=y_scales[:, t0 : t0 + w],
+                in_=y_grouped[:, PACK * t0 : PACK * (t0 + w)],
+            )
+
+        def multiply(acc, e, m, codes, scales):
+            weights = w_first[:, e, :] if m == 0 and e < 3 else w_sb[:, e, 2 * P * m : 2 * P * (m + 1)]
+            nc.tensor.matmul_mx(
+                out=acc,
+                lhsT=weights.bitcast(FP4X4),
+                lhsT_scale=w_sc[:, e, P * m : P * (m + 1)],
+                rhs=codes.bitcast(FP8X4),
+                rhs_scale=scales,
+                start=True,
+                stop=True,
+            )
+
+        def expert_products(m, s0, w, b):
+            acc = banks[b]
             j = s0
             while j < s0 + w:
                 e = j // C
                 n = min((e + 1) * C, s0 + w) - j
-                nc.tensor.matmul_mx(
-                    out=acc[:, j - s0 : j - s0 + n],
-                    lhsT=w_sb[:, e, 2 * P * m : 2 * P * (m + 1)].bitcast(FP4X4),
-                    lhsT_scale=w_sc[:, e, P * m : P * (m + 1)],
-                    rhs=g_codes[c][:, j - s0 : j - s0 + n].bitcast(FP8X4),
-                    rhs_scale=g_scales[c][:, j - s0 : j - s0 + n],
-                    start=True,
-                    stop=True,
-                )
+                multiply(acc[:, j - s0 : j - s0 + n], e, m, g_codes[:, j : j + n], g_scales[:, j : j + n])
                 j += n
-            return dx[m][:, s0 : s0 + w], acc[:, 0:w]
+            nc.scalar.copy(out=dx[m][:, s0 : s0 + w], in_=acc[:, 0:w])
 
-        def shared_matmul(m, t0, w):
-            acc = psum.tile([P, BANK], F32, name="acc", bufs=6)
-            nc.tensor.matmul_mx(
-                out=acc[:, 0:w],
-                lhsT=w_sb[:, E, 2 * P * m : 2 * P * (m + 1)].bitcast(FP4X4),
-                lhsT_scale=w_sc[:, E, P * m : P * (m + 1)],
-                rhs=y_codes[:, t0 : t0 + w].bitcast(FP8X4),
-                rhs_scale=y_scales[:, t0 : t0 + w],
-                start=True,
-                stop=True,
-            )
-            return ds[m][:, t0 : t0 + w], acc[:, 0:w]
+        def shared_product(m, parts, b):
+            acc = banks[b]
+            t0 = parts[0][0]
+            for u, w in parts:
+                multiply(acc[:, u - t0 : u - t0 + w], E, m, y_codes[u][:], y_scales[:, u : u + w])
+            t1 = parts[-1][0] + parts[-1][1]
+            nc.scalar.copy(out=ds[m][:, t0:t1], in_=acc[:, 0 : t1 - t0])
 
-        def empty(jobs):
-            for dst, src in jobs:
-                nc.scalar.copy(out=dst, in_=src)
+        firsts = {}
 
-        def gather_results(m, t0, w):
+        def add_first(m, t0, w):
+            first = keep.tile([P, w], F32, name=f"first{m}_{t0}")
             cols = slice(t0 // PER_COL, (t0 + w) // PER_COL)
-            first = ring.tile([P, w], F32, name="first", bufs=3)
-            nc.vector.tensor_copy(first[:], dx[m][:].indirect(pos1_sb[:, cols]))
-            second = ring.tile([P, w], F32, name="second", bufs=4)
-            nc.vector.tensor_copy(second[:], dx[m][:].indirect(pos2_sb[:, cols]))
-            return first, second
+            nc.vector.tensor_tensor(first[:], dx[m][:].indirect(pos1_sb[:, cols]), ds[m][:, t0 : t0 + w], ADD)
+            firsts[m, t0] = first
 
-        def store(m, t0, w, result):
-            nc.sync.dma_start(out[P * m : P * (m + 1), t0 : t0 + w], result)
+        def add_second(m, t0, w, base):
+            total = ring.tile([P, w], F32, name="total", bufs=3)
+            cols = slice(t0 // PER_COL, (t0 + w) // PER_COL)
+            first = firsts[m, base][:, t0 - base : t0 - base + w]
+            nc.vector.tensor_tensor(total[:], dx[m][:].indirect(pos2_sb[:, cols]), first, ADD)
+            nc.sync.dma_start(out[P * m : P * (m + 1), t0 : t0 + w], total[:])
 
-        def quantize_chunk(c):
-            quantize(nc, g_codes[c], g_scales[c], grouped[c], CHUNKS[c][1])
-
-        def interleave_tokens(q):
-            interleave(nc, y_grouped[q][:], dy_rows[q][:])
-
-        def quantize_tokens(q):
-            cols = slice(q * SHARED_PIECE, (q + 1) * SHARED_PIECE)
-            quantize(nc, y_codes[:, cols], y_scales[:, cols], y_grouped[q], SHARED_PIECE)
-
-        def products(pairs):
-            empty([expert_matmuls(c, m) for c, m in pairs])
-
+        for q in range(3):
+            interleave_tokens(q)
+        quantize_tokens(0, 512, "free")
         gather_slots(0)
-        interleave_tokens(0)
-        interleave_tokens(1)
-        gather_slots(1)
-        quantize_chunk(0)
-        interleave_tokens(2)
+        late["early"] = keep.tile([P, LATE * PACK], BF16, name="early_grouped", tag="dy_rows2", align_bytes=64)
+        interleave_slots(0)
         interleave_tokens(3)
+        gather_slots(1)
+        quantize_slots(0, 512)
+        quantize_slots(512, 256)
+        quantize_slots(768, 128)
+        interleave_slots(1)
+        shared_product(0, [(0, 512)], 0)
+        expert_products(0, 0, 512, 4)
+        expert_products(0, 512, 256, 3)
         gather_slots(2)
-        quantize_chunk(1)
-        products([(0, 0), (1, 0)])
+        quantize_slots(896, 128)
+        quantize_slots(1024, 512)
+        late["grouped"] = keep.tile([P, (S - LATE) * PACK], BF16, name="late_grouped", tag="held", align_bytes=64)
+        interleave_slots(2)
+        expert_products(0, 768, 256, 3)
         gather_slots(3)
-        quantize_chunk(2)
-        gather_slots(4)
-        quantize_tokens(0)
-        quantize_chunk(3)
-        products([(2, 0)])
-        quantize_tokens(1)
-        quantize_chunk(4)
-        products([(3, 0), (4, 0)])
-        quantize_tokens(2)
-        quantize_tokens(3)
+        interleave_slots(3)
+        quantize_slots(1536, 256)
+        quantize_slots(1792, 128)
+        expert_products(0, 1024, 512, 4)
+        quantize_slots(1920, 128)
+        expert_products(0, 1536, 384, 6)
+        expert_products(0, 1920, 128, 7)
+        quantize_tokens(512, 512, "held")
 
-        def combine(engine, m, t0, w, shared):
-            first, second = gather_results(m, t0, w)
-            partial = ring.tile([P, w], F32, name="partial", bufs=3)
-            engine.tensor_tensor(partial[:], first[:], shared, ADD)
-            total = ring.tile([P, w], F32, name="total", bufs=5)
-            engine.tensor_tensor(total[:], partial[:], second[:], ADD)
-            store(m, t0, w, total[:])
-
-        def combine_on_tensor(m, t0):
-            first, second = gather_results(m, t0, BANK)
-            turned_ps = psum.tile([P, BANK], F32, name="turned_ps", bufs=1)
-            for j in range(0, BANK, P):
-                terms = (ds[m][:, t0 + j : t0 + j + P], first[:, j : j + P], second[:, j : j + P])
-                for r, term in enumerate(terms):
-                    nc.tensor.matmul(
-                        turned_ps[:, j : j + P], term, ident[:], start=(r == 0), stop=(r == 2), is_transpose=True
-                    )
-            turned = ring.tile([P, BANK], F32, name="turned")
-            nc.scalar.copy(out=turned[:], in_=turned_ps[:])
-            back_ps = psum.tile([P, BANK], F32, name="back_ps", bufs=1)
-            for j in range(0, BANK, P):
-                nc.tensor.transpose(back_ps[:, j : j + P], turned[:, j : j + P], ident[:])
-            back = ring.tile([P, BANK], F32, name="back")
-            nc.scalar.copy(out=back[:], in_=back_ps[:])
-            store(m, t0, BANK, back[:])
-
-        for m in range(K // P):
-            halves = [shared_matmul(m, 0, BANK)]
-            if m + 1 < K // P:
-                halves.append(shared_matmul(m, BANK, BANK))
-            empty(halves)
-            if m + 1 < K // P:
-                products([(c, m + 1) for c in range(len(CHUNKS))])
-        direct = shared_matmul(3, T - 512, 512)[1]
-        for m, t0, w, on_tensor in [(0,0,T,0),(1,0,T,0),(2,0,512,0),(2,512,512,1),(3,0,512,0)]:
-            if on_tensor:
-                combine_on_tensor(m, t0)
+        jobs = [(0, [(512, 512)])]
+        for m in range(1, K // P):
+            jobs += [(m, [(0, 512)]), (m, [(512, 512)])]
+            jobs += [(m, s0) for s0 in range(0, S, BANK)]
+        late_banks = [5, 6, 4, 7]
+        for i, (m, what) in enumerate(jobs):
+            b = late_banks[i % len(late_banks)]
+            if isinstance(what, list):
+                shared_product(m, what, b)
             else:
-                combine(nc.gpsimd, m, t0, w, ds[m][:, t0 : t0 + w])
-        m, t0, half = 3, 512, 256
-        first = ring.tile([P, BANK], F32, name="first", bufs=3)
-        nc.vector.tensor_copy(first[:], dx[m][:].indirect(pos1_sb[:, t0 // PER_COL : T // PER_COL]))
-        partial = ring.tile([P, BANK], F32, name="partial", bufs=3)
-        seconds = []
-        for u in (0, half):
-            second = ring.tile([P, half], F32, name="second", bufs=4)
-            cols = slice((t0 + u) // PER_COL, (t0 + u + half) // PER_COL)
-            nc.vector.tensor_copy(second[:], dx[m][:].indirect(pos2_sb[:, cols]))
-            seconds.append(second)
-            if u == 0:
-                nc.vector.tensor_tensor(partial[:], first[:], direct, ADD)
-        for u, second in zip((0, half), seconds):
-            total = ring.tile([P, half], F32, name="total", bufs=5)
-            nc.vector.tensor_tensor(total[:], partial[:, u : u + half], second[:], ADD)
-            store(m, t0 + u, half, total[:])
+                expert_products(m, what, BANK, b)
+
+        pairs = [((0, 0, 256), (0, 256, 256)), ((0, 512, 256), (0, 768, 256))]
+        pairs += [((m, 0, 512), (m, 512, 512)) for m in (1, 2)]
+        pairs += [((3, 0, 768), (3, 768, 256))]
+        for pair in pairs:
+            for m, t0, w in pair:
+                add_first(m, t0, w)
+            for m, t0, w in pair:
+                add_second(m, t0, w, t0)

@@ -24,8 +24,8 @@ PER_COL = 16
 FLOPS = 2 * N * K * (S + T)
 BYTES = 4 * N * T + (E + 1) * (N * K // 2 + N * K // 32) + 4 * S + 2 * (S + 2 * T) + 4 * K * T
 
-CHUNKS = [(0, 896), (896, 640), (1536, 384), (1920, 128)]
-FIRST_GATE = 256
+CHUNKS = [(0, 992), (992, 544), (1536, 384), (1920, 128)]
+FIRST_GATE = 320
 LATE = CHUNKS[2][0]
 SHARED_PIECE = 256
 
@@ -92,8 +92,8 @@ def tile_moe_bds_lin_none_kernel(
         nc.sync.dma_start(planes[1][:], dy_view[:, 1, :])
         load_rows(0)
         nc.sync.dma_start(planes[2][:], dy_view[:, 2, :])
-        nc.sync.dma_start(planes[3][:], dy_view[:, 3, :])
         load_rows(1)
+        nc.sync.dma_start(planes[3][:], dy_view[:, 3, :])
         load_rows(2)
         load_gate(CHUNKS[1][0], CHUNKS[2][0])
         load_rows(3)
@@ -195,12 +195,12 @@ def tile_moe_bds_lin_none_kernel(
             nc.vector.tensor_tensor(first[:], dx[m][:].indirect(pos1_sb[:, cols]), ds[m][:, t0 : t0 + w], ADD)
             firsts[m, t0] = first
 
-        def add_second(m, t0, w, base):
+        def add_second(m, t0, w, base, queue=nc.sync):
             total = ring.tile([P, w], F32, name="total", bufs=3)
             cols = slice(t0 // PER_COL, (t0 + w) // PER_COL)
             first = firsts[m, base][:, t0 - base : t0 - base + w]
             nc.vector.tensor_tensor(total[:], dx[m][:].indirect(pos2_sb[:, cols]), first, ADD)
-            nc.sync.dma_start(out[P * m : P * (m + 1), t0 : t0 + w], total[:])
+            queue.dma_start(out[P * m : P * (m + 1), t0 : t0 + w], total[:])
 
         for q in range(3):
             interleave_tokens(q)
@@ -212,13 +212,12 @@ def tile_moe_bds_lin_none_kernel(
         gather_slots(1)
         quantize_slots(0, 512)
         quantize_slots(512, 256)
-        quantize_slots(768, 128)
         interleave_slots(1)
         shared_product(0, [(0, 512)], 0)
         expert_products(0, 0, 512, 4)
         expert_products(0, 512, 256, 3)
         gather_slots(2)
-        quantize_slots(896, 128)
+        quantize_slots(768, 256)
         quantize_slots(1024, 512)
         late["grouped"] = keep.tile([P, (S - LATE) * PACK], BF16, name="late_grouped", tag="held", align_bytes=64)
         interleave_slots(2)
@@ -247,9 +246,13 @@ def tile_moe_bds_lin_none_kernel(
 
         pairs = [((0, 0, 256), (0, 256, 256)), ((0, 512, 256), (0, 768, 256))]
         pairs += [((m, 0, 512), (m, 512, 512)) for m in (1, 2)]
-        pairs += [((3, 0, 768), (3, 768, 256))]
         for pair in pairs:
             for m, t0, w in pair:
                 add_first(m, t0, w)
             for m, t0, w in pair:
                 add_second(m, t0, w, t0)
+        add_first(3, 0, 640)
+        add_first(3, 640, 384)
+        add_second(3, 0, 640, 0)
+        add_second(3, 640, 256, 640)
+        add_second(3, 896, 128, 640, nc.scalar)

@@ -25,7 +25,7 @@ FLOPS = 2 * N * K * (S + T)
 BYTES = 4 * N * T + (E + 1) * (N * K // 2 + N * K // 32) + 4 * S + 2 * (S + 2 * T) + 4 * K * T
 
 CHUNKS = [(0, 992), (992, 544), (1536, 384), (1920, 128)]
-FIRST_GATE = 320
+FIRST_CUTS = [0, 128, 416, CHUNKS[0][1]]
 LATE = CHUNKS[2][0]
 SHARED_PIECE = 256
 
@@ -87,13 +87,13 @@ def tile_moe_bds_lin_none_kernel(
 
         nc.sync.dma_start(offs_sb[:], offs)
         nc.sync.dma_start(planes[0][:], dy_view[:, 0, :])
-        load_gate(0, FIRST_GATE)
-        load_gate(FIRST_GATE, CHUNKS[0][1])
+        for a, b in zip(FIRST_CUTS, FIRST_CUTS[1:]):
+            load_gate(a, b)
         nc.sync.dma_start(planes[1][:], dy_view[:, 1, :])
-        load_rows(0)
         nc.sync.dma_start(planes[2][:], dy_view[:, 2, :])
-        load_rows(1)
+        load_rows(0)
         nc.sync.dma_start(planes[3][:], dy_view[:, 3, :])
+        load_rows(1)
         load_rows(2)
         load_gate(CHUNKS[1][0], CHUNKS[2][0])
         load_rows(3)
@@ -124,8 +124,8 @@ def tile_moe_bds_lin_none_kernel(
             g_rows[c] = ring.tile([P, PACK, w], F32, name="g_rows")
             for t in range(PACK):
                 if c == 0 and t == 0:
-                    gather_plane(c, t, 0, FIRST_GATE)
-                    gather_plane(c, t, FIRST_GATE, w)
+                    for a, b in zip(FIRST_CUTS, FIRST_CUTS[1:]):
+                        gather_plane(c, t, a, b)
                 else:
                     gather_plane(c, t, 0, w)
 
@@ -195,12 +195,16 @@ def tile_moe_bds_lin_none_kernel(
             nc.vector.tensor_tensor(first[:], dx[m][:].indirect(pos1_sb[:, cols]), ds[m][:, t0 : t0 + w], ADD)
             firsts[m, t0] = first
 
-        def add_second(m, t0, w, base, queue=nc.sync):
-            total = ring.tile([P, w], F32, name="total", bufs=3)
-            cols = slice(t0 // PER_COL, (t0 + w) // PER_COL)
-            first = firsts[m, base][:, t0 - base : t0 - base + w]
-            nc.vector.tensor_tensor(total[:], dx[m][:].indirect(pos2_sb[:, cols]), first, ADD)
-            queue.dma_start(out[P * m : P * (m + 1), t0 : t0 + w], total[:])
+        def add_second(m, parts, queue=nc.sync):
+            start, stop = parts[0][0], parts[-1][0] + parts[-1][1]
+            total = ring.tile([P, stop - start], F32, name="total", bufs=3)
+            for t0, w, base in parts:
+                cols = slice(t0 // PER_COL, (t0 + w) // PER_COL)
+                first = firsts[m, base][:, t0 - base : t0 - base + w]
+                nc.vector.tensor_tensor(
+                    total[:, t0 - start : t0 - start + w], dx[m][:].indirect(pos2_sb[:, cols]), first, ADD
+                )
+            queue.dma_start(out[P * m : P * (m + 1), start:stop], total[:])
 
         for q in range(3):
             interleave_tokens(q)
@@ -234,9 +238,9 @@ def tile_moe_bds_lin_none_kernel(
 
         jobs = [(0, [(512, 512)])]
         for m in range(1, K // P):
-            jobs += [(m, [(0, 512)]), (m, [(512, 512)])]
+            jobs += [(m, [(512, 512)]), (m, [(0, 512)])]
             jobs += [(m, s0) for s0 in range(0, S, BANK)]
-        late_banks = [5, 6, 4, 7]
+        late_banks = [5, 4, 6, 1, 2, 7, 3]
         for i, (m, what) in enumerate(jobs):
             b = late_banks[i % len(late_banks)]
             if isinstance(what, list):
@@ -244,15 +248,17 @@ def tile_moe_bds_lin_none_kernel(
             else:
                 expert_products(m, what, BANK, b)
 
-        pairs = [((0, 0, 256), (0, 256, 256)), ((0, 512, 256), (0, 768, 256))]
-        pairs += [((m, 0, 512), (m, 512, 512)) for m in (1, 2)]
-        for pair in pairs:
-            for m, t0, w in pair:
-                add_first(m, t0, w)
-            for m, t0, w in pair:
-                add_second(m, t0, w, t0)
+        for t0 in (0, 512):
+            add_first(0, t0, 256)
+            add_first(0, t0 + 256, 256)
+            add_second(0, [(t0, 256, t0), (t0 + 256, 256, t0 + 256)])
+        for m in (1, 2):
+            add_first(m, 0, 512)
+            add_first(m, 512, 512)
+            add_second(m, [(0, 512, 0)])
+            add_second(m, [(512, 512, 512)])
         add_first(3, 0, 640)
         add_first(3, 640, 384)
-        add_second(3, 0, 640, 0)
-        add_second(3, 640, 256, 640)
-        add_second(3, 896, 128, 640, nc.scalar)
+        add_second(3, [(0, 640, 0)])
+        add_second(3, [(640, 256, 640)])
+        add_second(3, [(896, 128, 640)], nc.scalar)

@@ -1,6 +1,7 @@
 from contextlib import ExitStack
 
 import concourse.mybir as mybir
+from concourse.masks import make_identity
 
 K, T, E, C, N = 512, 1024, 8, 256, 512
 S = E * C
@@ -70,7 +71,9 @@ def tile_moe_bds_lin_none_kernel(
         y_codes = {}
         y_scales = keep.tile([P, T], U8, name="y_scales", align_bytes=64)
 
+        ident = keep.tile([P, P], F32, name="ident")
         nc.vector.memset(w_sc[:].bitcast(I32), 0)
+        make_identity(nc, ident[:])
 
         dy_view = dyT.rearrange("(p t) x -> p t x", t=PACK)
 
@@ -121,7 +124,7 @@ def tile_moe_bds_lin_none_kernel(
 
         def gather_slots(c):
             s0, w = CHUNKS[c]
-            g_rows[c] = ring.tile([P, PACK, w], F32, name="g_rows")
+            g_rows[c] = keep.tile([P, PACK, w], F32, name=f"g_rows{c}", tag=f"rows{c % 2}", align_bytes=64)
             for t in range(PACK):
                 if c == 0 and t == 0:
                     for a, b in zip(FIRST_CUTS, FIRST_CUTS[1:]):
@@ -132,7 +135,8 @@ def tile_moe_bds_lin_none_kernel(
         def grouped(s0, w):
             if s0 < LATE:
                 return late["early"][:, PACK * s0 : PACK * (s0 + w)]
-            return late["grouped"][:, PACK * (s0 - LATE) : PACK * (s0 - LATE + w)]
+            c = 2 if s0 < CHUNKS[3][0] else 3
+            return late[c][:, PACK * (s0 - CHUNKS[c][0]) : PACK * (s0 - CHUNKS[c][0] + w)]
 
         def interleave_slots(c):
             interleave(nc, grouped(*CHUNKS[c]).rearrange("p (w t) -> p w t", t=PACK), g_rows[c][:])
@@ -149,10 +153,13 @@ def tile_moe_bds_lin_none_kernel(
                 in_=grouped(s0, w),
             )
 
-        def quantize_tokens(t0, w, tag):
-            y_codes[t0] = keep.tile([P, w], U32, name=f"y_codes{t0}", tag=tag, align_bytes=64)
+        def token_codes(t0, w):
+            base = max(b for b in y_codes if b <= t0)
+            return y_codes[base][:, t0 - base : t0 - base + w]
+
+        def quantize_tokens(t0, w):
             nc.vector.quantize_mx(
-                out=y_codes[t0][:].bitcast(FP8X4),
+                out=token_codes(t0, w).bitcast(FP8X4),
                 scales=y_scales[:, t0 : t0 + w],
                 in_=y_grouped[:, PACK * t0 : PACK * (t0 + w)],
             )
@@ -183,7 +190,7 @@ def tile_moe_bds_lin_none_kernel(
             acc = banks[b]
             t0 = parts[0][0]
             for u, w in parts:
-                multiply(acc[:, u - t0 : u - t0 + w], E, m, y_codes[u][:], y_scales[:, u : u + w])
+                multiply(acc[:, u - t0 : u - t0 + w], E, m, token_codes(u, w), y_scales[:, u : u + w])
             t1 = parts[-1][0] + parts[-1][1]
             nc.scalar.copy(out=ds[m][:, t0:t1], in_=acc[:, 0 : t1 - t0])
 
@@ -208,7 +215,6 @@ def tile_moe_bds_lin_none_kernel(
 
         for q in range(3):
             interleave_tokens(q)
-        quantize_tokens(0, 512, "free")
         gather_slots(0)
         late["early"] = keep.tile([P, LATE * PACK], BF16, name="early_grouped", tag="dy_rows2", align_bytes=64)
         interleave_slots(0)
@@ -217,41 +223,67 @@ def tile_moe_bds_lin_none_kernel(
         quantize_slots(0, 512)
         quantize_slots(512, 256)
         interleave_slots(1)
-        shared_product(0, [(0, 512)], 0)
         expert_products(0, 0, 512, 4)
         expert_products(0, 512, 256, 3)
         gather_slots(2)
         quantize_slots(768, 256)
         quantize_slots(1024, 512)
-        late["grouped"] = keep.tile([P, (S - LATE) * PACK], BF16, name="late_grouped", tag="held", align_bytes=64)
+        late[2] = keep.tile([P, CHUNKS[2][1] * PACK], BF16, name="grouped2", tag="held", align_bytes=64)
         interleave_slots(2)
         expert_products(0, 768, 256, 3)
         gather_slots(3)
+        late[3] = keep.tile([P, CHUNKS[3][1] * PACK], BF16, name="grouped3", tag="rows0", align_bytes=64)
         interleave_slots(3)
         quantize_slots(1536, 256)
         quantize_slots(1792, 128)
         expert_products(0, 1024, 512, 4)
+        y_codes[0] = keep.tile([P, 256], U32, name="y_codes0", tag="held", align_bytes=64)
+        quantize_tokens(0, 256)
         quantize_slots(1920, 128)
         expert_products(0, 1536, 384, 6)
         expert_products(0, 1920, 128, 7)
-        quantize_tokens(512, 512, "held")
+        y_codes[256] = keep.tile([P, 768], U32, name="y_codes256", tag="rows0", align_bytes=64)
+        quantize_tokens(512, 512)
+        quantize_tokens(256, 256)
 
-        jobs = [(0, [(512, 512)])]
-        for m in range(1, K // P):
-            jobs += [(m, [(512, 512)]), (m, [(0, 512)])]
-            jobs += [(m, s0) for s0 in range(0, S, BANK)]
-        late_banks = [5, 4, 6, 1, 2, 7, 3]
-        for i, (m, what) in enumerate(jobs):
-            b = late_banks[i % len(late_banks)]
-            if isinstance(what, list):
-                shared_product(m, what, b)
-            else:
-                expert_products(m, what, BANK, b)
+        late_banks = [4, 6, 1, 2, 7, 3]
+        taken = []
 
-        for t0 in (0, 512):
-            add_first(0, t0, 256)
-            add_first(0, t0 + 256, 256)
-            add_second(0, [(t0, 256, t0), (t0 + 256, 256, t0 + 256)])
+        def next_bank():
+            taken.append(late_banks[len(taken) % len(late_banks)])
+            return taken[-1]
+
+        def products(m):
+            shared_product(m, [(512, 512)], next_bank())
+            shared_product(m, [(0, 256), (256, 256)], next_bank())
+            for s0 in range(0, S, BANK):
+                expert_products(m, s0, BANK, next_bank())
+
+        fetched = []
+        for r, pos in enumerate((pos1_sb, pos2_sb)):
+            fetched.append(keep.tile([P, T], F32, name=f"fetched{r}"))
+            nc.vector.tensor_copy(fetched[r][:], dx[0][:].indirect(pos[:]))
+        products(1)
+        products(2)
+        shared_product(0, [(0, 256), (256, 256)], next_bank())
+        shared_product(0, [(512, 512)], next_bank())
+        turned = {}
+        for t0, b in ((0, 0), (BANK, 5)):
+            for j in range(0, BANK, P):
+                cols = slice(t0 + j, t0 + j + P)
+                for r, term in enumerate((ds[0], fetched[0], fetched[1])):
+                    nc.tensor.matmul(
+                        banks[b][:, j : j + P], term[:, cols], ident[:], start=(r == 0), stop=(r == 2), is_transpose=True
+                    )
+            turned[t0] = ring.tile([P, BANK], F32, name="turned")
+            nc.scalar.copy(out=turned[t0][:], in_=banks[b][:])
+        for t0, b in ((0, 0), (BANK, 5)):
+            for j in range(0, BANK, P):
+                nc.tensor.transpose(banks[b][:, j : j + P], turned[t0][:, j : j + P], ident[:])
+            back = ring.tile([P, BANK], F32, name="back")
+            nc.scalar.copy(out=back[:], in_=banks[b][:])
+            nc.sync.dma_start(out[0:P, t0 : t0 + BANK], back[:])
+        products(3)
         for m in (1, 2):
             add_first(m, 0, 512)
             add_first(m, 512, 512)

@@ -21,14 +21,18 @@ P = 128
 PACK = 4
 BANK = 512
 PER_COL = 16
+BLOCK_BYTES = 2 * P
 
 FLOPS = 2 * N * K * (S + T)
 BYTES = 4 * N * T + (E + 1) * (N * K // 2 + N * K // 32) + 4 * S + 2 * (S + 2 * T) + 4 * K * T
 
 CHUNKS = [(0, 992), (992, 544), (1536, 384), (1920, 128)]
 FIRST_CUTS = [0, 128, 416, CHUNKS[0][1]]
-LATE = CHUNKS[2][0]
-SHARED_PIECE = 256
+TOKEN_PIECE = 256
+FIRST_EXPERTS = 3
+AHEAD_EXPERTS = 4
+EARLY_TOKENS = 256
+LAST_CUTS = [0, 640, 896, T]
 
 
 def interleave(nc, dst, src):
@@ -50,122 +54,122 @@ def tile_moe_bds_lin_none_kernel(
         offs_sb = keep.tile([P, S // PER_COL], U16, name="offs_sb")
         pos1_sb = keep.tile([P, T // PER_COL], U16, name="pos1_sb")
         pos2_sb = keep.tile([P, T // PER_COL], U16, name="pos2_sb")
-        planes = [keep.tile([P, T], F32, name=f"plane{t}") for t in range(PACK)]
+        planes = [keep.tile([P, T], F32, name=f"plane{d}") for d in range(PACK)]
         gate_sb = keep.tile([P, S], F32, name="gate_sb")
-        n_shared = T // SHARED_PIECE
         dy_rows = [
-            keep.tile([P, PACK, SHARED_PIECE], F32, name=f"dy_rows{q}", tag=f"dy_rows{q}", align_bytes=64)
-            for q in range(n_shared)
+            keep.tile([P, PACK, TOKEN_PIECE], F32, name=f"dy_rows{q}", tag=f"dy_rows{q}", align_bytes=64)
+            for q in range(T // TOKEN_PIECE)
         ]
-        w_sb = keep.tile([P, E + 1, 2 * K], U8, name="w_sb", align_bytes=64)
+        w_second = keep.tile([P, E - FIRST_EXPERTS, BLOCK_BYTES], U8, name="w_second", align_bytes=64)
+        w_ahead = keep.tile([P, AHEAD_EXPERTS, 2 * K - BLOCK_BYTES], U8, name="w_ahead", align_bytes=64)
+        w_rest = keep.tile([P, E - AHEAD_EXPERTS, 2 * K - BLOCK_BYTES], U8, name="w_rest", align_bytes=64)
+        w_shared = keep.tile([P, 2 * K], U8, name="w_shared", align_bytes=64)
         w_sc = keep.tile([P, E + 1, K], U8, name="w_sc", align_bytes=64)
         dx = [keep.tile([P, S], F32, name=f"dx{m}") for m in range(K // P)]
         ds = [keep.tile([P, T], F32, name=f"ds{m}") for m in range(K // P)]
-        g_rows = {}
-        w_first = keep.tile([P, 3, 2 * P], U8, name="w_first", tag="held", align_bytes=64)
-        late = {}
+        w_first = keep.tile([P, FIRST_EXPERTS, BLOCK_BYTES], U8, name="w_first", tag="held", align_bytes=64)
         banks = [psum.tile([P, BANK], F32, name=f"bank{b}") for b in range(8)]
         g_codes = keep.tile([P, S], U32, name="g_codes", align_bytes=64)
         g_scales = keep.tile([P, S], U8, name="g_scales", align_bytes=64)
         y_grouped = keep.tile([P, T * PACK], BF16, name="y_grouped", align_bytes=64)
-        y_codes = {}
         y_scales = keep.tile([P, T], U8, name="y_scales", align_bytes=64)
+        g_rows = {}
+        g_grouped = {}
+        y_codes = {}
+        firsts = {}
 
         ident = keep.tile([P, P], F32, name="ident")
         nc.vector.memset(w_sc[:].bitcast(I32), 0)
         make_identity(nc, ident[:])
 
-        dy_view = dyT.rearrange("(p t) x -> p t x", t=PACK)
+        dy_view = dyT.rearrange("(p d) x -> p d x", d=PACK)
+        words = w_words.rearrange("e a p b -> p (e a) b")
+
+        def load_plane(d):
+            nc.sync.dma_start(planes[d][:], dy_view[:, d, :])
 
         def load_gate(s0, s1):
             nc.sync.dma_start(gate_sb[:, s0:s1], gate[0:P, s0:s1])
 
         def load_rows(q):
-            nc.sync.dma_start(dy_rows[q][:], dy_view[:, :, q * SHARED_PIECE : (q + 1) * SHARED_PIECE])
+            nc.sync.dma_start(dy_rows[q][:], dy_view[:, :, q * TOKEN_PIECE : (q + 1) * TOKEN_PIECE])
 
-        def load_words(e0, e1):
-            nc.sync.dma_start(
-                w_sb[:, e0:e1, :].bitcast(I32), w_words[e0:e1].rearrange("e a p b -> p (e a) b").bitcast(I32)
-            )
+        def load_bytes(dst, src):
+            nc.sync.dma_start(dst.bitcast(I32), src.bitcast(I32))
 
         nc.sync.dma_start(offs_sb[:], offs)
-        nc.sync.dma_start(planes[0][:], dy_view[:, 0, :])
+        load_plane(0)
         for a, b in zip(FIRST_CUTS, FIRST_CUTS[1:]):
             load_gate(a, b)
-        nc.sync.dma_start(planes[1][:], dy_view[:, 1, :])
-        nc.sync.dma_start(planes[2][:], dy_view[:, 2, :])
+        load_plane(1)
+        load_plane(2)
         load_rows(0)
-        nc.sync.dma_start(planes[3][:], dy_view[:, 3, :])
+        load_plane(3)
         load_rows(1)
-        load_rows(2)
         load_gate(CHUNKS[1][0], CHUNKS[2][0])
+        load_rows(2)
         load_rows(3)
         load_gate(CHUNKS[2][0], S)
-        for q in range(4):
-            nc.sync.dma_start(
-                w_sc[32 * q : 32 * q + 4, :, :].bitcast(I32),
-                w_scales[:, 0, 4 * q : 4 * q + 4, :].rearrange("e f k -> f e k").bitcast(I32),
-            )
-        words = w_words.rearrange("e a p b -> p (e a) b")
-        load_words(3, E + 1)
-        nc.sync.dma_start(w_first[:].bitcast(I32), words[:, 0:3, 0 : 2 * P].bitcast(I32))
-        nc.sync.dma_start(w_sb[:, 0:3, 2 * P :].bitcast(I32), words[:, 0:3, 2 * P :].bitcast(I32))
         nc.sync.dma_start(pos1_sb[:], pos1)
         nc.sync.dma_start(pos2_sb[:], pos2)
-
-        def gather_plane(c, t, a, b):
-            s0 = CHUNKS[c][0]
-            nc.vector.tensor_tensor(
-                g_rows[c][:, t, a:b],
-                planes[t][:].indirect(offs_sb[:, (s0 + a) // PER_COL : (s0 + b) // PER_COL]),
-                gate_sb[:, s0 + a : s0 + b],
-                MULT,
+        for q in range(4):
+            load_bytes(
+                w_sc[32 * q : 32 * q + 4, :, :], w_scales[:, 0, 4 * q : 4 * q + 4, :].rearrange("e f k -> f e k")
             )
+        load_bytes(w_first[:], words[:, 0:FIRST_EXPERTS, 0:BLOCK_BYTES])
+        load_bytes(w_second[:], words[:, FIRST_EXPERTS:E, 0:BLOCK_BYTES])
+        load_bytes(w_ahead[:], words[:, 0:AHEAD_EXPERTS, BLOCK_BYTES:])
+        load_bytes(w_rest[:], words[:, AHEAD_EXPERTS:E, BLOCK_BYTES:])
+        load_bytes(w_shared[:], w_words[E, 0])
 
         def gather_slots(c):
             s0, w = CHUNKS[c]
             g_rows[c] = keep.tile([P, PACK, w], F32, name=f"g_rows{c}", tag=f"rows{c % 2}", align_bytes=64)
-            for t in range(PACK):
-                if c == 0 and t == 0:
-                    for a, b in zip(FIRST_CUTS, FIRST_CUTS[1:]):
-                        gather_plane(c, t, a, b)
-                else:
-                    gather_plane(c, t, 0, w)
+            for d in range(PACK):
+                cuts = FIRST_CUTS if c == 0 and d == 0 else [0, w]
+                for a, b in zip(cuts, cuts[1:]):
+                    nc.vector.tensor_tensor(
+                        g_rows[c][:, d, a:b],
+                        planes[d][:].indirect(offs_sb[:, (s0 + a) // PER_COL : (s0 + b) // PER_COL]),
+                        gate_sb[:, s0 + a : s0 + b],
+                        MULT,
+                    )
 
-        def grouped(s0, w):
-            if s0 < LATE:
-                return late["early"][:, PACK * s0 : PACK * (s0 + w)]
-            c = 2 if s0 < CHUNKS[3][0] else 3
-            return late[c][:, PACK * (s0 - CHUNKS[c][0]) : PACK * (s0 - CHUNKS[c][0] + w)]
+        def columns(tiles, start, width, per=1):
+            base = max(b for b in tiles if b <= start)
+            return tiles[base][:, per * (start - base) : per * (start - base + width)]
 
         def interleave_slots(c):
-            interleave(nc, grouped(*CHUNKS[c]).rearrange("p (w t) -> p w t", t=PACK), g_rows[c][:])
+            dst = columns(g_grouped, *CHUNKS[c], per=PACK)
+            interleave(nc, dst.rearrange("p (w t) -> p w t", t=PACK), g_rows[c][:])
 
         def interleave_tokens(q):
-            t0 = q * SHARED_PIECE
-            dst = y_grouped[:, PACK * t0 : PACK * (t0 + SHARED_PIECE)].rearrange("p (w t) -> p w t", t=PACK)
-            interleave(nc, dst, dy_rows[q][:])
+            dst = y_grouped[:, PACK * TOKEN_PIECE * q : PACK * TOKEN_PIECE * (q + 1)]
+            interleave(nc, dst.rearrange("p (w t) -> p w t", t=PACK), dy_rows[q][:])
 
         def quantize_slots(s0, w):
             nc.vector.quantize_mx(
                 out=g_codes[:, s0 : s0 + w].bitcast(FP8X4),
                 scales=g_scales[:, s0 : s0 + w],
-                in_=grouped(s0, w),
+                in_=columns(g_grouped, s0, w, per=PACK),
             )
-
-        def token_codes(t0, w):
-            base = max(b for b in y_codes if b <= t0)
-            return y_codes[base][:, t0 - base : t0 - base + w]
 
         def quantize_tokens(t0, w):
             nc.vector.quantize_mx(
-                out=token_codes(t0, w).bitcast(FP8X4),
+                out=columns(y_codes, t0, w).bitcast(FP8X4),
                 scales=y_scales[:, t0 : t0 + w],
                 in_=y_grouped[:, PACK * t0 : PACK * (t0 + w)],
             )
 
         def multiply(acc, e, m, codes, scales):
-            weights = w_first[:, e, :] if m == 0 and e < 3 else w_sb[:, e, 2 * P * m : 2 * P * (m + 1)]
+            if e == E:
+                weights = w_shared[:, BLOCK_BYTES * m : BLOCK_BYTES * (m + 1)]
+            elif m == 0:
+                weights = w_first[:, e, :] if e < FIRST_EXPERTS else w_second[:, e - FIRST_EXPERTS, :]
+            elif e < AHEAD_EXPERTS:
+                weights = w_ahead[:, e, BLOCK_BYTES * (m - 1) : BLOCK_BYTES * m]
+            else:
+                weights = w_rest[:, e - AHEAD_EXPERTS, BLOCK_BYTES * (m - 1) : BLOCK_BYTES * m]
             nc.tensor.matmul_mx(
                 out=acc,
                 lhsT=weights.bitcast(FP4X4),
@@ -176,121 +180,112 @@ def tile_moe_bds_lin_none_kernel(
                 stop=True,
             )
 
-        def expert_products(m, s0, w, b):
-            acc = banks[b]
+        def expert_products(m, s0, w, bank):
             j = s0
             while j < s0 + w:
                 e = j // C
                 n = min((e + 1) * C, s0 + w) - j
-                multiply(acc[:, j - s0 : j - s0 + n], e, m, g_codes[:, j : j + n], g_scales[:, j : j + n])
+                multiply(banks[bank][:, j - s0 : j - s0 + n], e, m, g_codes[:, j : j + n], g_scales[:, j : j + n])
                 j += n
-            nc.scalar.copy(out=dx[m][:, s0 : s0 + w], in_=acc[:, 0:w])
+            nc.scalar.copy(out=dx[m][:, s0 : s0 + w], in_=banks[bank][:, 0:w])
 
-        def shared_product(m, parts, b):
-            acc = banks[b]
-            t0 = parts[0][0]
-            for u, w in parts:
-                multiply(acc[:, u - t0 : u - t0 + w], E, m, token_codes(u, w), y_scales[:, u : u + w])
-            t1 = parts[-1][0] + parts[-1][1]
-            nc.scalar.copy(out=ds[m][:, t0:t1], in_=acc[:, 0 : t1 - t0])
+        def shared_product(m, t0, bank):
+            cuts = [t0] + [b for b in y_codes if t0 < b < t0 + BANK] + [t0 + BANK]
+            for a, b in zip(cuts, cuts[1:]):
+                multiply(banks[bank][:, a - t0 : b - t0], E, m, columns(y_codes, a, b - a), y_scales[:, a:b])
+            nc.scalar.copy(out=ds[m][:, t0 : t0 + BANK], in_=banks[bank][:, 0:BANK])
 
-        firsts = {}
+        def add_first(m, t0, t1):
+            first = keep.tile([P, t1 - t0], F32, name=f"first{m}_{t0}")
+            window = dx[m][:].indirect(pos1_sb[:, t0 // PER_COL : t1 // PER_COL])
+            nc.vector.tensor_tensor(first[:], window, ds[m][:, t0:t1], ADD)
+            firsts.setdefault(m, {})[t0] = first
 
-        def add_first(m, t0, w):
-            first = keep.tile([P, w], F32, name=f"first{m}_{t0}")
-            cols = slice(t0 // PER_COL, (t0 + w) // PER_COL)
-            nc.vector.tensor_tensor(first[:], dx[m][:].indirect(pos1_sb[:, cols]), ds[m][:, t0 : t0 + w], ADD)
-            firsts[m, t0] = first
+        def add_second(m, cuts):
+            total = ring.tile([P, cuts[-1] - cuts[0]], F32, name="total", bufs=3)
+            for a, b in zip(cuts, cuts[1:]):
+                window = dx[m][:].indirect(pos2_sb[:, a // PER_COL : b // PER_COL])
+                nc.vector.tensor_tensor(total[:, a - cuts[0] : b - cuts[0]], window, columns(firsts[m], a, b - a), ADD)
+            nc.sync.dma_start(out[P * m : P * (m + 1), cuts[0] : cuts[-1]], total[:])
 
-        def add_second(m, parts, queue=nc.sync):
-            start, stop = parts[0][0], parts[-1][0] + parts[-1][1]
-            total = ring.tile([P, stop - start], F32, name="total", bufs=3)
-            for t0, w, base in parts:
-                cols = slice(t0 // PER_COL, (t0 + w) // PER_COL)
-                first = firsts[m, base][:, t0 - base : t0 - base + w]
-                nc.vector.tensor_tensor(
-                    total[:, t0 - start : t0 - start + w], dx[m][:].indirect(pos2_sb[:, cols]), first, ADD
-                )
-            queue.dma_start(out[P * m : P * (m + 1), start:stop], total[:])
-
-        for q in range(3):
-            interleave_tokens(q)
+        interleave_tokens(0)
+        interleave_tokens(1)
         gather_slots(0)
-        late["early"] = keep.tile([P, LATE * PACK], BF16, name="early_grouped", tag="dy_rows2", align_bytes=64)
+        g_grouped[0] = keep.tile([P, CHUNKS[2][0] * PACK], BF16, name="early_grouped", tag="dy_rows1", align_bytes=64)
         interleave_slots(0)
+        interleave_tokens(2)
         interleave_tokens(3)
         gather_slots(1)
         quantize_slots(0, 512)
         quantize_slots(512, 256)
         interleave_slots(1)
-        expert_products(0, 0, 512, 4)
-        expert_products(0, 512, 256, 3)
+        expert_products(0, 0, 512, bank=4)
+        expert_products(0, 512, 256, bank=3)
         gather_slots(2)
         quantize_slots(768, 256)
         quantize_slots(1024, 512)
-        late[2] = keep.tile([P, CHUNKS[2][1] * PACK], BF16, name="grouped2", tag="held", align_bytes=64)
+        g_grouped[CHUNKS[2][0]] = keep.tile([P, CHUNKS[2][1] * PACK], BF16, name="grouped2", tag="held", align_bytes=64)
         interleave_slots(2)
-        expert_products(0, 768, 256, 3)
+        expert_products(0, 768, 256, bank=3)
         gather_slots(3)
-        late[3] = keep.tile([P, CHUNKS[3][1] * PACK], BF16, name="grouped3", tag="rows0", align_bytes=64)
+        g_grouped[CHUNKS[3][0]] = keep.tile([P, CHUNKS[3][1] * PACK], BF16, name="grouped3", tag="rows0", align_bytes=64)
         interleave_slots(3)
         quantize_slots(1536, 256)
         quantize_slots(1792, 128)
-        expert_products(0, 1024, 512, 4)
-        y_codes[0] = keep.tile([P, 256], U32, name="y_codes0", tag="held", align_bytes=64)
-        quantize_tokens(0, 256)
-        quantize_slots(1920, 128)
-        expert_products(0, 1536, 384, 6)
-        expert_products(0, 1920, 128, 7)
-        y_codes[256] = keep.tile([P, 768], U32, name="y_codes256", tag="rows0", align_bytes=64)
-        quantize_tokens(512, 512)
-        quantize_tokens(256, 256)
+        expert_products(0, 1024, 512, bank=4)
+        y_codes[0] = keep.tile([P, EARLY_TOKENS], U32, name="y_codes0", tag="held", align_bytes=64)
+        quantize_tokens(0, EARLY_TOKENS)
+        quantize_slots(*CHUNKS[3])
+        expert_products(0, *CHUNKS[2], bank=6)
+        expert_products(0, *CHUNKS[3], bank=7)
+        y_codes[EARLY_TOKENS] = keep.tile([P, T - EARLY_TOKENS], U32, name="y_codes256", tag="rows0", align_bytes=64)
+        quantize_tokens(BANK, T - BANK)
+        quantize_tokens(EARLY_TOKENS, BANK - EARLY_TOKENS)
 
-        late_banks = [4, 6, 1, 2, 7, 3]
-        taken = []
-
-        def next_bank():
-            taken.append(late_banks[len(taken) % len(late_banks)])
-            return taken[-1]
-
-        def products(m):
-            shared_product(m, [(512, 512)], next_bank())
-            shared_product(m, [(0, 256), (256, 256)], next_bank())
-            for s0 in range(0, S, BANK):
-                expert_products(m, s0, BANK, next_bank())
+        def products(m, through):
+            shared_product(m, BANK, through[0])
+            shared_product(m, 0, through[1])
+            for s0, bank in zip(range(0, S, BANK), through[2:]):
+                expert_products(m, s0, BANK, bank)
 
         fetched = []
-        for r, pos in enumerate((pos1_sb, pos2_sb)):
+        for r, pos_sb in enumerate((pos1_sb, pos2_sb)):
             fetched.append(keep.tile([P, T], F32, name=f"fetched{r}"))
-            nc.vector.tensor_copy(fetched[r][:], dx[0][:].indirect(pos[:]))
-        products(1)
-        products(2)
-        shared_product(0, [(0, 256), (256, 256)], next_bank())
-        shared_product(0, [(512, 512)], next_bank())
+            nc.vector.tensor_copy(fetched[r][:], dx[0][:].indirect(pos_sb[:]))
+        products(1, through=[4, 6, 3, 0, 7, 1])
+        round_of_banks = [2, 4, 6, 7, 3, 1]
+        products(2, through=round_of_banks)
+        products(3, through=round_of_banks)
+        shared_product(0, 0, round_of_banks[0])
+        shared_product(0, BANK, round_of_banks[1])
+
+        halves = ((0, banks[0]), (BANK, banks[5]))
         turned = {}
-        for t0, b in ((0, 0), (BANK, 5)):
+        for t0, acc in halves:
             for j in range(0, BANK, P):
-                cols = slice(t0 + j, t0 + j + P)
                 for r, term in enumerate((ds[0], fetched[0], fetched[1])):
                     nc.tensor.matmul(
-                        banks[b][:, j : j + P], term[:, cols], ident[:], start=(r == 0), stop=(r == 2), is_transpose=True
+                        acc[:, j : j + P],
+                        term[:, t0 + j : t0 + j + P],
+                        ident[:],
+                        start=(r == 0),
+                        stop=(r == 2),
+                        is_transpose=True,
                     )
             turned[t0] = ring.tile([P, BANK], F32, name="turned")
-            nc.scalar.copy(out=turned[t0][:], in_=banks[b][:])
-        for t0, b in ((0, 0), (BANK, 5)):
+            nc.scalar.copy(out=turned[t0][:], in_=acc[:])
+        for t0, acc in halves:
             for j in range(0, BANK, P):
-                nc.tensor.transpose(banks[b][:, j : j + P], turned[t0][:, j : j + P], ident[:])
+                nc.tensor.transpose(acc[:, j : j + P], turned[t0][:, j : j + P], ident[:])
             back = ring.tile([P, BANK], F32, name="back")
-            nc.scalar.copy(out=back[:], in_=banks[b][:])
-            nc.sync.dma_start(out[0:P, t0 : t0 + BANK], back[:])
-        products(3)
+            nc.scalar.copy(out=back[:], in_=acc[:])
+            nc.scalar.dma_start(out[0:P, t0 : t0 + BANK], back[:])
+
         for m in (1, 2):
-            add_first(m, 0, 512)
-            add_first(m, 512, 512)
-            add_second(m, [(0, 512, 0)])
-            add_second(m, [(512, 512, 512)])
-        add_first(3, 0, 640)
-        add_first(3, 640, 384)
-        add_second(3, [(0, 640, 0)])
-        add_second(3, [(640, 256, 640)])
-        add_second(3, [(896, 128, 640)], nc.scalar)
+            add_first(m, 0, BANK)
+            add_first(m, BANK, T)
+            add_second(m, [0, BANK, T])
+        add_first(3, 0, LAST_CUTS[1])
+        add_first(3, LAST_CUTS[1], T)
+        for a, b in zip(LAST_CUTS, LAST_CUTS[1:]):
+            add_second(3, [a, b])

@@ -1,7 +1,6 @@
 from contextlib import ExitStack
 
 import concourse.mybir as mybir
-from concourse.masks import make_identity
 
 K, T, E, C, N = 512, 1024, 8, 256, 512
 S = E * C
@@ -16,30 +15,25 @@ FP8X4 = mybir.dt.float8_e4m3fn_x4
 FP4X4 = mybir.dt.float4_e2m1fn_x4
 MULT = mybir.AluOpType.mult
 ADD = mybir.AluOpType.add
+COPY = mybir.ActivationFunctionType.Copy
 
 P = 128
 PACK = 4
 BANK = 512
 PER_COL = 16
 BLOCK_BYTES = 2 * P
+BLOCKS = K // P
 
 FLOPS = 2 * N * K * (S + T)
 BYTES = 4 * N * T + (E + 1) * (N * K // 2 + N * K // 32) + 4 * S + 2 * (S + 2 * T) + 4 * K * T
 
-CHUNKS = [(0, 992), (992, 544), (1536, 384), (1920, 128)]
-FIRST_CUTS = [0, 128, 416, CHUNKS[0][1]]
+PAIR = 2 * C
+PAIRS = S // PAIR
+CHUNKS = [(0, 640), (640, 512), (1152, 512), (1664, 384)]
+FIRST_CUTS = [0, 128, CHUNKS[0][1]]
 TOKEN_PIECE = 256
-FIRST_EXPERTS = 3
-AHEAD_EXPERTS = 4
-EARLY_TOKENS = 256
-LAST_CUTS = [0, 640, 896, T]
-
-
-def interleave(nc, dst, src):
-    nc.scalar.copy(
-        out=dst.rearrange("p (c i) t -> p c t i", i=4),
-        in_=src.rearrange("p t (c i) -> p c t i", i=4),
-    )
+RUN = 4
+CUTS = [[0, 256, 512, T], [0, 512, T], [0, 512, T], [0, 256, 512, 768, 896, T]]
 
 
 def tile_moe_bds_lin_none_kernel(
@@ -48,7 +42,7 @@ def tile_moe_bds_lin_none_kernel(
     nc = tc.nc
     with ExitStack() as ctx:
         keep = ctx.enter_context(tc.tile_pool(name="keep", bufs=1))
-        ring = ctx.enter_context(tc.tile_pool(name="ring", bufs=2))
+        ring = ctx.enter_context(tc.tile_pool(name="ring", bufs=5))
         psum = ctx.enter_context(tc.psum_pool(name="psum", bufs=1))
 
         offs_sb = keep.tile([P, S // PER_COL], U16, name="offs_sb")
@@ -57,30 +51,28 @@ def tile_moe_bds_lin_none_kernel(
         planes = [keep.tile([P, T], F32, name=f"plane{d}") for d in range(PACK)]
         gate_sb = keep.tile([P, S], F32, name="gate_sb")
         dy_rows = [
-            keep.tile([P, PACK, TOKEN_PIECE], F32, name=f"dy_rows{q}", tag=f"dy_rows{q}", align_bytes=64)
+            keep.tile([P, PACK, TOKEN_PIECE], F32, name=f"dy_rows{q}", align_bytes=64)
             for q in range(T // TOKEN_PIECE)
         ]
-        w_second = keep.tile([P, E - FIRST_EXPERTS, BLOCK_BYTES], U8, name="w_second", align_bytes=64)
-        w_ahead = keep.tile([P, AHEAD_EXPERTS, 2 * K - BLOCK_BYTES], U8, name="w_ahead", align_bytes=64)
-        w_rest = keep.tile([P, E - AHEAD_EXPERTS, 2 * K - BLOCK_BYTES], U8, name="w_rest", align_bytes=64)
-        w_shared = keep.tile([P, 2 * K], U8, name="w_shared", align_bytes=64)
+        w_cuts = [0, 2, 6, E + 1]
+        w_sb = [
+            keep.tile([P, b - a, 2 * K], U8, name=f"w_sb{a}", align_bytes=64) for a, b in zip(w_cuts, w_cuts[1:])
+        ]
         w_sc = keep.tile([P, E + 1, K], U8, name="w_sc", align_bytes=64)
-        dx = [keep.tile([P, S], F32, name=f"dx{m}") for m in range(K // P)]
-        ds = [keep.tile([P, T], F32, name=f"ds{m}") for m in range(K // P)]
-        w_first = keep.tile([P, FIRST_EXPERTS, BLOCK_BYTES], U8, name="w_first", tag="held", align_bytes=64)
+        dx = [keep.tile([P, S], F32, name=f"dx{m}") for m in range(BLOCKS)]
         banks = [psum.tile([P, BANK], F32, name=f"bank{b}") for b in range(8)]
         g_codes = keep.tile([P, S], U32, name="g_codes", align_bytes=64)
         g_scales = keep.tile([P, S], U8, name="g_scales", align_bytes=64)
-        y_grouped = keep.tile([P, T * PACK], BF16, name="y_grouped", align_bytes=64)
+        g_grouped = keep.tile([P, S * PACK], BF16, name="g_grouped", align_bytes=64)
+        y_grouped = {}
+        y_codes = keep.tile([P, T], U32, name="y_codes", align_bytes=64)
         y_scales = keep.tile([P, T], U8, name="y_scales", align_bytes=64)
         g_rows = {}
-        g_grouped = {}
-        y_codes = {}
-        firsts = {}
 
-        ident = keep.tile([P, P], F32, name="ident")
+        warm = keep.tile([P, 2], F32, name="warm")
+        nc.gpsimd.memset(warm[:, 0:1], 0.0)
+        nc.scalar.activation(warm[:, 1:2], warm[:, 0:1], COPY)
         nc.vector.memset(w_sc[:].bitcast(I32), 0)
-        make_identity(nc, ident[:])
 
         dy_view = dyT.rearrange("(p d) x -> p d x", d=PACK)
         words = w_words.rearrange("e a p b -> p (e a) b")
@@ -97,82 +89,98 @@ def tile_moe_bds_lin_none_kernel(
         def load_bytes(dst, src):
             nc.sync.dma_start(dst.bitcast(I32), src.bitcast(I32))
 
+        def load_weights(i):
+            load_bytes(w_sb[i][:], words[:, w_cuts[i] : w_cuts[i + 1], :])
+
         nc.sync.dma_start(offs_sb[:], offs)
         load_plane(0)
         for a, b in zip(FIRST_CUTS, FIRST_CUTS[1:]):
             load_gate(a, b)
         load_plane(1)
         load_plane(2)
-        load_rows(0)
         load_plane(3)
+        load_rows(0)
         load_rows(1)
-        load_gate(CHUNKS[1][0], CHUNKS[2][0])
-        load_rows(2)
-        load_rows(3)
-        load_gate(CHUNKS[2][0], S)
-        nc.sync.dma_start(pos1_sb[:], pos1)
-        nc.sync.dma_start(pos2_sb[:], pos2)
+        load_gate(CHUNKS[1][0], CHUNKS[3][0])
         for q in range(4):
             load_bytes(
                 w_sc[32 * q : 32 * q + 4, :, :], w_scales[:, 0, 4 * q : 4 * q + 4, :].rearrange("e f k -> f e k")
             )
-        load_bytes(w_first[:], words[:, 0:FIRST_EXPERTS, 0:BLOCK_BYTES])
-        load_bytes(w_second[:], words[:, FIRST_EXPERTS:E, 0:BLOCK_BYTES])
-        load_bytes(w_ahead[:], words[:, 0:AHEAD_EXPERTS, BLOCK_BYTES:])
-        load_bytes(w_rest[:], words[:, AHEAD_EXPERTS:E, BLOCK_BYTES:])
-        load_bytes(w_shared[:], w_words[E, 0])
+        load_weights(0)
+        load_weights(1)
+        load_gate(CHUNKS[3][0], S)
+        load_weights(2)
+        load_rows(2)
+        load_rows(3)
+        nc.sync.dma_start(pos1_sb[:], pos1)
+        nc.sync.dma_start(pos2_sb[:], pos2)
 
-        def gather_slots(c):
+        def runs_out(dst):
+            return dst.rearrange("p (c i t) -> p c t i", i=RUN, t=PACK)
+
+        def runs_in(src):
+            return src.rearrange("p t (c i) -> p c t i", i=RUN)
+
+        def offsets(lst, a, b):
+            return lst[:, a // PER_COL : b // PER_COL]
+
+        def gather_gated(c):
             s0, w = CHUNKS[c]
-            g_rows[c] = keep.tile([P, PACK, w], F32, name=f"g_rows{c}", tag=f"rows{c % 2}", align_bytes=64)
+            g_rows[c] = keep.tile([P, PACK, w], F32, name=f"g_rows{c}", tag=f"rows{c % 3}", align_bytes=64)
             for d in range(PACK):
-                cuts = FIRST_CUTS if c == 0 and d == 0 else [0, w]
+                cuts = FIRST_CUTS if d == 0 else [0, w]
                 for a, b in zip(cuts, cuts[1:]):
-                    nc.vector.tensor_tensor(
-                        g_rows[c][:, d, a:b],
-                        planes[d][:].indirect(offs_sb[:, (s0 + a) // PER_COL : (s0 + b) // PER_COL]),
-                        gate_sb[:, s0 + a : s0 + b],
-                        MULT,
-                    )
+                    window = planes[d][:].indirect(offsets(offs_sb, s0 + a, s0 + b))
+                    nc.vector.tensor_tensor(g_rows[c][:, d, a:b], window, gate_sb[:, s0 + a : s0 + b], MULT)
 
-        def columns(tiles, start, width, per=1):
-            base = max(b for b in tiles if b <= start)
-            return tiles[base][:, per * (start - base) : per * (start - base + width)]
+        def gather_plain(c):
+            s0, w = CHUNKS[c]
+            g_rows[c] = keep.tile([P, PACK, w], F32, name=f"g_rows{c}", tag=f"rows{c % 3}", align_bytes=64)
+            for d in range(PACK):
+                window = planes[d][:].indirect(offsets(offs_sb, s0, s0 + w))
+                nc.scalar.activation(g_rows[c][:, d, :], window, COPY)
 
         def interleave_slots(c):
-            dst = columns(g_grouped, *CHUNKS[c], per=PACK)
-            interleave(nc, dst.rearrange("p (w t) -> p w t", t=PACK), g_rows[c][:])
+            s0, w = CHUNKS[c]
+            nc.vector.tensor_copy(runs_out(g_grouped[:, PACK * s0 : PACK * (s0 + w)]), runs_in(g_rows[c][:]))
+
+        def gate_and_interleave(c, a, b):
+            s0 = CHUNKS[c][0]
+            weights = gate_sb[:, s0 + a : s0 + b].rearrange("p (c i) -> p c i", i=RUN).unsqueeze(2)
+            nc.vector.tensor_tensor(
+                runs_out(g_grouped[:, PACK * (s0 + a) : PACK * (s0 + b)]),
+                runs_in(g_rows[c][:, :, a:b]),
+                weights.to_broadcast([P, (b - a) // RUN, PACK, RUN]),
+                MULT,
+            )
+
+        def grouped_tokens(t0, w):
+            base = max(b for b in y_grouped if b <= t0)
+            return y_grouped[base][:, PACK * (t0 - base) : PACK * (t0 - base + w)]
 
         def interleave_tokens(q):
-            dst = y_grouped[:, PACK * TOKEN_PIECE * q : PACK * TOKEN_PIECE * (q + 1)]
-            interleave(nc, dst.rearrange("p (w t) -> p w t", t=PACK), dy_rows[q][:])
+            dst = grouped_tokens(q * TOKEN_PIECE, TOKEN_PIECE)
+            nc.vector.tensor_copy(runs_out(dst), runs_in(dy_rows[q][:]))
 
         def quantize_slots(s0, w):
             nc.vector.quantize_mx(
                 out=g_codes[:, s0 : s0 + w].bitcast(FP8X4),
                 scales=g_scales[:, s0 : s0 + w],
-                in_=columns(g_grouped, s0, w, per=PACK),
+                in_=g_grouped[:, PACK * s0 : PACK * (s0 + w)],
             )
 
         def quantize_tokens(t0, w):
             nc.vector.quantize_mx(
-                out=columns(y_codes, t0, w).bitcast(FP8X4),
+                out=y_codes[:, t0 : t0 + w].bitcast(FP8X4),
                 scales=y_scales[:, t0 : t0 + w],
-                in_=y_grouped[:, PACK * t0 : PACK * (t0 + w)],
+                in_=grouped_tokens(t0, w),
             )
 
         def multiply(acc, e, m, codes, scales):
-            if e == E:
-                weights = w_shared[:, BLOCK_BYTES * m : BLOCK_BYTES * (m + 1)]
-            elif m == 0:
-                weights = w_first[:, e, :] if e < FIRST_EXPERTS else w_second[:, e - FIRST_EXPERTS, :]
-            elif e < AHEAD_EXPERTS:
-                weights = w_ahead[:, e, BLOCK_BYTES * (m - 1) : BLOCK_BYTES * m]
-            else:
-                weights = w_rest[:, e - AHEAD_EXPERTS, BLOCK_BYTES * (m - 1) : BLOCK_BYTES * m]
+            i = max(j for j in range(len(w_sb)) if w_cuts[j] <= e)
             nc.tensor.matmul_mx(
                 out=acc,
-                lhsT=weights.bitcast(FP4X4),
+                lhsT=w_sb[i][:, e - w_cuts[i], BLOCK_BYTES * m : BLOCK_BYTES * (m + 1)].bitcast(FP4X4),
                 lhsT_scale=w_sc[:, e, P * m : P * (m + 1)],
                 rhs=codes.bitcast(FP8X4),
                 rhs_scale=scales,
@@ -180,112 +188,75 @@ def tile_moe_bds_lin_none_kernel(
                 stop=True,
             )
 
-        def expert_products(m, s0, w, bank):
-            j = s0
-            while j < s0 + w:
-                e = j // C
-                n = min((e + 1) * C, s0 + w) - j
-                multiply(banks[bank][:, j - s0 : j - s0 + n], e, m, g_codes[:, j : j + n], g_scales[:, j : j + n])
-                j += n
-            nc.scalar.copy(out=dx[m][:, s0 : s0 + w], in_=banks[bank][:, 0:w])
+        def expert_products(m, c, bank):
+            s0 = c * PAIR
+            for j in range(s0, s0 + PAIR, C):
+                multiply(banks[bank][:, j - s0 : j - s0 + C], j // C, m, g_codes[:, j : j + C], g_scales[:, j : j + C])
+            nc.scalar.copy(out=dx[m][:, s0 : s0 + PAIR], in_=banks[bank][:])
 
         def shared_product(m, t0, bank):
-            cuts = [t0] + [b for b in y_codes if t0 < b < t0 + BANK] + [t0 + BANK]
-            for a, b in zip(cuts, cuts[1:]):
-                multiply(banks[bank][:, a - t0 : b - t0], E, m, columns(y_codes, a, b - a), y_scales[:, a:b])
-            nc.scalar.copy(out=ds[m][:, t0 : t0 + BANK], in_=banks[bank][:, 0:BANK])
+            multiply(banks[bank][:], E, m, y_codes[:, t0 : t0 + BANK], y_scales[:, t0 : t0 + BANK])
 
-        def add_first(m, t0, t1):
-            first = keep.tile([P, t1 - t0], F32, name=f"first{m}_{t0}")
-            window = dx[m][:].indirect(pos1_sb[:, t0 // PER_COL : t1 // PER_COL])
-            nc.vector.tensor_tensor(first[:], window, ds[m][:, t0:t1], ADD)
-            firsts.setdefault(m, {})[t0] = first
+        firsts = {}
+        pairs = {}
 
-        def add_second(m, cuts):
-            total = ring.tile([P, cuts[-1] - cuts[0]], F32, name="total", bufs=3)
-            for a, b in zip(cuts, cuts[1:]):
-                window = dx[m][:].indirect(pos2_sb[:, a // PER_COL : b // PER_COL])
-                nc.vector.tensor_tensor(total[:, a - cuts[0] : b - cuts[0]], window, columns(firsts[m], a, b - a), ADD)
-            nc.sync.dma_start(out[P * m : P * (m + 1), cuts[0] : cuts[-1]], total[:])
+        def fetch_first(m, a, b):
+            firsts[m, a] = ring.tile([P, b - a], F32, name="first")
+            nc.scalar.activation(firsts[m, a][:], dx[m][:].indirect(offsets(pos1_sb, a, b)), COPY)
 
-        interleave_tokens(0)
-        interleave_tokens(1)
-        gather_slots(0)
-        g_grouped[0] = keep.tile([P, CHUNKS[2][0] * PACK], BF16, name="early_grouped", tag="dy_rows1", align_bytes=64)
+        def add_second(m, a, b):
+            pairs[m, a] = ring.tile([P, b - a], F32, name="pair")
+            nc.vector.tensor_tensor(pairs[m, a][:], dx[m][:].indirect(offsets(pos2_sb, a, b)), firsts[m, a][:], ADD)
+
+        def add_shared(m, a, b, bank):
+            total = ring.tile([P, b - a], F32, name="total")
+            nc.vector.tensor_tensor(total[:], pairs[m, a][:], banks[bank][:, a % BANK : a % BANK + b - a], ADD)
+            nc.sync.dma_start(out[P * m : P * (m + 1), a:b], total[:])
+
+        gather_gated(0)
+        gather_plain(1)
+        gather_plain(2)
         interleave_slots(0)
-        interleave_tokens(2)
-        interleave_tokens(3)
-        gather_slots(1)
-        quantize_slots(0, 512)
-        quantize_slots(512, 256)
-        interleave_slots(1)
-        expert_products(0, 0, 512, bank=4)
-        expert_products(0, 512, 256, bank=3)
-        gather_slots(2)
-        quantize_slots(768, 256)
-        quantize_slots(1024, 512)
-        g_grouped[CHUNKS[2][0]] = keep.tile([P, CHUNKS[2][1] * PACK], BF16, name="grouped2", tag="held", align_bytes=64)
-        interleave_slots(2)
-        expert_products(0, 768, 256, bank=3)
-        gather_slots(3)
-        g_grouped[CHUNKS[3][0]] = keep.tile([P, CHUNKS[3][1] * PACK], BF16, name="grouped3", tag="rows0", align_bytes=64)
-        interleave_slots(3)
-        quantize_slots(1536, 256)
-        quantize_slots(1792, 128)
-        expert_products(0, 1024, 512, bank=4)
-        y_codes[0] = keep.tile([P, EARLY_TOKENS], U32, name="y_codes0", tag="held", align_bytes=64)
-        quantize_tokens(0, EARLY_TOKENS)
-        quantize_slots(*CHUNKS[3])
-        expert_products(0, *CHUNKS[2], bank=6)
-        expert_products(0, *CHUNKS[3], bank=7)
-        y_codes[EARLY_TOKENS] = keep.tile([P, T - EARLY_TOKENS], U32, name="y_codes256", tag="rows0", align_bytes=64)
-        quantize_tokens(BANK, T - BANK)
-        quantize_tokens(EARLY_TOKENS, BANK - EARLY_TOKENS)
+        gather_plain(3)
+        y_grouped[0] = keep.tile([P, TOKEN_PIECE * PACK], BF16, name="y_early", align_bytes=64)
+        interleave_tokens(0)
+        quantize_slots(0, PAIR)
+        quantize_tokens(0, TOKEN_PIECE)
+        gate_and_interleave(1, 0, CHUNKS[1][1])
+        gate_and_interleave(2, 0, CHUNKS[2][1])
+        quantize_slots(PAIR, PAIR)
+        quantize_slots(2 * PAIR, PAIR)
+        expert_products(0, 0, bank=0)
+        expert_products(1, 0, bank=1)
+        expert_products(0, 1, bank=2)
+        expert_products(1, 1, bank=3)
+        expert_products(0, 2, bank=4)
+        expert_products(1, 2, bank=5)
+        half = CHUNKS[3][1] // 2
+        gate_and_interleave(3, 0, half)
+        gate_and_interleave(3, half, 2 * half)
+        quantize_slots(3 * PAIR, C)
+        quantize_slots(3 * PAIR + C, C)
+        expert_products(0, 3, bank=6)
+        y_grouped[TOKEN_PIECE] = keep.tile(
+            [P, (T - TOKEN_PIECE) * PACK], BF16, name="y_late", tag="rows0", align_bytes=64
+        )
+        for q in range(1, T // TOKEN_PIECE):
+            interleave_tokens(q)
+        quantize_tokens(TOKEN_PIECE, TOKEN_PIECE)
+        quantize_tokens(BANK, BANK)
 
-        def products(m, through):
-            shared_product(m, BANK, through[0])
-            shared_product(m, 0, through[1])
-            for s0, bank in zip(range(0, S, BANK), through[2:]):
-                expert_products(m, s0, BANK, bank)
-
-        fetched = []
-        for r, pos_sb in enumerate((pos1_sb, pos2_sb)):
-            fetched.append(keep.tile([P, T], F32, name=f"fetched{r}"))
-            nc.vector.tensor_copy(fetched[r][:], dx[0][:].indirect(pos_sb[:]))
-        products(1, through=[4, 6, 3, 0, 7, 1])
-        round_of_banks = [2, 4, 6, 7, 3, 1]
-        products(2, through=round_of_banks)
-        products(3, through=round_of_banks)
-        shared_product(0, 0, round_of_banks[0])
-        shared_product(0, BANK, round_of_banks[1])
-
-        halves = ((0, banks[0]), (BANK, banks[5]))
-        turned = {}
-        for t0, acc in halves:
-            for j in range(0, BANK, P):
-                for r, term in enumerate((ds[0], fetched[0], fetched[1])):
-                    nc.tensor.matmul(
-                        acc[:, j : j + P],
-                        term[:, t0 + j : t0 + j + P],
-                        ident[:],
-                        start=(r == 0),
-                        stop=(r == 2),
-                        is_transpose=True,
-                    )
-            turned[t0] = ring.tile([P, BANK], F32, name="turned")
-            nc.scalar.copy(out=turned[t0][:], in_=acc[:])
-        for t0, acc in halves:
-            for j in range(0, BANK, P):
-                nc.tensor.transpose(acc[:, j : j + P], turned[t0][:, j : j + P], ident[:])
-            back = ring.tile([P, BANK], F32, name="back")
-            nc.scalar.copy(out=back[:], in_=acc[:])
-            nc.scalar.dma_start(out[0:P, t0 : t0 + BANK], back[:])
-
-        for m in (1, 2):
-            add_first(m, 0, BANK)
-            add_first(m, BANK, T)
-            add_second(m, [0, BANK, T])
-        add_first(3, 0, LAST_CUTS[1])
-        add_first(3, LAST_CUTS[1], T)
-        for a, b in zip(LAST_CUTS, LAST_CUTS[1:]):
-            add_second(3, [a, b])
+        dx_banks = {1: {3: 7}, 2: {0: 0, 1: 1, 2: 2, 3: 3}, 3: {0: 0, 1: 1, 2: 2, 3: 3}}
+        ds_banks = {0: [4, 5], 1: [6, 7], 2: [4, 5], 3: [6, 7]}
+        for m in range(BLOCKS):
+            pieces = list(zip(CUTS[m], CUTS[m][1:]))
+            for a, b in pieces:
+                fetch_first(m, a, b)
+            for h in range(T // BANK):
+                shared_product(m, h * BANK, ds_banks[m][h])
+            for c, bank in dx_banks.get(m + 1, {}).items():
+                expert_products(m + 1, c, bank)
+            for a, b in pieces:
+                add_second(m, a, b)
+            for a, b in pieces:
+                add_shared(m, a, b, ds_banks[m][a // BANK])

@@ -29,11 +29,13 @@ BYTES = 4 * N * T + (E + 1) * (N * K // 2 + N * K // 32) + 4 * S + 2 * (S + 2 * 
 
 PAIR = 2 * C
 PAIRS = S // PAIR
-CHUNKS = [(0, 640), (640, 512), (1152, 512), (1664, 384)]
+CHUNKS = [(0, 608), (608, 608), (1216, 448), (1664, 384)]
 FIRST_CUTS = [0, 128, CHUNKS[0][1]]
-TOKEN_PIECE = 256
+TOKEN_CUTS = [0, 256, T]
 RUN = 4
-CUTS = [[0, 256, 512, T], [0, 512, T], [0, 512, T], [0, 256, 512, 768, 896, T]]
+FIRST_PIECE = 256
+LAST_PIECE = 128
+BOTH_FROM = 512
 
 
 def tile_moe_bds_lin_none_kernel(
@@ -42,28 +44,29 @@ def tile_moe_bds_lin_none_kernel(
     nc = tc.nc
     with ExitStack() as ctx:
         keep = ctx.enter_context(tc.tile_pool(name="keep", bufs=1))
-        ring = ctx.enter_context(tc.tile_pool(name="ring", bufs=5))
+        ring = ctx.enter_context(tc.tile_pool(name="ring", bufs=4))
         psum = ctx.enter_context(tc.psum_pool(name="psum", bufs=1))
 
         offs_sb = keep.tile([P, S // PER_COL], U16, name="offs_sb")
         pos1_sb = keep.tile([P, T // PER_COL], U16, name="pos1_sb")
         pos2_sb = keep.tile([P, T // PER_COL], U16, name="pos2_sb")
         planes = [keep.tile([P, T], F32, name=f"plane{d}") for d in range(PACK)]
+        gate_first = keep.tile([P, CHUNKS[0][1]], F32, name="gate_first", tag="rows2", align_bytes=64)
         gate_sb = keep.tile([P, S], F32, name="gate_sb")
         dy_rows = [
-            keep.tile([P, PACK, TOKEN_PIECE], F32, name=f"dy_rows{q}", align_bytes=64)
-            for q in range(T // TOKEN_PIECE)
+            keep.tile([P, PACK, b - a], F32, name=f"dy_rows{a}", tag=f"dy_rows{a}", align_bytes=64)
+            for a, b in zip(TOKEN_CUTS, TOKEN_CUTS[1:])
         ]
         w_cuts = [0, 2, 6, E + 1]
         w_sb = [
             keep.tile([P, b - a, 2 * K], U8, name=f"w_sb{a}", align_bytes=64) for a, b in zip(w_cuts, w_cuts[1:])
         ]
         w_sc = keep.tile([P, E + 1, K], U8, name="w_sc", align_bytes=64)
-        dx = [keep.tile([P, S], F32, name=f"dx{m}") for m in range(BLOCKS)]
+        dx = {m: keep.tile([P, S], F32, name=f"dx{m}") for m in (0, 1)}
         banks = [psum.tile([P, BANK], F32, name=f"bank{b}") for b in range(8)]
         g_codes = keep.tile([P, S], U32, name="g_codes", align_bytes=64)
         g_scales = keep.tile([P, S], U8, name="g_scales", align_bytes=64)
-        g_grouped = keep.tile([P, S * PACK], BF16, name="g_grouped", align_bytes=64)
+        g_grouped = keep.tile([P, S * PACK], BF16, name="g_grouped", tag="grouped", align_bytes=64)
         y_grouped = {}
         y_codes = keep.tile([P, T], U32, name="y_codes", align_bytes=64)
         y_scales = keep.tile([P, T], U8, name="y_scales", align_bytes=64)
@@ -84,7 +87,7 @@ def tile_moe_bds_lin_none_kernel(
             nc.sync.dma_start(gate_sb[:, s0:s1], gate[0:P, s0:s1])
 
         def load_rows(q):
-            nc.sync.dma_start(dy_rows[q][:], dy_view[:, :, q * TOKEN_PIECE : (q + 1) * TOKEN_PIECE])
+            nc.sync.dma_start(dy_rows[q][:], dy_view[:, :, TOKEN_CUTS[q] : TOKEN_CUTS[q + 1]])
 
         def load_bytes(dst, src):
             nc.sync.dma_start(dst.bitcast(I32), src.bitcast(I32))
@@ -95,23 +98,21 @@ def tile_moe_bds_lin_none_kernel(
         nc.sync.dma_start(offs_sb[:], offs)
         load_plane(0)
         for a, b in zip(FIRST_CUTS, FIRST_CUTS[1:]):
-            load_gate(a, b)
+            nc.sync.dma_start(gate_first[:, a:b], gate[0:P, a:b])
         load_plane(1)
         load_plane(2)
         load_plane(3)
         load_rows(0)
-        load_rows(1)
         load_gate(CHUNKS[1][0], CHUNKS[3][0])
         for q in range(4):
             load_bytes(
                 w_sc[32 * q : 32 * q + 4, :, :], w_scales[:, 0, 4 * q : 4 * q + 4, :].rearrange("e f k -> f e k")
             )
         load_weights(0)
+        load_rows(1)
         load_weights(1)
         load_gate(CHUNKS[3][0], S)
         load_weights(2)
-        load_rows(2)
-        load_rows(3)
         nc.sync.dma_start(pos1_sb[:], pos1)
         nc.sync.dma_start(pos2_sb[:], pos2)
 
@@ -131,7 +132,7 @@ def tile_moe_bds_lin_none_kernel(
                 cuts = FIRST_CUTS if d == 0 else [0, w]
                 for a, b in zip(cuts, cuts[1:]):
                     window = planes[d][:].indirect(offsets(offs_sb, s0 + a, s0 + b))
-                    nc.vector.tensor_tensor(g_rows[c][:, d, a:b], window, gate_sb[:, s0 + a : s0 + b], MULT)
+                    nc.vector.tensor_tensor(g_rows[c][:, d, a:b], window, gate_first[:, a:b], MULT)
 
         def gather_plain(c):
             s0, w = CHUNKS[c]
@@ -159,7 +160,7 @@ def tile_moe_bds_lin_none_kernel(
             return y_grouped[base][:, PACK * (t0 - base) : PACK * (t0 - base + w)]
 
         def interleave_tokens(q):
-            dst = grouped_tokens(q * TOKEN_PIECE, TOKEN_PIECE)
+            dst = grouped_tokens(TOKEN_CUTS[q], TOKEN_CUTS[q + 1] - TOKEN_CUTS[q])
             nc.vector.tensor_copy(runs_out(dst), runs_in(dy_rows[q][:]))
 
         def quantize_slots(s0, w):
@@ -197,20 +198,22 @@ def tile_moe_bds_lin_none_kernel(
         def shared_product(m, t0, bank):
             multiply(banks[bank][:], E, m, y_codes[:, t0 : t0 + BANK], y_scales[:, t0 : t0 + BANK])
 
-        firsts = {}
-        pairs = {}
+        firsts = [ring.tile([P, T], F32, name="first") for m in range(BLOCKS)]
+        pairs = {m: ring.tile([P, T], F32, name="pair") for m in range(1, BLOCKS)}
 
-        def fetch_first(m, a, b):
-            firsts[m, a] = ring.tile([P, b - a], F32, name="first")
-            nc.scalar.activation(firsts[m, a][:], dx[m][:].indirect(offsets(pos1_sb, a, b)), COPY)
+        def fetch(dst, pos_sb, m, a, b):
+            nc.scalar.activation(dst[:, a:b], dx[m][:].indirect(offsets(pos_sb, a, b)), COPY)
 
         def add_second(m, a, b):
-            pairs[m, a] = ring.tile([P, b - a], F32, name="pair")
-            nc.vector.tensor_tensor(pairs[m, a][:], dx[m][:].indirect(offsets(pos2_sb, a, b)), firsts[m, a][:], ADD)
+            window = dx[m][:].indirect(offsets(pos2_sb, a, b))
+            nc.vector.tensor_tensor(pairs[m][:, a:b], window, firsts[m][:, a:b], ADD)
 
-        def add_shared(m, a, b, bank):
+        def add_shared(dst, src, a, b, bank):
+            nc.vector.tensor_tensor(dst, src, banks[bank][:, a % BANK : a % BANK + b - a], ADD)
+
+        def finish(m, a, b, bank):
             total = ring.tile([P, b - a], F32, name="total")
-            nc.vector.tensor_tensor(total[:], pairs[m, a][:], banks[bank][:, a % BANK : a % BANK + b - a], ADD)
+            add_shared(total[:], pairs[m][:, a:b], a, b, bank)
             nc.sync.dma_start(out[P * m : P * (m + 1), a:b], total[:])
 
         gather_gated(0)
@@ -218,45 +221,66 @@ def tile_moe_bds_lin_none_kernel(
         gather_plain(2)
         interleave_slots(0)
         gather_plain(3)
-        y_grouped[0] = keep.tile([P, TOKEN_PIECE * PACK], BF16, name="y_early", align_bytes=64)
+        y_grouped[0] = keep.tile([P, TOKEN_CUTS[1] * PACK], BF16, name="y_early", align_bytes=64)
         interleave_tokens(0)
         quantize_slots(0, PAIR)
-        quantize_tokens(0, TOKEN_PIECE)
         gate_and_interleave(1, 0, CHUNKS[1][1])
         gate_and_interleave(2, 0, CHUNKS[2][1])
         quantize_slots(PAIR, PAIR)
         quantize_slots(2 * PAIR, PAIR)
-        expert_products(0, 0, bank=0)
-        expert_products(1, 0, bank=1)
-        expert_products(0, 1, bank=2)
-        expert_products(1, 1, bank=3)
-        expert_products(0, 2, bank=4)
-        expert_products(1, 2, bank=5)
-        half = CHUNKS[3][1] // 2
-        gate_and_interleave(3, 0, half)
-        gate_and_interleave(3, half, 2 * half)
+        for c in range(PAIRS - 1):
+            expert_products(0, c, bank=2 * c)
+            expert_products(1, c, bank=2 * c + 1)
+        cut = 3 * PAIR + C - CHUNKS[3][0]
+        gate_and_interleave(3, 0, cut)
+        gate_and_interleave(3, cut, CHUNKS[3][1])
         quantize_slots(3 * PAIR, C)
         quantize_slots(3 * PAIR + C, C)
-        expert_products(0, 3, bank=6)
-        y_grouped[TOKEN_PIECE] = keep.tile(
-            [P, (T - TOKEN_PIECE) * PACK], BF16, name="y_late", tag="rows0", align_bytes=64
-        )
-        for q in range(1, T // TOKEN_PIECE):
-            interleave_tokens(q)
-        quantize_tokens(TOKEN_PIECE, TOKEN_PIECE)
+        expert_products(0, 3, bank=0)
+        late = TOKEN_CUTS[1]
+        y_grouped[late] = keep.tile([P, (T - late) * PACK], BF16, name="y_late", tag="rows0", align_bytes=64)
+        interleave_tokens(1)
+        quantize_tokens(0, late)
+        quantize_tokens(late, BANK - late)
         quantize_tokens(BANK, BANK)
 
-        dx_banks = {1: {3: 7}, 2: {0: 0, 1: 1, 2: 2, 3: 3}, 3: {0: 0, 1: 1, 2: 2, 3: 3}}
-        ds_banks = {0: [4, 5], 1: [6, 7], 2: [4, 5], 3: [6, 7]}
+        pairs[0] = keep.tile([P, T], F32, name="pair0", tag=f"dy_rows{late}", align_bytes=64)
+        dx[2] = keep.tile([P, S], F32, name="dx2", tag="grouped", align_bytes=64)
+        dx[3] = keep.tile([P, S], F32, name="dx3", tag="rows0", align_bytes=64)
+        last = BLOCKS - 1
+        cuts = {last: [0, FIRST_PIECE, BOTH_FROM]}
+        fetch(firsts[0], pos1_sb, 0, 0, BANK)
+        expert_products(1, 3, bank=1)
+        fetch(firsts[0], pos1_sb, 0, BANK, T)
+        dx_banks = [6, 7, 0, 1]
+        ds_banks = {0: [2, 3], 1: [4, 5], 2: [2, 3], 3: [4, 5]}
         for m in range(BLOCKS):
-            pieces = list(zip(CUTS[m], CUTS[m][1:]))
-            for a, b in pieces:
-                fetch_first(m, a, b)
+            mine = cuts.get(m, [0, BANK, T])
             for h in range(T // BANK):
                 shared_product(m, h * BANK, ds_banks[m][h])
-            for c, bank in dx_banks.get(m + 1, {}).items():
-                expert_products(m + 1, c, bank)
-            for a, b in pieces:
+            for a, b in zip(mine, mine[1:]):
                 add_second(m, a, b)
-            for a, b in pieces:
-                add_shared(m, a, b, ds_banks[m][a // BANK])
+            if m < last:
+                nxt = cuts.get(m + 1, [0, BANK, T])
+                fetch(firsts[m + 1], pos1_sb, m + 1, nxt[0], nxt[1])
+                if m + 2 < BLOCKS:
+                    expert_products(m + 2, 0, dx_banks[0])
+                    expert_products(m + 2, 1, dx_banks[1])
+                for a, b in zip(nxt[1:], nxt[2:]):
+                    fetch(firsts[m + 1], pos1_sb, m + 1, a, b)
+                if m + 2 < BLOCKS:
+                    expert_products(m + 2, 2, dx_banks[2])
+                    expert_products(m + 2, 3, dx_banks[3])
+                for h in range(T // BANK):
+                    finish(m, h * BANK, (h + 1) * BANK, ds_banks[m][h])
+        fetch(firsts[last], pos1_sb, last, BOTH_FROM, T)
+        seconds = keep.tile([P, T], F32, name="seconds")
+        ends = [BOTH_FROM, T - LAST_PIECE, T]
+        for a, b in zip(ends, ends[1:]):
+            fetch(seconds, pos2_sb, last, a, b)
+        finish(last, 0, BANK, ds_banks[last][0])
+        add_shared(pairs[last][:, BOTH_FROM:T], firsts[last][:, BOTH_FROM:T], BOTH_FROM, T, ds_banks[last][1])
+        for a, b in zip(ends, ends[1:]):
+            total = ring.tile([P, b - a], F32, name="total")
+            nc.vector.tensor_tensor(total[:], pairs[last][:, a:b], seconds[:, a:b], ADD)
+            nc.sync.dma_start(out[P * last : P * BLOCKS, a:b], total[:])

@@ -29,9 +29,9 @@ BYTES = 4 * N * T + (E + 1) * (N * K // 2 + N * K // 32) + 4 * S + 2 * (S + 2 * 
 
 PAIR = 2 * C
 PAIRS = S // PAIR
-CHUNKS = [(0, 608), (608, 608), (1216, 448), (1664, 384)]
+CHUNKS = [(0, 608), (608, 736), (1344, 320), (1664, 384)]
 FIRST_CUTS = [0, 128, CHUNKS[0][1]]
-TOKEN_CUTS = [0, 256, T]
+TOKEN_CUTS = [0, 512, T]
 RUN = 4
 FIRST_PIECE = 256
 LAST_PIECE = 128
@@ -45,6 +45,7 @@ def tile_moe_bds_lin_none_kernel(
     with ExitStack() as ctx:
         keep = ctx.enter_context(tc.tile_pool(name="keep", bufs=1))
         ring = ctx.enter_context(tc.tile_pool(name="ring", bufs=4))
+        late = ctx.enter_context(tc.tile_pool(name="late", bufs=1))
         psum = ctx.enter_context(tc.psum_pool(name="psum", bufs=1))
 
         offs_sb = keep.tile([P, S // PER_COL], U16, name="offs_sb")
@@ -54,8 +55,8 @@ def tile_moe_bds_lin_none_kernel(
         gate_first = keep.tile([P, CHUNKS[0][1]], F32, name="gate_first", tag="rows2", align_bytes=64)
         gate_sb = keep.tile([P, S], F32, name="gate_sb")
         dy_rows = [
-            keep.tile([P, PACK, b - a], F32, name=f"dy_rows{a}", tag=f"dy_rows{a}", align_bytes=64)
-            for a, b in zip(TOKEN_CUTS, TOKEN_CUTS[1:])
+            keep.tile([P, PACK, BANK], F32, name="dy_rows0", align_bytes=64),
+            late.tile([P, PACK, BANK], F32, name="dy_rows1", offset=0),
         ]
         w_cuts = [0, 2, 6, E + 1]
         w_sb = [
@@ -102,19 +103,19 @@ def tile_moe_bds_lin_none_kernel(
         load_plane(1)
         load_plane(2)
         load_plane(3)
-        load_rows(0)
         load_gate(CHUNKS[1][0], CHUNKS[3][0])
+        nc.sync.dma_start(pos1_sb[:], pos1)
+        nc.sync.dma_start(pos2_sb[:], pos2)
         for q in range(4):
             load_bytes(
                 w_sc[32 * q : 32 * q + 4, :, :], w_scales[:, 0, 4 * q : 4 * q + 4, :].rearrange("e f k -> f e k")
             )
         load_weights(0)
+        load_rows(0)
         load_rows(1)
         load_weights(1)
         load_gate(CHUNKS[3][0], S)
         load_weights(2)
-        nc.sync.dma_start(pos1_sb[:], pos1)
-        nc.sync.dma_start(pos2_sb[:], pos2)
 
         def runs_out(dst):
             return dst.rearrange("p (c i t) -> p c t i", i=RUN, t=PACK)
@@ -199,21 +200,27 @@ def tile_moe_bds_lin_none_kernel(
             multiply(banks[bank][:], E, m, y_codes[:, t0 : t0 + BANK], y_scales[:, t0 : t0 + BANK])
 
         firsts = [ring.tile([P, T], F32, name="first") for m in range(BLOCKS)]
-        pairs = {m: ring.tile([P, T], F32, name="pair") for m in range(1, BLOCKS)}
+        pairs = {}
+
+        def pair(m, a, b):
+            t0 = a - a % BANK
+            if (m, t0) not in pairs:
+                pairs[m, t0] = late.tile([P, BANK], F32, name=f"pair{m}_{t0}", tag=f"half{t0}", offset=4 * t0)
+            return pairs[m, t0][:, a - t0 : b - t0]
 
         def fetch(dst, pos_sb, m, a, b):
             nc.scalar.activation(dst[:, a:b], dx[m][:].indirect(offsets(pos_sb, a, b)), COPY)
 
         def add_second(m, a, b):
             window = dx[m][:].indirect(offsets(pos2_sb, a, b))
-            nc.vector.tensor_tensor(pairs[m][:, a:b], window, firsts[m][:, a:b], ADD)
+            nc.vector.tensor_tensor(pair(m, a, b), window, firsts[m][:, a:b], ADD)
 
         def add_shared(dst, src, a, b, bank):
             nc.vector.tensor_tensor(dst, src, banks[bank][:, a % BANK : a % BANK + b - a], ADD)
 
         def finish(m, a, b, bank):
             total = ring.tile([P, b - a], F32, name="total")
-            add_shared(total[:], pairs[m][:, a:b], a, b, bank)
+            add_shared(total[:], pair(m, a, b), a, b, bank)
             nc.sync.dma_start(out[P * m : P * (m + 1), a:b], total[:])
 
         gather_gated(0)
@@ -221,8 +228,6 @@ def tile_moe_bds_lin_none_kernel(
         gather_plain(2)
         interleave_slots(0)
         gather_plain(3)
-        y_grouped[0] = keep.tile([P, TOKEN_CUTS[1] * PACK], BF16, name="y_early", align_bytes=64)
-        interleave_tokens(0)
         quantize_slots(0, PAIR)
         gate_and_interleave(1, 0, CHUNKS[1][1])
         gate_and_interleave(2, 0, CHUNKS[2][1])
@@ -237,14 +242,12 @@ def tile_moe_bds_lin_none_kernel(
         quantize_slots(3 * PAIR, C)
         quantize_slots(3 * PAIR + C, C)
         expert_products(0, 3, bank=0)
-        late = TOKEN_CUTS[1]
-        y_grouped[late] = keep.tile([P, (T - late) * PACK], BF16, name="y_late", tag="rows0", align_bytes=64)
+        y_grouped[0] = keep.tile([P, T * PACK], BF16, name="y_grouped", tag="rows0", align_bytes=64)
+        interleave_tokens(0)
         interleave_tokens(1)
-        quantize_tokens(0, late)
-        quantize_tokens(late, BANK - late)
+        quantize_tokens(0, BANK)
         quantize_tokens(BANK, BANK)
 
-        pairs[0] = keep.tile([P, T], F32, name="pair0", tag=f"dy_rows{late}", align_bytes=64)
         dx[2] = keep.tile([P, S], F32, name="dx2", tag="grouped", align_bytes=64)
         dx[3] = keep.tile([P, S], F32, name="dx3", tag="rows0", align_bytes=64)
         last = BLOCKS - 1
@@ -252,7 +255,7 @@ def tile_moe_bds_lin_none_kernel(
         fetch(firsts[0], pos1_sb, 0, 0, BANK)
         expert_products(1, 3, bank=1)
         fetch(firsts[0], pos1_sb, 0, BANK, T)
-        dx_banks = [6, 7, 0, 1]
+        dx_banks = {2: [6, 7, 0, 1], 3: [6, 7, 0, 1]}
         ds_banks = {0: [2, 3], 1: [4, 5], 2: [2, 3], 3: [4, 5]}
         for m in range(BLOCKS):
             mine = cuts.get(m, [0, BANK, T])
@@ -264,23 +267,23 @@ def tile_moe_bds_lin_none_kernel(
                 nxt = cuts.get(m + 1, [0, BANK, T])
                 fetch(firsts[m + 1], pos1_sb, m + 1, nxt[0], nxt[1])
                 if m + 2 < BLOCKS:
-                    expert_products(m + 2, 0, dx_banks[0])
-                    expert_products(m + 2, 1, dx_banks[1])
+                    expert_products(m + 2, 0, dx_banks[m + 2][0])
+                    expert_products(m + 2, 1, dx_banks[m + 2][1])
                 for a, b in zip(nxt[1:], nxt[2:]):
                     fetch(firsts[m + 1], pos1_sb, m + 1, a, b)
-                if m + 2 < BLOCKS:
-                    expert_products(m + 2, 2, dx_banks[2])
-                    expert_products(m + 2, 3, dx_banks[3])
                 for h in range(T // BANK):
                     finish(m, h * BANK, (h + 1) * BANK, ds_banks[m][h])
+                if m + 2 < BLOCKS:
+                    expert_products(m + 2, 2, dx_banks[m + 2][2])
+                    expert_products(m + 2, 3, dx_banks[m + 2][3])
         fetch(firsts[last], pos1_sb, last, BOTH_FROM, T)
         seconds = keep.tile([P, T], F32, name="seconds")
         ends = [BOTH_FROM, T - LAST_PIECE, T]
         for a, b in zip(ends, ends[1:]):
             fetch(seconds, pos2_sb, last, a, b)
         finish(last, 0, BANK, ds_banks[last][0])
-        add_shared(pairs[last][:, BOTH_FROM:T], firsts[last][:, BOTH_FROM:T], BOTH_FROM, T, ds_banks[last][1])
+        add_shared(pair(last, BOTH_FROM, T), firsts[last][:, BOTH_FROM:T], BOTH_FROM, T, ds_banks[last][1])
         for a, b in zip(ends, ends[1:]):
             total = ring.tile([P, b - a], F32, name="total")
-            nc.vector.tensor_tensor(total[:], pairs[last][:, a:b], seconds[:, a:b], ADD)
+            nc.vector.tensor_tensor(total[:], pair(last, a, b), seconds[:, a:b], ADD)
             nc.sync.dma_start(out[P * last : P * BLOCKS, a:b], total[:])

@@ -54,16 +54,11 @@ def tile_moe_bds_lin_none_kernel(
         planes = [keep.tile([P, T], F32, name=f"plane{d}") for d in range(PACK)]
         gate_first = keep.tile([P, CHUNKS[0][1]], F32, name="gate_first", tag="rows2", align_bytes=64)
         gate_sb = keep.tile([P, S], F32, name="gate_sb")
-        dy_rows = [
-            keep.tile([P, PACK, BANK], F32, name="dy_rows0", align_bytes=64),
-            late.tile([P, PACK, BANK], F32, name="dy_rows1", offset=0),
-        ]
-        w_cuts = [0, 2, 6, E + 1]
-        w_sb = [
-            keep.tile([P, b - a, 2 * K], U8, name=f"w_sb{a}", align_bytes=64) for a, b in zip(w_cuts, w_cuts[1:])
-        ]
+        dy_rows = late.tile([P, PACK, T], F32, name="dy_rows", offset=0)
+        w_front = keep.tile([P, E, 2 * K - BLOCK_BYTES], U8, name="w_front", align_bytes=64)
+        w_shared = keep.tile([P, 2 * K], U8, name="w_shared", align_bytes=64)
         w_sc = keep.tile([P, E + 1, K], U8, name="w_sc", align_bytes=64)
-        dx = {m: keep.tile([P, S], F32, name=f"dx{m}") for m in (0, 1)}
+        dx = {m: keep.tile([P, S], F32, name=f"dx{m}") for m in (0, 1, 3)}
         banks = [psum.tile([P, BANK], F32, name=f"bank{b}") for b in range(8)]
         g_codes = keep.tile([P, S], U32, name="g_codes", align_bytes=64)
         g_scales = keep.tile([P, S], U8, name="g_scales", align_bytes=64)
@@ -87,14 +82,8 @@ def tile_moe_bds_lin_none_kernel(
         def load_gate(s0, s1):
             nc.sync.dma_start(gate_sb[:, s0:s1], gate[0:P, s0:s1])
 
-        def load_rows(q):
-            nc.sync.dma_start(dy_rows[q][:], dy_view[:, :, TOKEN_CUTS[q] : TOKEN_CUTS[q + 1]])
-
         def load_bytes(dst, src):
             nc.sync.dma_start(dst.bitcast(I32), src.bitcast(I32))
-
-        def load_weights(i):
-            load_bytes(w_sb[i][:], words[:, w_cuts[i] : w_cuts[i + 1], :])
 
         nc.sync.dma_start(offs_sb[:], offs)
         load_plane(0)
@@ -103,19 +92,16 @@ def tile_moe_bds_lin_none_kernel(
         load_plane(1)
         load_plane(2)
         load_plane(3)
-        load_gate(CHUNKS[1][0], CHUNKS[3][0])
+        load_gate(CHUNKS[1][0], S)
         nc.sync.dma_start(pos1_sb[:], pos1)
         nc.sync.dma_start(pos2_sb[:], pos2)
         for q in range(4):
             load_bytes(
                 w_sc[32 * q : 32 * q + 4, :, :], w_scales[:, 0, 4 * q : 4 * q + 4, :].rearrange("e f k -> f e k")
             )
-        load_weights(0)
-        load_rows(0)
-        load_rows(1)
-        load_weights(1)
-        load_gate(CHUNKS[3][0], S)
-        load_weights(2)
+        load_bytes(w_front[:], words[:, 0:E, 0 : 2 * K - BLOCK_BYTES])
+        load_bytes(w_shared[:], w_words[E, 0])
+        nc.sync.dma_start(dy_rows[:], dy_view)
 
         def runs_out(dst):
             return dst.rearrange("p (c i t) -> p c t i", i=RUN, t=PACK)
@@ -162,7 +148,7 @@ def tile_moe_bds_lin_none_kernel(
 
         def interleave_tokens(q):
             dst = grouped_tokens(TOKEN_CUTS[q], TOKEN_CUTS[q + 1] - TOKEN_CUTS[q])
-            nc.vector.tensor_copy(runs_out(dst), runs_in(dy_rows[q][:]))
+            nc.vector.tensor_copy(runs_out(dst), runs_in(dy_rows[:, :, TOKEN_CUTS[q] : TOKEN_CUTS[q + 1]]))
 
         def quantize_slots(s0, w):
             nc.vector.quantize_mx(
@@ -179,10 +165,15 @@ def tile_moe_bds_lin_none_kernel(
             )
 
         def multiply(acc, e, m, codes, scales):
-            i = max(j for j in range(len(w_sb)) if w_cuts[j] <= e)
+            if e == E:
+                weights = w_shared[:, BLOCK_BYTES * m : BLOCK_BYTES * (m + 1)]
+            elif m < BLOCKS - 1:
+                weights = w_front[:, e, BLOCK_BYTES * m : BLOCK_BYTES * (m + 1)]
+            else:
+                weights = w_last[:, e, :]
             nc.tensor.matmul_mx(
                 out=acc,
-                lhsT=w_sb[i][:, e - w_cuts[i], BLOCK_BYTES * m : BLOCK_BYTES * (m + 1)].bitcast(FP4X4),
+                lhsT=weights.bitcast(FP4X4),
                 lhsT_scale=w_sc[:, e, P * m : P * (m + 1)],
                 rhs=codes.bitcast(FP8X4),
                 rhs_scale=scales,
@@ -249,13 +240,14 @@ def tile_moe_bds_lin_none_kernel(
         quantize_tokens(BANK, BANK)
 
         dx[2] = keep.tile([P, S], F32, name="dx2", tag="grouped", align_bytes=64)
-        dx[3] = keep.tile([P, S], F32, name="dx3", tag="rows0", align_bytes=64)
+        w_last = keep.tile([P, E, BLOCK_BYTES], U8, name="w_last", tag="rows0", align_bytes=64)
+        load_bytes(w_last[:], words[:, 0:E, 2 * K - BLOCK_BYTES :])
         last = BLOCKS - 1
         cuts = {last: [0, FIRST_PIECE, BOTH_FROM]}
         fetch(firsts[0], pos1_sb, 0, 0, BANK)
         expert_products(1, 3, bank=1)
         fetch(firsts[0], pos1_sb, 0, BANK, T)
-        dx_banks = {2: [6, 7, 0, 1], 3: [6, 7, 0, 1]}
+        dx_banks = [6, 7, 0, 1]
         ds_banks = {0: [2, 3], 1: [4, 5], 2: [2, 3], 3: [4, 5]}
         for m in range(BLOCKS):
             mine = cuts.get(m, [0, BANK, T])
@@ -265,24 +257,21 @@ def tile_moe_bds_lin_none_kernel(
                 add_second(m, a, b)
             if m < last:
                 nxt = cuts.get(m + 1, [0, BANK, T])
-                fetch(firsts[m + 1], pos1_sb, m + 1, nxt[0], nxt[1])
-                if m + 2 < BLOCKS:
-                    expert_products(m + 2, 0, dx_banks[m + 2][0])
-                    expert_products(m + 2, 1, dx_banks[m + 2][1])
-                for a, b in zip(nxt[1:], nxt[2:]):
+                for a, b in zip(nxt, nxt[1:]):
                     fetch(firsts[m + 1], pos1_sb, m + 1, a, b)
+                if m + 2 < BLOCKS:
+                    for c in range(PAIRS):
+                        expert_products(m + 2, c, dx_banks[c])
                 for h in range(T // BANK):
                     finish(m, h * BANK, (h + 1) * BANK, ds_banks[m][h])
-                if m + 2 < BLOCKS:
-                    expert_products(m + 2, 2, dx_banks[m + 2][2])
-                    expert_products(m + 2, 3, dx_banks[m + 2][3])
         fetch(firsts[last], pos1_sb, last, BOTH_FROM, T)
         seconds = keep.tile([P, T], F32, name="seconds")
         ends = [BOTH_FROM, T - LAST_PIECE, T]
         for a, b in zip(ends, ends[1:]):
             fetch(seconds, pos2_sb, last, a, b)
-        finish(last, 0, BANK, ds_banks[last][0])
+        finish(last, 0, FIRST_PIECE, ds_banks[last][0])
         add_shared(pair(last, BOTH_FROM, T), firsts[last][:, BOTH_FROM:T], BOTH_FROM, T, ds_banks[last][1])
+        finish(last, FIRST_PIECE, BOTH_FROM, ds_banks[last][0])
         for a, b in zip(ends, ends[1:]):
             total = ring.tile([P, b - a], F32, name="total")
             nc.vector.tensor_tensor(total[:], pair(last, a, b), seconds[:, a:b], ADD)

@@ -29,13 +29,12 @@ BYTES = 4 * N * T + (E + 1) * (N * K // 2 + N * K // 32) + 4 * S + 2 * (S + 2 * 
 
 PAIR = 2 * C
 PAIRS = S // PAIR
+LAST = BLOCKS - 1
 CHUNKS = [(0, 608), (608, 736), (1344, 320), (1664, 384)]
 FIRST_CUTS = [0, 128, CHUNKS[0][1]]
-TOKEN_CUTS = [0, 512, T]
 RUN = 4
 FIRST_PIECE = 256
 LAST_PIECE = 128
-BOTH_FROM = 512
 
 
 def tile_moe_bds_lin_none_kernel(
@@ -44,7 +43,7 @@ def tile_moe_bds_lin_none_kernel(
     nc = tc.nc
     with ExitStack() as ctx:
         keep = ctx.enter_context(tc.tile_pool(name="keep", bufs=1))
-        ring = ctx.enter_context(tc.tile_pool(name="ring", bufs=4))
+        ring = ctx.enter_context(tc.tile_pool(name="ring", bufs=BLOCKS))
         late = ctx.enter_context(tc.tile_pool(name="late", bufs=1))
         psum = ctx.enter_context(tc.psum_pool(name="psum", bufs=1))
 
@@ -53,18 +52,20 @@ def tile_moe_bds_lin_none_kernel(
         pos2_sb = keep.tile([P, T // PER_COL], U16, name="pos2_sb")
         planes = [keep.tile([P, T], F32, name=f"plane{d}") for d in range(PACK)]
         gate_first = keep.tile([P, CHUNKS[0][1]], F32, name="gate_first", tag="rows2", align_bytes=64)
-        gate_sb = keep.tile([P, S], F32, name="gate_sb")
-        dy_rows = late.tile([P, PACK, T], F32, name="dy_rows", offset=0)
-        w_front = keep.tile([P, E, 2 * K - BLOCK_BYTES], U8, name="w_front", align_bytes=64)
+        gate_rest = keep.tile([P, S - CHUNKS[0][1]], F32, name="gate_rest")
+        dy_rows = [
+            keep.tile([P, PACK, BANK], F32, name="dy_rows0", align_bytes=64),
+            late.tile([P, PACK, BANK], F32, name="dy_rows1", offset=0, align_bytes=64),
+        ]
+        w_front = keep.tile([P, E, 2 * BLOCK_BYTES], U8, name="w_front", align_bytes=64)
+        w_third = keep.tile([P, E, BLOCK_BYTES], U8, name="w_third", align_bytes=64)
         w_shared = keep.tile([P, 2 * K], U8, name="w_shared", align_bytes=64)
         w_sc = keep.tile([P, E + 1, K], U8, name="w_sc", align_bytes=64)
-        dx = {m: keep.tile([P, S], F32, name=f"dx{m}") for m in (0, 1, 3)}
+        dx = {m: keep.tile([P, S], F32, name=f"dx{m}") for m in (0, 1, LAST)}
         banks = [psum.tile([P, BANK], F32, name=f"bank{b}") for b in range(8)]
         g_codes = keep.tile([P, S], U32, name="g_codes", align_bytes=64)
         g_scales = keep.tile([P, S], U8, name="g_scales", align_bytes=64)
         g_grouped = keep.tile([P, S * PACK], BF16, name="g_grouped", tag="grouped", align_bytes=64)
-        y_grouped = {}
-        y_codes = keep.tile([P, T], U32, name="y_codes", align_bytes=64)
         y_scales = keep.tile([P, T], U8, name="y_scales", align_bytes=64)
         g_rows = {}
 
@@ -76,32 +77,34 @@ def tile_moe_bds_lin_none_kernel(
         dy_view = dyT.rearrange("(p d) x -> p d x", d=PACK)
         words = w_words.rearrange("e a p b -> p (e a) b")
 
-        def load_plane(d):
-            nc.sync.dma_start(planes[d][:], dy_view[:, d, :])
+        def load_gate(dst, first, s0, s1):
+            nc.sync.dma_start(dst[:, s0 - first : s1 - first], gate[0:P, s0:s1])
 
-        def load_gate(s0, s1):
-            nc.sync.dma_start(gate_sb[:, s0:s1], gate[0:P, s0:s1])
+        def load_rows(h):
+            nc.sync.dma_start(dy_rows[h][:], dy_view[:, :, h * BANK : (h + 1) * BANK])
 
         def load_bytes(dst, src):
             nc.sync.dma_start(dst.bitcast(I32), src.bitcast(I32))
 
         nc.sync.dma_start(offs_sb[:], offs)
-        load_plane(0)
+        nc.sync.dma_start(planes[0][:], dy_view[:, 0, :])
         for a, b in zip(FIRST_CUTS, FIRST_CUTS[1:]):
-            nc.sync.dma_start(gate_first[:, a:b], gate[0:P, a:b])
-        load_plane(1)
-        load_plane(2)
-        load_plane(3)
-        load_gate(CHUNKS[1][0], S)
-        nc.sync.dma_start(pos1_sb[:], pos1)
-        nc.sync.dma_start(pos2_sb[:], pos2)
+            load_gate(gate_first, 0, a, b)
+        for d in range(1, PACK):
+            nc.sync.dma_start(planes[d][:], dy_view[:, d, :])
+        load_gate(gate_rest, CHUNKS[1][0], CHUNKS[1][0], CHUNKS[3][0])
         for q in range(4):
             load_bytes(
                 w_sc[32 * q : 32 * q + 4, :, :], w_scales[:, 0, 4 * q : 4 * q + 4, :].rearrange("e f k -> f e k")
             )
-        load_bytes(w_front[:], words[:, 0:E, 0 : 2 * K - BLOCK_BYTES])
+        load_bytes(w_front[:], words[:, 0:E, 0 : 2 * BLOCK_BYTES])
+        load_gate(gate_rest, CHUNKS[1][0], CHUNKS[3][0], S)
+        load_rows(0)
+        nc.sync.dma_start(pos1_sb[:], pos1)
+        nc.sync.dma_start(pos2_sb[:], pos2)
+        load_rows(1)
         load_bytes(w_shared[:], w_words[E, 0])
-        nc.sync.dma_start(dy_rows[:], dy_view)
+        load_bytes(w_third[:], words[:, 0:E, 2 * BLOCK_BYTES : 3 * BLOCK_BYTES])
 
         def runs_out(dst):
             return dst.rearrange("p (c i t) -> p c t i", i=RUN, t=PACK)
@@ -112,65 +115,48 @@ def tile_moe_bds_lin_none_kernel(
         def offsets(lst, a, b):
             return lst[:, a // PER_COL : b // PER_COL]
 
-        def gather_gated(c):
-            s0, w = CHUNKS[c]
-            g_rows[c] = keep.tile([P, PACK, w], F32, name=f"g_rows{c}", tag=f"rows{c % 3}", align_bytes=64)
+        def rows_tile(c):
+            g_rows[c] = keep.tile([P, PACK, CHUNKS[c][1]], F32, name=f"g_rows{c}", tag=f"rows{c % 3}", align_bytes=64)
+            return g_rows[c]
+
+        def gather_gated():
+            rows = rows_tile(0)
             for d in range(PACK):
-                cuts = FIRST_CUTS if d == 0 else [0, w]
+                cuts = FIRST_CUTS if d == 0 else [0, CHUNKS[0][1]]
                 for a, b in zip(cuts, cuts[1:]):
-                    window = planes[d][:].indirect(offsets(offs_sb, s0 + a, s0 + b))
-                    nc.vector.tensor_tensor(g_rows[c][:, d, a:b], window, gate_first[:, a:b], MULT)
+                    window = planes[d][:].indirect(offsets(offs_sb, a, b))
+                    nc.vector.tensor_tensor(rows[:, d, a:b], window, gate_first[:, a:b], MULT)
 
         def gather_plain(c):
             s0, w = CHUNKS[c]
-            g_rows[c] = keep.tile([P, PACK, w], F32, name=f"g_rows{c}", tag=f"rows{c % 3}", align_bytes=64)
+            rows = rows_tile(c)
             for d in range(PACK):
-                window = planes[d][:].indirect(offsets(offs_sb, s0, s0 + w))
-                nc.scalar.activation(g_rows[c][:, d, :], window, COPY)
+                nc.scalar.activation(rows[:, d, :], planes[d][:].indirect(offsets(offs_sb, s0, s0 + w)), COPY)
 
-        def interleave_slots(c):
-            s0, w = CHUNKS[c]
-            nc.vector.tensor_copy(runs_out(g_grouped[:, PACK * s0 : PACK * (s0 + w)]), runs_in(g_rows[c][:]))
+        def interleave(dst, src):
+            nc.vector.tensor_copy(runs_out(dst), runs_in(src))
 
-        def gate_and_interleave(c, a, b):
-            s0 = CHUNKS[c][0]
-            weights = gate_sb[:, s0 + a : s0 + b].rearrange("p (c i) -> p c i", i=RUN).unsqueeze(2)
+        def gate_and_interleave(c, s0, s1):
+            gates = gate_rest[:, s0 - CHUNKS[1][0] : s1 - CHUNKS[1][0]].rearrange("p (c i) -> p c i", i=RUN)
             nc.vector.tensor_tensor(
-                runs_out(g_grouped[:, PACK * (s0 + a) : PACK * (s0 + b)]),
-                runs_in(g_rows[c][:, :, a:b]),
-                weights.to_broadcast([P, (b - a) // RUN, PACK, RUN]),
+                runs_out(g_grouped[:, PACK * s0 : PACK * s1]),
+                runs_in(g_rows[c][:, :, s0 - CHUNKS[c][0] : s1 - CHUNKS[c][0]]),
+                gates.unsqueeze(2).to_broadcast([P, (s1 - s0) // RUN, PACK, RUN]),
                 MULT,
             )
 
-        def grouped_tokens(t0, w):
-            base = max(b for b in y_grouped if b <= t0)
-            return y_grouped[base][:, PACK * (t0 - base) : PACK * (t0 - base + w)]
-
-        def interleave_tokens(q):
-            dst = grouped_tokens(TOKEN_CUTS[q], TOKEN_CUTS[q + 1] - TOKEN_CUTS[q])
-            nc.vector.tensor_copy(runs_out(dst), runs_in(dy_rows[:, :, TOKEN_CUTS[q] : TOKEN_CUTS[q + 1]]))
-
-        def quantize_slots(s0, w):
+        def quantize(codes, scales, grouped, a, b):
             nc.vector.quantize_mx(
-                out=g_codes[:, s0 : s0 + w].bitcast(FP8X4),
-                scales=g_scales[:, s0 : s0 + w],
-                in_=g_grouped[:, PACK * s0 : PACK * (s0 + w)],
-            )
-
-        def quantize_tokens(t0, w):
-            nc.vector.quantize_mx(
-                out=y_codes[:, t0 : t0 + w].bitcast(FP8X4),
-                scales=y_scales[:, t0 : t0 + w],
-                in_=grouped_tokens(t0, w),
+                out=codes[:, a:b].bitcast(FP8X4), scales=scales[:, a:b], in_=grouped[:, PACK * a : PACK * b]
             )
 
         def multiply(acc, e, m, codes, scales):
             if e == E:
                 weights = w_shared[:, BLOCK_BYTES * m : BLOCK_BYTES * (m + 1)]
-            elif m < BLOCKS - 1:
+            elif m < 2:
                 weights = w_front[:, e, BLOCK_BYTES * m : BLOCK_BYTES * (m + 1)]
             else:
-                weights = w_last[:, e, :]
+                weights = (w_third, w_last)[m - 2][:, e, :]
             nc.tensor.matmul_mx(
                 out=acc,
                 lhsT=weights.bitcast(FP4X4),
@@ -191,88 +177,86 @@ def tile_moe_bds_lin_none_kernel(
             multiply(banks[bank][:], E, m, y_codes[:, t0 : t0 + BANK], y_scales[:, t0 : t0 + BANK])
 
         firsts = [ring.tile([P, T], F32, name="first") for m in range(BLOCKS)]
-        pairs = {}
+        partials = {}
 
-        def pair(m, a, b):
+        def partial(m, a, b):
             t0 = a - a % BANK
-            if (m, t0) not in pairs:
-                pairs[m, t0] = late.tile([P, BANK], F32, name=f"pair{m}_{t0}", tag=f"half{t0}", offset=4 * t0)
-            return pairs[m, t0][:, a - t0 : b - t0]
+            if (m, t0) not in partials:
+                partials[m, t0] = late.tile([P, BANK], F32, name=f"partial{m}_{t0}", tag=f"half{t0}", offset=4 * t0)
+            return partials[m, t0][:, a - t0 : b - t0]
 
         def fetch(dst, pos_sb, m, a, b):
-            nc.scalar.activation(dst[:, a:b], dx[m][:].indirect(offsets(pos_sb, a, b)), COPY)
+            nc.scalar.activation(dst, dx[m][:].indirect(offsets(pos_sb, a, b)), COPY)
 
         def add_second(m, a, b):
             window = dx[m][:].indirect(offsets(pos2_sb, a, b))
-            nc.vector.tensor_tensor(pair(m, a, b), window, firsts[m][:, a:b], ADD)
+            nc.vector.tensor_tensor(partial(m, a, b), window, firsts[m][:, a:b], ADD)
 
-        def add_shared(dst, src, a, b, bank):
-            nc.vector.tensor_tensor(dst, src, banks[bank][:, a % BANK : a % BANK + b - a], ADD)
+        def shared_sums(m, a, b):
+            return banks[ds_banks[m % 2][a // BANK]][:, a % BANK : a % BANK + b - a]
 
-        def finish(m, a, b, bank):
+        def finish(m, a, b, term):
             total = ring.tile([P, b - a], F32, name="total")
-            add_shared(total[:], pair(m, a, b), a, b, bank)
+            nc.vector.tensor_tensor(total[:], partial(m, a, b), term, ADD)
             nc.sync.dma_start(out[P * m : P * (m + 1), a:b], total[:])
 
-        gather_gated(0)
+        gather_gated()
         gather_plain(1)
         gather_plain(2)
-        interleave_slots(0)
+        interleave(g_grouped[:, 0 : PACK * CHUNKS[0][1]], g_rows[0][:])
         gather_plain(3)
-        quantize_slots(0, PAIR)
-        gate_and_interleave(1, 0, CHUNKS[1][1])
-        gate_and_interleave(2, 0, CHUNKS[2][1])
-        quantize_slots(PAIR, PAIR)
-        quantize_slots(2 * PAIR, PAIR)
+        quantize(g_codes, g_scales, g_grouped, 0, PAIR)
+        gate_and_interleave(1, CHUNKS[1][0], CHUNKS[2][0])
+        gate_and_interleave(2, CHUNKS[2][0], CHUNKS[3][0])
+        quantize(g_codes, g_scales, g_grouped, PAIR, 2 * PAIR)
+        quantize(g_codes, g_scales, g_grouped, 2 * PAIR, 3 * PAIR)
         for c in range(PAIRS - 1):
             expert_products(0, c, bank=2 * c)
             expert_products(1, c, bank=2 * c + 1)
-        cut = 3 * PAIR + C - CHUNKS[3][0]
-        gate_and_interleave(3, 0, cut)
-        gate_and_interleave(3, cut, CHUNKS[3][1])
-        quantize_slots(3 * PAIR, C)
-        quantize_slots(3 * PAIR + C, C)
-        expert_products(0, 3, bank=0)
-        y_grouped[0] = keep.tile([P, T * PACK], BF16, name="y_grouped", tag="rows0", align_bytes=64)
-        interleave_tokens(0)
-        interleave_tokens(1)
-        quantize_tokens(0, BANK)
-        quantize_tokens(BANK, BANK)
+        gate_and_interleave(3, CHUNKS[3][0], S - C)
+        gate_and_interleave(3, S - C, S)
+        quantize(g_codes, g_scales, g_grouped, S - PAIR, S - C)
+        quantize(g_codes, g_scales, g_grouped, S - C, S)
+        expert_products(0, PAIRS - 1, bank=0)
+
+        y_grouped = keep.tile([P, T * PACK], BF16, name="y_grouped", tag="rows0", align_bytes=64)
+        for h in range(T // BANK):
+            interleave(y_grouped[:, PACK * BANK * h : PACK * BANK * (h + 1)], dy_rows[h][:])
+        y_codes = late.tile([P, T], U32, name="y_codes", offset=4 * T, align_bytes=64)
+        for t0 in range(0, T, BANK):
+            quantize(y_codes, y_scales, y_grouped, t0, t0 + BANK)
 
         dx[2] = keep.tile([P, S], F32, name="dx2", tag="grouped", align_bytes=64)
         w_last = keep.tile([P, E, BLOCK_BYTES], U8, name="w_last", tag="rows0", align_bytes=64)
-        load_bytes(w_last[:], words[:, 0:E, 2 * K - BLOCK_BYTES :])
-        last = BLOCKS - 1
-        cuts = {last: [0, FIRST_PIECE, BOTH_FROM]}
-        fetch(firsts[0], pos1_sb, 0, 0, BANK)
-        expert_products(1, 3, bank=1)
-        fetch(firsts[0], pos1_sb, 0, BANK, T)
+        load_bytes(w_last[:], words[:, 0:E, LAST * BLOCK_BYTES :])
+
         dx_banks = [6, 7, 0, 1]
-        ds_banks = {0: [2, 3], 1: [4, 5], 2: [2, 3], 3: [4, 5]}
+        ds_banks = [[2, 3], [4, 5]]
+        cuts = [[0, BANK, T]] * LAST + [[0, FIRST_PIECE, BANK]]
+        fetch(firsts[0][:, 0:BANK], pos1_sb, 0, 0, BANK)
+        expert_products(1, PAIRS - 1, bank=1)
+        fetch(firsts[0][:, BANK:T], pos1_sb, 0, BANK, T)
         for m in range(BLOCKS):
-            mine = cuts.get(m, [0, BANK, T])
             for h in range(T // BANK):
-                shared_product(m, h * BANK, ds_banks[m][h])
-            for a, b in zip(mine, mine[1:]):
+                shared_product(m, h * BANK, ds_banks[m % 2][h])
+            for a, b in zip(cuts[m], cuts[m][1:]):
                 add_second(m, a, b)
-            if m < last:
-                nxt = cuts.get(m + 1, [0, BANK, T])
-                for a, b in zip(nxt, nxt[1:]):
-                    fetch(firsts[m + 1], pos1_sb, m + 1, a, b)
+            if m < LAST:
+                for a, b in zip(cuts[m + 1], cuts[m + 1][1:]):
+                    fetch(firsts[m + 1][:, a:b], pos1_sb, m + 1, a, b)
                 if m + 2 < BLOCKS:
                     for c in range(PAIRS):
                         expert_products(m + 2, c, dx_banks[c])
-                for h in range(T // BANK):
-                    finish(m, h * BANK, (h + 1) * BANK, ds_banks[m][h])
-        fetch(firsts[last], pos1_sb, last, BOTH_FROM, T)
-        seconds = keep.tile([P, T], F32, name="seconds")
-        ends = [BOTH_FROM, T - LAST_PIECE, T]
+                for t0 in range(0, T, BANK):
+                    finish(m, t0, t0 + BANK, shared_sums(m, t0, t0 + BANK))
+
+        fetch(firsts[LAST][:, BANK:T], pos1_sb, LAST, BANK, T)
+        seconds = keep.tile([P, T - BANK], F32, name="seconds")
+        ends = [BANK, T - LAST_PIECE, T]
         for a, b in zip(ends, ends[1:]):
-            fetch(seconds, pos2_sb, last, a, b)
-        finish(last, 0, FIRST_PIECE, ds_banks[last][0])
-        add_shared(pair(last, BOTH_FROM, T), firsts[last][:, BOTH_FROM:T], BOTH_FROM, T, ds_banks[last][1])
-        finish(last, FIRST_PIECE, BOTH_FROM, ds_banks[last][0])
+            fetch(seconds[:, a - BANK : b - BANK], pos2_sb, LAST, a, b)
+        finish(LAST, 0, FIRST_PIECE, shared_sums(LAST, 0, FIRST_PIECE))
+        nc.vector.tensor_tensor(partial(LAST, BANK, T), firsts[LAST][:, BANK:T], shared_sums(LAST, BANK, T), ADD)
+        finish(LAST, FIRST_PIECE, BANK, shared_sums(LAST, FIRST_PIECE, BANK))
         for a, b in zip(ends, ends[1:]):
-            total = ring.tile([P, b - a], F32, name="total")
-            nc.vector.tensor_tensor(total[:], pair(last, a, b), seconds[:, a:b], ADD)
-            nc.sync.dma_start(out[P * last : P * BLOCKS, a:b], total[:])
+            finish(LAST, a, b, seconds[:, a - BANK : b - BANK])

@@ -167,11 +167,13 @@ def tile_moe_bds_lin_none_kernel(
                 stop=True,
             )
 
-        def expert_products(m, c, bank):
-            s0 = c * PAIR
-            for j in range(s0, s0 + PAIR, C):
+        def expert_sums(m, s0, s1, bank):
+            for j in range(s0, s1, C):
                 multiply(banks[bank][:, j - s0 : j - s0 + C], j // C, m, g_codes[:, j : j + C], g_scales[:, j : j + C])
-            nc.scalar.copy(out=dx[m][:, s0 : s0 + PAIR], in_=banks[bank][:])
+            return banks[bank][:, 0 : s1 - s0]
+
+        def expert_products(m, c, bank):
+            nc.scalar.copy(out=dx[m][:, c * PAIR : (c + 1) * PAIR], in_=expert_sums(m, c * PAIR, (c + 1) * PAIR, bank))
 
         def shared_product(m, t0, bank):
             multiply(banks[bank][:], E, m, y_codes[:, t0 : t0 + BANK], y_scales[:, t0 : t0 + BANK])
@@ -244,9 +246,14 @@ def tile_moe_bds_lin_none_kernel(
             if m < LAST:
                 for a, b in zip(cuts[m + 1], cuts[m + 1][1:]):
                     fetch(firsts[m + 1][:, a:b], pos1_sb, m + 1, a, b)
-                if m + 2 < BLOCKS:
+                if m + 2 < LAST:
                     for c in range(PAIRS):
                         expert_products(m + 2, c, dx_banks[c])
+                if m + 2 == LAST:
+                    for c in range(PAIRS - 1):
+                        expert_products(LAST, c, dx_banks[c])
+                    nc.scalar.copy(out=dx[LAST][:, S - PAIR : S - C], in_=expert_sums(LAST, S - PAIR, S - C, dx_banks[-1]))
+                    nc.vector.tensor_copy(dx[LAST][:, S - C : S], expert_sums(LAST, S - C, S, dx_banks[0]))
                 for t0 in range(0, T, BANK):
                     finish(m, t0, t0 + BANK, shared_sums(m, t0, t0 + BANK))
 

@@ -1,6 +1,7 @@
 from contextlib import ExitStack
 
 import concourse.mybir as mybir
+from concourse.masks import make_identity
 
 K, T, E, C, N = 512, 1024, 8, 256, 512
 S = E * C
@@ -30,7 +31,9 @@ BYTES = 4 * N * T + (E + 1) * (N * K // 2 + N * K // 32) + 4 * S + 2 * (S + 2 * 
 PAIR = 2 * C
 PAIRS = S // PAIR
 LAST = BLOCKS - 1
-CHUNKS = [(0, 608), (608, 736), (1344, 320), (1664, 384)]
+CHUNKS = [(0, 608), (608, 736), (1344, 288), (1632, 416)]
+GATE_BANKS = [6, 7]
+GATE_BLOCKS = len(GATE_BANKS) * BANK // P
 FIRST_CUTS = [0, 128, CHUNKS[0][1]]
 RUN = 4
 FIRST_PIECE = 256
@@ -45,14 +48,19 @@ def tile_moe_bds_lin_none_kernel(
         keep = ctx.enter_context(tc.tile_pool(name="keep", bufs=1))
         ring = ctx.enter_context(tc.tile_pool(name="ring", bufs=BLOCKS))
         late = ctx.enter_context(tc.tile_pool(name="late", bufs=1))
+        held = ctx.enter_context(tc.tile_pool(name="held", bufs=1))
         psum = ctx.enter_context(tc.psum_pool(name="psum", bufs=1))
 
         offs_sb = keep.tile([P, S // PER_COL], U16, name="offs_sb")
         pos1_sb = keep.tile([P, T // PER_COL], U16, name="pos1_sb")
         pos2_sb = keep.tile([P, T // PER_COL], U16, name="pos2_sb")
         planes = [keep.tile([P, T], F32, name=f"plane{d}") for d in range(PACK)]
-        gate_first = keep.tile([P, CHUNKS[0][1]], F32, name="gate_first", tag="rows2", align_bytes=64)
-        gate_rest = keep.tile([P, S - CHUNKS[0][1]], F32, name="gate_rest")
+        border = 4 * PACK * CHUNKS[2][1]
+        gate_first = held.tile([P, CHUNKS[0][1]], F32, name="gate_first", offset=border - 64, align_bytes=64)
+        gate_last = keep.tile([P, CHUNKS[3][1]], F32, name="gate_last")
+        gate_rows = keep.tile([P, P], F32, name="gate_rows")
+        gate_cols = keep.tile([P, GATE_BLOCKS], F32, name="gate_cols")
+        ident = keep.tile([P, P], F32, name="ident")
         dy_rows = [
             keep.tile([P, PACK, BANK], F32, name="dy_rows0", align_bytes=64),
             late.tile([P, PACK, BANK], F32, name="dy_rows1", offset=0, align_bytes=64),
@@ -73,6 +81,7 @@ def tile_moe_bds_lin_none_kernel(
         nc.gpsimd.memset(warm[:, 0:1], 0.0)
         nc.scalar.activation(warm[:, 1:2], warm[:, 0:1], COPY)
         nc.vector.memset(w_sc[:].bitcast(I32), 0)
+        make_identity(nc, ident[:])
 
         dy_view = dyT.rearrange("(p d) x -> p d x", d=PACK)
         words = w_words.rearrange("e a p b -> p (e a) b")
@@ -90,16 +99,18 @@ def tile_moe_bds_lin_none_kernel(
         nc.sync.dma_start(planes[0][:], dy_view[:, 0, :])
         for a, b in zip(FIRST_CUTS, FIRST_CUTS[1:]):
             load_gate(gate_first, 0, a, b)
-        for d in range(1, PACK):
+        nc.sync.dma_start(planes[1][:], dy_view[:, 1, :])
+        flat = gate.rearrange("r s -> (r s)")[CHUNKS[1][0] : CHUNKS[1][0] + P * P]
+        nc.sync.dma_start(gate_rows[:], flat.rearrange("(j c) -> j c", c=P))
+        for d in range(2, PACK):
             nc.sync.dma_start(planes[d][:], dy_view[:, d, :])
-        load_gate(gate_rest, CHUNKS[1][0], CHUNKS[1][0], CHUNKS[3][0])
+        load_rows(0)
         for q in range(4):
             load_bytes(
                 w_sc[32 * q : 32 * q + 4, :, :], w_scales[:, 0, 4 * q : 4 * q + 4, :].rearrange("e f k -> f e k")
             )
         load_bytes(w_front[:], words[:, 0:E, 0 : 2 * BLOCK_BYTES])
-        load_gate(gate_rest, CHUNKS[1][0], CHUNKS[3][0], S)
-        load_rows(0)
+        load_gate(gate_last, CHUNKS[3][0], CHUNKS[3][0], S)
         nc.sync.dma_start(pos1_sb[:], pos1)
         nc.sync.dma_start(pos2_sb[:], pos2)
         load_rows(1)
@@ -116,7 +127,11 @@ def tile_moe_bds_lin_none_kernel(
             return lst[:, a // PER_COL : b // PER_COL]
 
         def rows_tile(c):
-            g_rows[c] = keep.tile([P, PACK, CHUNKS[c][1]], F32, name=f"g_rows{c}", tag=f"rows{c % 3}", align_bytes=64)
+            shape = [P, PACK, CHUNKS[c][1]]
+            if c < 2:
+                g_rows[c] = keep.tile(shape, F32, name=f"g_rows{c}", tag=f"rows{c}", align_bytes=64)
+            else:
+                g_rows[c] = held.tile(shape, F32, name=f"g_rows{c}", offset=(c - 2) * border, align_bytes=64)
             return g_rows[c]
 
         def gather_gated():
@@ -137,7 +152,12 @@ def tile_moe_bds_lin_none_kernel(
             nc.vector.tensor_copy(runs_out(dst), runs_in(src))
 
         def gate_and_interleave(c, s0, s1):
-            gates = gate_rest[:, s0 - CHUNKS[1][0] : s1 - CHUNKS[1][0]].rearrange("p (c i) -> p c i", i=RUN)
+            if c == len(CHUNKS) - 1:
+                gates = gate_last[:, s0 - CHUNKS[c][0] : s1 - CHUNKS[c][0]]
+            else:
+                bank, start = divmod(s0 - CHUNKS[1][0], BANK)
+                gates = banks[GATE_BANKS[bank]][:, start : start + s1 - s0]
+            gates = gates.rearrange("p (c i) -> p c i", i=RUN)
             nc.vector.tensor_tensor(
                 runs_out(g_grouped[:, PACK * s0 : PACK * s1]),
                 runs_in(g_rows[c][:, :, s0 - CHUNKS[c][0] : s1 - CHUNKS[c][0]]),
@@ -145,9 +165,11 @@ def tile_moe_bds_lin_none_kernel(
                 MULT,
             )
 
-        def quantize(codes, scales, grouped, a, b):
+        def quantize(codes, scales, grouped, first, a, b):
             nc.vector.quantize_mx(
-                out=codes[:, a:b].bitcast(FP8X4), scales=scales[:, a:b], in_=grouped[:, PACK * a : PACK * b]
+                out=codes[:, a:b].bitcast(FP8X4),
+                scales=scales[:, a:b],
+                in_=grouped[:, PACK * (a - first) : PACK * (b - first)],
             )
 
         def multiply(acc, e, m, codes, scales):
@@ -202,37 +224,54 @@ def tile_moe_bds_lin_none_kernel(
             nc.vector.tensor_tensor(total[:], partial(m, a, b), term, ADD)
             nc.sync.dma_start(out[P * m : P * (m + 1), a:b], total[:])
 
+        nc.tensor.transpose(banks[0][:, 0:P], gate_rows[:], ident[:])
+        nc.vector.tensor_copy(gate_cols[:], banks[0][:, 0 : GATE_BLOCKS])
+        for j in range(GATE_BLOCKS):
+            bank, start = divmod(j * P, BANK)
+            column = gate_cols[:, j : j + 1].to_broadcast([P, P])
+            nc.tensor.transpose(banks[GATE_BANKS[bank]][:, start : start + P], column, ident[:])
+
         gather_gated()
         gather_plain(1)
         gather_plain(2)
-        interleave(g_grouped[:, 0 : PACK * CHUNKS[0][1]], g_rows[0][:])
         gather_plain(3)
-        quantize(g_codes, g_scales, g_grouped, 0, PAIR)
-        gate_and_interleave(1, CHUNKS[1][0], CHUNKS[2][0])
+        interleave(g_grouped[:, 0 : PACK * CHUNKS[0][1]], g_rows[0][:])
+        y_early = keep.tile([P, BANK * PACK], BF16, name="y_early", tag="rows0", align_bytes=64)
+        nc.gpsimd.tensor_scalar(
+            y_early[:].rearrange("p (c t) -> p c t", t=PACK),
+            dy_rows[0][:].rearrange("p t c -> p c t"),
+            1.0,
+            0.0,
+            op0=MULT,
+            op1=ADD,
+        )
+        gate_and_interleave(1, CHUNKS[1][0], CHUNKS[1][0] + BANK)
+        gate_and_interleave(1, CHUNKS[1][0] + BANK, CHUNKS[2][0])
         gate_and_interleave(2, CHUNKS[2][0], CHUNKS[3][0])
-        quantize(g_codes, g_scales, g_grouped, PAIR, 2 * PAIR)
-        quantize(g_codes, g_scales, g_grouped, 2 * PAIR, 3 * PAIR)
+        for c in range(PAIRS - 1):
+            quantize(g_codes, g_scales, g_grouped, 0, c * PAIR, (c + 1) * PAIR)
         for c in range(PAIRS - 1):
             expert_products(0, c, bank=2 * c)
             expert_products(1, c, bank=2 * c + 1)
         gate_and_interleave(3, CHUNKS[3][0], S - C)
         gate_and_interleave(3, S - C, S)
-        quantize(g_codes, g_scales, g_grouped, S - PAIR, S - C)
-        quantize(g_codes, g_scales, g_grouped, S - C, S)
+        quantize(g_codes, g_scales, g_grouped, 0, S - PAIR, S - C)
+        quantize(g_codes, g_scales, g_grouped, 0, S - C, S)
         expert_products(0, PAIRS - 1, bank=0)
 
-        y_grouped = keep.tile([P, T * PACK], BF16, name="y_grouped", tag="rows0", align_bytes=64)
-        for h in range(T // BANK):
-            interleave(y_grouped[:, PACK * BANK * h : PACK * BANK * (h + 1)], dy_rows[h][:])
+        y_late = held.tile([P, BANK * PACK], BF16, name="y_late", offset=border, align_bytes=64)
+        interleave(y_late[:], dy_rows[1][:])
         y_codes = late.tile([P, T], U32, name="y_codes", offset=4 * T, align_bytes=64)
-        for t0 in range(0, T, BANK):
-            quantize(y_codes, y_scales, y_grouped, t0, t0 + BANK)
+        quantize(y_codes, y_scales, y_early, 0, 0, BANK)
+        quantize(y_codes, y_scales, y_late, BANK, BANK, T)
 
         dx[2] = keep.tile([P, S], F32, name="dx2", tag="grouped", align_bytes=64)
-        w_last = keep.tile([P, E, BLOCK_BYTES], U8, name="w_last", tag="rows0", align_bytes=64)
+        w_last = held.tile([P, E, BLOCK_BYTES], U8, name="w_last", offset=border, align_bytes=64)
         load_bytes(w_last[:], words[:, 0:E, LAST * BLOCK_BYTES :])
 
         dx_banks = [6, 7, 0, 1]
+        nc.vector.tensor_copy(dx[2][:, 0:PAIR], expert_sums(2, 0, PAIR, dx_banks[0]))
+
         ds_banks = [[2, 3], [4, 5]]
         cuts = [[0, BANK, T]] * LAST + [[0, FIRST_PIECE, BANK]]
         fetch(firsts[0][:, 0:BANK], pos1_sb, 0, 0, BANK)
@@ -246,14 +285,9 @@ def tile_moe_bds_lin_none_kernel(
             if m < LAST:
                 for a, b in zip(cuts[m + 1], cuts[m + 1][1:]):
                     fetch(firsts[m + 1][:, a:b], pos1_sb, m + 1, a, b)
-                if m + 2 < LAST:
-                    for c in range(PAIRS):
+                if m + 2 < BLOCKS:
+                    for c in range(1 if m == 0 else 0, PAIRS):
                         expert_products(m + 2, c, dx_banks[c])
-                if m + 2 == LAST:
-                    for c in range(PAIRS - 1):
-                        expert_products(LAST, c, dx_banks[c])
-                    nc.scalar.copy(out=dx[LAST][:, S - PAIR : S - C], in_=expert_sums(LAST, S - PAIR, S - C, dx_banks[-1]))
-                    nc.vector.tensor_copy(dx[LAST][:, S - C : S], expert_sums(LAST, S - C, S, dx_banks[0]))
                 for t0 in range(0, T, BANK):
                     finish(m, t0, t0 + BANK, shared_sums(m, t0, t0 + BANK))
 

@@ -257,7 +257,8 @@ def tile_moe_bds_lin_none_kernel(
         gate_and_interleave(3, S - C, S)
         quantize(g_codes, g_scales, g_grouped, 0, S - PAIR, S - C)
         quantize(g_codes, g_scales, g_grouped, 0, S - C, S)
-        expert_products(0, PAIRS - 1, bank=0)
+        for s0, bank in ((S - PAIR, 0), (S - C, 2)):
+            nc.scalar.copy(out=dx[0][:, s0 : s0 + C], in_=expert_sums(0, s0, s0 + C, bank))
 
         y_late = held.tile([P, BANK * PACK], BF16, name="y_late", offset=border, align_bytes=64)
         interleave(y_late[:], dy_rows[1][:])
@@ -273,9 +274,10 @@ def tile_moe_bds_lin_none_kernel(
         nc.vector.tensor_copy(dx[2][:, 0:PAIR], expert_sums(2, 0, PAIR, dx_banks[0]))
 
         ds_banks = [[2, 3], [4, 5]]
-        cuts = [[0, BANK, T]] * LAST + [[0, FIRST_PIECE, BANK]]
-        fetch(firsts[0][:, 0:BANK], pos1_sb, 0, 0, BANK)
+        cuts = [[0, FIRST_PIECE, BANK, T]] + [[0, BANK, T]] * (LAST - 1) + [[0, FIRST_PIECE, BANK]]
+        fetch(firsts[0][:, 0:FIRST_PIECE], pos1_sb, 0, 0, FIRST_PIECE)
         expert_products(1, PAIRS - 1, bank=1)
+        fetch(firsts[0][:, FIRST_PIECE:BANK], pos1_sb, 0, FIRST_PIECE, BANK)
         fetch(firsts[0][:, BANK:T], pos1_sb, 0, BANK, T)
         for m in range(BLOCKS):
             for h in range(T // BANK):

@@ -31,13 +31,25 @@ BYTES = 4 * N * T + (E + 1) * (N * K // 2 + N * K // 32) + 4 * S + 2 * (S + 2 * 
 PAIR = 2 * C
 PAIRS = S // PAIR
 LAST = BLOCKS - 1
-CHUNKS = [(0, 608), (608, 736), (1344, 288), (1632, 416)]
-GATE_BANKS = [6, 7]
+GATED = (0, 512)
+PLAIN = (512, 768)
+LONG = (768, 1536)
+SHORT = (1536, 2048)
+GATE_BANKS = [5, 6, 7]
 GATE_BLOCKS = len(GATE_BANKS) * BANK // P
-FIRST_CUTS = [0, 128, CHUNKS[0][1]]
+LONG_RUN = 704
+EARLY_TOKENS = 832
+TOKENS_AT = 384
+PLAIN_AT = TOKENS_AT - 128
+AT = {PLAIN[0]: PLAIN_AT, S - C: PLAIN_AT - 128 - 64, 1024: TOKENS_AT + T - 64}
+AT[0] = AT[1024] + 384
+AT[LONG[0]] = AT[1024] + 512
+AT[SHORT[0]] = AT[LONG[0]] + 256
+WOVEN = AT[SHORT[0]] + 256
 RUN = 4
 FIRST_PIECE = 256
 LAST_PIECE = 128
+HALF_BYTES = 2 * BLOCK_BYTES
 
 
 def tile_moe_bds_lin_none_kernel(
@@ -48,34 +60,37 @@ def tile_moe_bds_lin_none_kernel(
         keep = ctx.enter_context(tc.tile_pool(name="keep", bufs=1))
         ring = ctx.enter_context(tc.tile_pool(name="ring", bufs=BLOCKS))
         late = ctx.enter_context(tc.tile_pool(name="late", bufs=1))
-        held = ctx.enter_context(tc.tile_pool(name="held", bufs=1))
         psum = ctx.enter_context(tc.psum_pool(name="psum", bufs=1))
 
         offs_sb = keep.tile([P, S // PER_COL], U16, name="offs_sb")
         pos1_sb = keep.tile([P, T // PER_COL], U16, name="pos1_sb")
         pos2_sb = keep.tile([P, T // PER_COL], U16, name="pos2_sb")
         planes = [keep.tile([P, T], F32, name=f"plane{d}") for d in range(PACK)]
-        border = 4 * PACK * CHUNKS[2][1]
-        gate_first = held.tile([P, CHUNKS[0][1]], F32, name="gate_first", offset=border - 64, align_bytes=64)
-        gate_last = keep.tile([P, CHUNKS[3][1]], F32, name="gate_last")
+        plain_width = PLAIN[1] - PLAIN[0]
+        plain_flat = keep.tile([P, PACK * plain_width], F32, name="plain_flat", align_bytes=64)
+        gate_at = plain_width + plain_width // 2
+        gate_first = plain_flat[:, gate_at : gate_at + GATED[1]]
         gate_rows = keep.tile([P, P], F32, name="gate_rows")
-        gate_cols = keep.tile([P, GATE_BLOCKS], F32, name="gate_cols")
+        gate_cols = keep.tile([P, GATE_BLOCKS], F32, name="gate_cols", tag="short", align_bytes=64)
         ident = keep.tile([P, P], F32, name="ident")
-        dy_rows = [
-            keep.tile([P, PACK, BANK], F32, name="dy_rows0", align_bytes=64),
-            late.tile([P, PACK, BANK], F32, name="dy_rows1", offset=0, align_bytes=64),
-        ]
-        w_front = keep.tile([P, E, 2 * BLOCK_BYTES], U8, name="w_front", align_bytes=64)
-        w_third = keep.tile([P, E, BLOCK_BYTES], U8, name="w_third", align_bytes=64)
+        early_rows = keep.tile([P, PACK, EARLY_TOKENS], F32, name="early_rows", align_bytes=64)
+        late_rows = late.tile([P, PACK, T - EARLY_TOKENS], F32, name="late_rows", offset=0, align_bytes=64)
+        w_first = keep.tile([P, 2, 2 * K], U8, name="w_first", align_bytes=64)
+        w_front = keep.tile([P, E - 2, HALF_BYTES], U8, name="w_front", align_bytes=64)
         w_shared = keep.tile([P, 2 * K], U8, name="w_shared", align_bytes=64)
         w_sc = keep.tile([P, E + 1, K], U8, name="w_sc", align_bytes=64)
-        dx = {m: keep.tile([P, S], F32, name=f"dx{m}") for m in (0, 1, LAST)}
+        dx = [keep.tile([P, S], F32, name=f"dx{m}", tag=f"dx{m}", align_bytes=64) for m in range(BLOCKS)]
         banks = [psum.tile([P, BANK], F32, name=f"bank{b}") for b in range(8)]
-        g_codes = keep.tile([P, S], U32, name="g_codes", align_bytes=64)
         g_scales = keep.tile([P, S], U8, name="g_scales", align_bytes=64)
-        g_grouped = keep.tile([P, S * PACK], BF16, name="g_grouped", tag="grouped", align_bytes=64)
+        y_codes = keep.tile([P, T], U32, name="y_codes", align_bytes=64)
         y_scales = keep.tile([P, T], U8, name="y_scales", align_bytes=64)
-        g_rows = {}
+        woven = keep.tile([P, PACK * WOVEN], BF16, name="woven", tag="woven", align_bytes=64)
+
+        def slots_woven(s0, s1):
+            return woven[:, PACK * AT[s0] : PACK * (AT[s0] + s1 - s0)]
+
+        def tokens_woven(a, b):
+            return woven[:, PACK * (TOKENS_AT + a) : PACK * (TOKENS_AT + b)]
 
         warm = keep.tile([P, 2], F32, name="warm")
         nc.gpsimd.memset(warm[:, 0:1], 0.0)
@@ -86,36 +101,28 @@ def tile_moe_bds_lin_none_kernel(
         dy_view = dyT.rearrange("(p d) x -> p d x", d=PACK)
         words = w_words.rearrange("e a p b -> p (e a) b")
 
-        def load_gate(dst, first, s0, s1):
-            nc.sync.dma_start(dst[:, s0 - first : s1 - first], gate[0:P, s0:s1])
-
-        def load_rows(h):
-            nc.sync.dma_start(dy_rows[h][:], dy_view[:, :, h * BANK : (h + 1) * BANK])
-
         def load_bytes(dst, src):
             nc.sync.dma_start(dst.bitcast(I32), src.bitcast(I32))
 
         nc.sync.dma_start(offs_sb[:], offs)
         nc.sync.dma_start(planes[0][:], dy_view[:, 0, :])
-        for a, b in zip(FIRST_CUTS, FIRST_CUTS[1:]):
-            load_gate(gate_first, 0, a, b)
+        nc.sync.dma_start(gate_first, gate[0:P, GATED[0] : GATED[1]])
         nc.sync.dma_start(planes[1][:], dy_view[:, 1, :])
-        flat = gate.rearrange("r s -> (r s)")[CHUNKS[1][0] : CHUNKS[1][0] + P * P]
+        flat = gate.rearrange("r s -> (r s)")[PLAIN[0] : PLAIN[0] + P * P]
         nc.sync.dma_start(gate_rows[:], flat.rearrange("(j c) -> j c", c=P))
         for d in range(2, PACK):
             nc.sync.dma_start(planes[d][:], dy_view[:, d, :])
-        load_rows(0)
+        nc.sync.dma_start(early_rows[:], dy_view[:, :, 0:EARLY_TOKENS])
         for q in range(4):
             load_bytes(
                 w_sc[32 * q : 32 * q + 4, :, :], w_scales[:, 0, 4 * q : 4 * q + 4, :].rearrange("e f k -> f e k")
             )
-        load_bytes(w_front[:], words[:, 0:E, 0 : 2 * BLOCK_BYTES])
-        load_gate(gate_last, CHUNKS[3][0], CHUNKS[3][0], S)
+        load_bytes(w_first[:], words[:, 0:2, :])
+        load_bytes(w_front[:], words[:, 2:E, 0:HALF_BYTES])
         nc.sync.dma_start(pos1_sb[:], pos1)
         nc.sync.dma_start(pos2_sb[:], pos2)
-        load_rows(1)
+        nc.sync.dma_start(late_rows[:], dy_view[:, :, EARLY_TOKENS:T])
         load_bytes(w_shared[:], w_words[E, 0])
-        load_bytes(w_third[:], words[:, 0:E, 2 * BLOCK_BYTES : 3 * BLOCK_BYTES])
 
         def runs_out(dst):
             return dst.rearrange("p (c i t) -> p c t i", i=RUN, t=PACK)
@@ -126,59 +133,33 @@ def tile_moe_bds_lin_none_kernel(
         def offsets(lst, a, b):
             return lst[:, a // PER_COL : b // PER_COL]
 
-        def rows_tile(c):
-            shape = [P, PACK, CHUNKS[c][1]]
-            if c < 2:
-                g_rows[c] = keep.tile(shape, F32, name=f"g_rows{c}", tag=f"rows{c}", align_bytes=64)
-            else:
-                g_rows[c] = held.tile(shape, F32, name=f"g_rows{c}", offset=(c - 2) * border, align_bytes=64)
-            return g_rows[c]
+        def window(d, chunk):
+            return planes[d][:].indirect(offsets(offs_sb, chunk[0], chunk[1]))
 
-        def gather_gated():
-            rows = rows_tile(0)
-            for d in range(PACK):
-                cuts = FIRST_CUTS if d == 0 else [0, CHUNKS[0][1]]
-                for a, b in zip(cuts, cuts[1:]):
-                    window = planes[d][:].indirect(offsets(offs_sb, a, b))
-                    nc.vector.tensor_tensor(rows[:, d, a:b], window, gate_first[:, a:b], MULT)
+        def weave_on_gpsimd(dst, src):
+            nc.gpsimd.tensor_scalar(
+                dst.rearrange("p (c t) -> p c t", t=PACK), src.rearrange("p t c -> p c t"), 1.0, 0.0, op0=MULT, op1=ADD
+            )
 
-        def gather_plain(c):
-            s0, w = CHUNKS[c]
-            rows = rows_tile(c)
-            for d in range(PACK):
-                nc.scalar.activation(rows[:, d, :], planes[d][:].indirect(offsets(offs_sb, s0, s0 + w)), COPY)
-
-        def interleave(dst, src):
-            nc.vector.tensor_copy(runs_out(dst), runs_in(src))
-
-        def gate_and_interleave(c, s0, s1):
-            if c == len(CHUNKS) - 1:
-                gates = gate_last[:, s0 - CHUNKS[c][0] : s1 - CHUNKS[c][0]]
-            else:
-                bank, start = divmod(s0 - CHUNKS[1][0], BANK)
-                gates = banks[GATE_BANKS[bank]][:, start : start + s1 - s0]
-            gates = gates.rearrange("p (c i) -> p c i", i=RUN)
+        def gate_and_weave(dst, src, s0, s1):
+            bank, start = divmod(s0 - PLAIN[0], BANK)
+            gates = banks[GATE_BANKS[bank]][:, start : start + s1 - s0].rearrange("p (c i) -> p c i", i=RUN)
             nc.vector.tensor_tensor(
-                runs_out(g_grouped[:, PACK * s0 : PACK * s1]),
-                runs_in(g_rows[c][:, :, s0 - CHUNKS[c][0] : s1 - CHUNKS[c][0]]),
-                gates.unsqueeze(2).to_broadcast([P, (s1 - s0) // RUN, PACK, RUN]),
-                MULT,
+                runs_out(dst), runs_in(src), gates.unsqueeze(2).to_broadcast([P, (s1 - s0) // RUN, PACK, RUN]), MULT
             )
 
-        def quantize(codes, scales, grouped, first, a, b):
-            nc.vector.quantize_mx(
-                out=codes[:, a:b].bitcast(FP8X4),
-                scales=scales[:, a:b],
-                in_=grouped[:, PACK * (a - first) : PACK * (b - first)],
-            )
+        def quantize(codes, scales, grouped, a, b):
+            nc.vector.quantize_mx(out=codes[:, a:b].bitcast(FP8X4), scales=scales[:, a:b], in_=grouped(a, b))
 
         def multiply(acc, e, m, codes, scales):
             if e == E:
                 weights = w_shared[:, BLOCK_BYTES * m : BLOCK_BYTES * (m + 1)]
+            elif e < 2:
+                weights = w_first[:, e, BLOCK_BYTES * m : BLOCK_BYTES * (m + 1)]
             elif m < 2:
-                weights = w_front[:, e, BLOCK_BYTES * m : BLOCK_BYTES * (m + 1)]
+                weights = w_front[:, e - 2, BLOCK_BYTES * m : BLOCK_BYTES * (m + 1)]
             else:
-                weights = (w_third, w_last)[m - 2][:, e, :]
+                weights = w_back[m][:, e - 2, :]
             nc.tensor.matmul_mx(
                 out=acc,
                 lhsT=weights.bitcast(FP4X4),
@@ -194,14 +175,72 @@ def tile_moe_bds_lin_none_kernel(
                 multiply(banks[bank][:, j - s0 : j - s0 + C], j // C, m, g_codes[:, j : j + C], g_scales[:, j : j + C])
             return banks[bank][:, 0 : s1 - s0]
 
-        def expert_products(m, c, bank):
-            nc.scalar.copy(out=dx[m][:, c * PAIR : (c + 1) * PAIR], in_=expert_sums(m, c * PAIR, (c + 1) * PAIR, bank))
+        def expert_products(m, s0, s1, bank):
+            nc.scalar.copy(out=dx[m][:, s0:s1], in_=expert_sums(m, s0, s1, bank))
 
-        def shared_product(m, t0, bank):
-            multiply(banks[bank][:], E, m, y_codes[:, t0 : t0 + BANK], y_scales[:, t0 : t0 + BANK])
+        def pair_products(m, c, bank):
+            expert_products(m, c * PAIR, (c + 1) * PAIR, bank)
+
+        gated_rows = keep.tile([P, PACK, GATED[1]], F32, name="gated_rows", tag="codes", align_bytes=64)
+        plain_rows = plain_flat[:].rearrange("p (t c) -> p t c", t=PACK)
+        long_rows = keep.tile([P, PACK, LONG[1] - LONG[0]], F32, name="long_rows", align_bytes=64)
+        nc.vector.tensor_copy(plain_rows[:, 0, :], window(0, PLAIN))
+        for d in range(PACK):
+            nc.vector.tensor_tensor(gated_rows[:, d, :], window(d, GATED), gate_first, MULT)
+            nc.scalar.activation(long_rows[:, d, :], window(d, LONG), COPY)
+        nc.tensor.transpose(banks[0][:, 0:P], gate_rows[:], ident[:])
+        nc.vector.tensor_copy(gate_cols[:], banks[0][:, 0:GATE_BLOCKS])
+        for j in range(GATE_BLOCKS):
+            bank, start = divmod(j * P, BANK)
+            column = gate_cols[:, j : j + 1].to_broadcast([P, P])
+            nc.tensor.transpose(banks[GATE_BANKS[bank]][:, start : start + P], column, ident[:])
+        short_rows = keep.tile([P, PACK, SHORT[1] - SHORT[0]], F32, name="short_rows", tag="short", align_bytes=64)
+        for d in range(PACK):
+            nc.scalar.activation(short_rows[:, d, :], window(d, SHORT), COPY)
+        for d in range(1, PACK):
+            nc.vector.tensor_copy(plain_rows[:, d, :], window(d, PLAIN))
+        def gate_slots(rows, first, s0, s1):
+            gate_and_weave(slots_woven(s0, s1), rows[:, :, s0 - first : s1 - first], s0, s1)
+
+        weave_on_gpsimd(slots_woven(0, GATED[1]), gated_rows[:])
+        gate_slots(plain_rows, PLAIN[0], PLAIN[0], PLAIN[1])
+        g_codes = keep.tile([P, S], U32, name="g_codes", tag="codes", align_bytes=64)
+        quantize(g_codes, g_scales, slots_woven, 0, GATED[1])
+        quantize(g_codes, g_scales, slots_woven, PLAIN[0], PLAIN[1])
+        weave_on_gpsimd(tokens_woven(0, LONG_RUN), early_rows[:, :, 0:LONG_RUN])
+        nc.scalar.copy(
+            out=runs_out(tokens_woven(LONG_RUN, EARLY_TOKENS)), in_=runs_in(early_rows[:, :, LONG_RUN:EARLY_TOKENS])
+        )
+        for m in range(BLOCKS):
+            pair_products(m, 0, bank=m)
+        gate_slots(long_rows, LONG[0], LONG[0], 1024)
+        gate_slots(long_rows, LONG[0], 1024, LONG[1])
+        gate_slots(short_rows, SHORT[0], SHORT[0], S - C)
+        quantize(g_codes, g_scales, slots_woven, LONG[0], 1024)
+        quantize(g_codes, g_scales, slots_woven, 1024, LONG[1])
+        weave_on_gpsimd(tokens_woven(EARLY_TOKENS, T), late_rows[:])
+        pair_products(0, 1, bank=4)
+        pair_products(1, 1, bank=5)
+        pair_products(0, 2, bank=6)
+        pair_products(1, 2, bank=0)
+        gate_slots(short_rows, SHORT[0], S - C, S)
+        quantize(g_codes, g_scales, slots_woven, SHORT[0], S - C)
+        quantize(g_codes, g_scales, slots_woven, S - C, S)
+        expert_products(0, SHORT[0], S - C, bank=1)
+        expert_products(0, S - C, S, bank=2)
+        for t0 in range(0, T, BANK):
+            quantize(y_codes, y_scales, tokens_woven, t0, t0 + BANK)
+        nc.vector.tensor_copy(dx[1][:, SHORT[0] : S], expert_sums(1, SHORT[0], S, 3))
+        w_back = {2: keep.tile([P, E - 2, BLOCK_BYTES], U8, name="w_third", tag="woven", align_bytes=64)}
+        load_bytes(w_back[2][:], words[:, 2:E, HALF_BYTES : HALF_BYTES + BLOCK_BYTES])
 
         firsts = [ring.tile([P, T], F32, name="first") for m in range(BLOCKS)]
         partials = {}
+        ds_banks = [[0, 4], [5, 6], [3, 2], [7, 0]]
+        dx_banks = {2: [2, 1, 7], 3: [0, 4, 1]}
+
+        def shared_product(m, t0, bank):
+            multiply(banks[bank][:], E, m, y_codes[:, t0 : t0 + BANK], y_scales[:, t0 : t0 + BANK])
 
         def partial(m, a, b):
             t0 = a - a % BANK
@@ -213,83 +252,34 @@ def tile_moe_bds_lin_none_kernel(
             nc.scalar.activation(dst, dx[m][:].indirect(offsets(pos_sb, a, b)), COPY)
 
         def add_second(m, a, b):
-            window = dx[m][:].indirect(offsets(pos2_sb, a, b))
-            nc.vector.tensor_tensor(partial(m, a, b), window, firsts[m][:, a:b], ADD)
+            nc.vector.tensor_tensor(partial(m, a, b), dx[m][:].indirect(offsets(pos2_sb, a, b)), firsts[m][:, a:b], ADD)
 
         def shared_sums(m, a, b):
-            return banks[ds_banks[m % 2][a // BANK]][:, a % BANK : a % BANK + b - a]
+            return banks[ds_banks[m][a // BANK]][:, a % BANK : a % BANK + b - a]
 
         def finish(m, a, b, term):
             total = ring.tile([P, b - a], F32, name="total")
             nc.vector.tensor_tensor(total[:], partial(m, a, b), term, ADD)
             nc.sync.dma_start(out[P * m : P * (m + 1), a:b], total[:])
 
-        nc.tensor.transpose(banks[0][:, 0:P], gate_rows[:], ident[:])
-        nc.vector.tensor_copy(gate_cols[:], banks[0][:, 0 : GATE_BLOCKS])
-        for j in range(GATE_BLOCKS):
-            bank, start = divmod(j * P, BANK)
-            column = gate_cols[:, j : j + 1].to_broadcast([P, P])
-            nc.tensor.transpose(banks[GATE_BANKS[bank]][:, start : start + P], column, ident[:])
-
-        gather_gated()
-        gather_plain(1)
-        gather_plain(2)
-        gather_plain(3)
-        interleave(g_grouped[:, 0 : PACK * CHUNKS[0][1]], g_rows[0][:])
-        y_early = keep.tile([P, BANK * PACK], BF16, name="y_early", tag="rows0", align_bytes=64)
-        nc.gpsimd.tensor_scalar(
-            y_early[:].rearrange("p (c t) -> p c t", t=PACK),
-            dy_rows[0][:].rearrange("p t c -> p c t"),
-            1.0,
-            0.0,
-            op0=MULT,
-            op1=ADD,
-        )
-        gate_and_interleave(1, CHUNKS[1][0], CHUNKS[1][0] + BANK)
-        gate_and_interleave(1, CHUNKS[1][0] + BANK, CHUNKS[2][0])
-        gate_and_interleave(2, CHUNKS[2][0], CHUNKS[3][0])
-        for c in range(PAIRS - 1):
-            quantize(g_codes, g_scales, g_grouped, 0, c * PAIR, (c + 1) * PAIR)
-        for c in range(PAIRS - 1):
-            expert_products(0, c, bank=2 * c)
-            expert_products(1, c, bank=2 * c + 1)
-        gate_and_interleave(3, CHUNKS[3][0], S - C)
-        gate_and_interleave(3, S - C, S)
-        quantize(g_codes, g_scales, g_grouped, 0, S - PAIR, S - C)
-        quantize(g_codes, g_scales, g_grouped, 0, S - C, S)
-        for s0, bank in ((S - PAIR, 0), (S - C, 2)):
-            nc.scalar.copy(out=dx[0][:, s0 : s0 + C], in_=expert_sums(0, s0, s0 + C, bank))
-
-        y_late = held.tile([P, BANK * PACK], BF16, name="y_late", offset=border, align_bytes=64)
-        interleave(y_late[:], dy_rows[1][:])
-        y_codes = late.tile([P, T], U32, name="y_codes", offset=4 * T, align_bytes=64)
-        quantize(y_codes, y_scales, y_early, 0, 0, BANK)
-        quantize(y_codes, y_scales, y_late, BANK, BANK, T)
-
-        dx[2] = keep.tile([P, S], F32, name="dx2", tag="grouped", align_bytes=64)
-        w_last = held.tile([P, E, BLOCK_BYTES], U8, name="w_last", offset=border, align_bytes=64)
-        load_bytes(w_last[:], words[:, 0:E, LAST * BLOCK_BYTES :])
-
-        dx_banks = [6, 7, 0, 1]
-        nc.vector.tensor_copy(dx[2][:, 0:PAIR], expert_sums(2, 0, PAIR, dx_banks[0]))
-
-        ds_banks = [[2, 3], [4, 5]]
         cuts = [[0, FIRST_PIECE, BANK, T]] + [[0, BANK, T]] * (LAST - 1) + [[0, FIRST_PIECE, BANK]]
         fetch(firsts[0][:, 0:FIRST_PIECE], pos1_sb, 0, 0, FIRST_PIECE)
-        expert_products(1, PAIRS - 1, bank=1)
         fetch(firsts[0][:, FIRST_PIECE:BANK], pos1_sb, 0, FIRST_PIECE, BANK)
         fetch(firsts[0][:, BANK:T], pos1_sb, 0, BANK, T)
         for m in range(BLOCKS):
             for h in range(T // BANK):
-                shared_product(m, h * BANK, ds_banks[m % 2][h])
+                shared_product(m, h * BANK, ds_banks[m][h])
             for a, b in zip(cuts[m], cuts[m][1:]):
                 add_second(m, a, b)
+            if m == 0:
+                w_back[LAST] = keep.tile([P, E - 2, BLOCK_BYTES], U8, name="w_last", tag="dx0", align_bytes=64)
+                load_bytes(w_back[LAST][:], words[:, 2:E, LAST * BLOCK_BYTES :])
             if m < LAST:
                 for a, b in zip(cuts[m + 1], cuts[m + 1][1:]):
                     fetch(firsts[m + 1][:, a:b], pos1_sb, m + 1, a, b)
                 if m + 2 < BLOCKS:
-                    for c in range(1 if m == 0 else 0, PAIRS):
-                        expert_products(m + 2, c, dx_banks[c])
+                    for c in range(1, PAIRS):
+                        pair_products(m + 2, c, dx_banks[m + 2][c - 1])
                 for t0 in range(0, T, BANK):
                     finish(m, t0, t0 + BANK, shared_sums(m, t0, t0 + BANK))
 

@@ -31,21 +31,26 @@ BYTES = 4 * N * T + (E + 1) * (N * K // 2 + N * K // 32) + 4 * S + 2 * (S + 2 * 
 PAIR = 2 * C
 PAIRS = S // PAIR
 LAST = BLOCKS - 1
-GATED = (0, 512)
-PLAIN = (512, 768)
-LONG = (768, 1536)
+GATED = (0, 416)
+PLAIN = (416, 640)
+LONG = (640, 1536)
 SHORT = (1536, 2048)
-GATE_BANKS = [5, 6, 7]
-GATE_BLOCKS = len(GATE_BANKS) * BANK // P
-LONG_RUN = 704
-EARLY_TOKENS = 832
-TOKENS_AT = 384
-PLAIN_AT = TOKENS_AT - 128
-AT = {PLAIN[0]: PLAIN_AT, S - C: PLAIN_AT - 128 - 64, 1024: TOKENS_AT + T - 64}
-AT[0] = AT[1024] + 384
-AT[LONG[0]] = AT[1024] + 512
-AT[SHORT[0]] = AT[LONG[0]] + 256
-WOVEN = AT[SHORT[0]] + 256
+GATES_FROM = PLAIN[0] - PLAIN[0] % P
+GATE_BANKS = {GATES_FROM: 4, LONG[0]: 5, 1024: 6, SHORT[0]: 7}
+GATE_BLOCKS = (S - GATES_FROM) // P
+FIRST_CUT = 384
+EARLY_TOKENS = 640
+LAP = 64
+TOKENS_AT = {EARLY_TOKENS: 0}
+AT = {LONG[0]: T - EARLY_TOKENS - LAP}
+AT[SHORT[0]] = AT[LONG[0]] + LAP
+AT[0] = AT[LONG[0]] + 1024 - LONG[0] - LAP
+AT[FIRST_CUT] = AT[0] + FIRST_CUT
+AT[PLAIN[0]] = AT[0] + PLAIN[0]
+AT[1024] = AT[0] + LAP
+AT[S - C] = AT[1024]
+TOKENS_AT[0] = AT[1024] + BANK
+WOVEN = TOKENS_AT[0] + EARLY_TOKENS
 RUN = 4
 FIRST_PIECE = 256
 LAST_PIECE = 128
@@ -68,7 +73,7 @@ def tile_moe_bds_lin_none_kernel(
         planes = [keep.tile([P, T], F32, name=f"plane{d}") for d in range(PACK)]
         plain_width = PLAIN[1] - PLAIN[0]
         plain_flat = keep.tile([P, PACK * plain_width], F32, name="plain_flat", align_bytes=64)
-        gate_at = plain_width + plain_width // 2
+        gate_at = 2 * plain_width - P
         gate_first = plain_flat[:, gate_at : gate_at + GATED[1]]
         gate_rows = keep.tile([P, P], F32, name="gate_rows")
         gate_cols = keep.tile([P, GATE_BLOCKS], F32, name="gate_cols", tag="short", align_bytes=64)
@@ -90,7 +95,8 @@ def tile_moe_bds_lin_none_kernel(
             return woven[:, PACK * AT[s0] : PACK * (AT[s0] + s1 - s0)]
 
         def tokens_woven(a, b):
-            return woven[:, PACK * (TOKENS_AT + a) : PACK * (TOKENS_AT + b)]
+            first = 0 if a < EARLY_TOKENS else EARLY_TOKENS
+            return woven[:, PACK * (TOKENS_AT[first] + a - first) : PACK * (TOKENS_AT[first] + b - first)]
 
         warm = keep.tile([P, 2], F32, name="warm")
         nc.gpsimd.memset(warm[:, 0:1], 0.0)
@@ -108,7 +114,7 @@ def tile_moe_bds_lin_none_kernel(
         nc.sync.dma_start(planes[0][:], dy_view[:, 0, :])
         nc.sync.dma_start(gate_first, gate[0:P, GATED[0] : GATED[1]])
         nc.sync.dma_start(planes[1][:], dy_view[:, 1, :])
-        flat = gate.rearrange("r s -> (r s)")[PLAIN[0] : PLAIN[0] + P * P]
+        flat = gate.rearrange("r s -> (r s)")[GATES_FROM : GATES_FROM + P * P]
         nc.sync.dma_start(gate_rows[:], flat.rearrange("(j c) -> j c", c=P))
         for d in range(2, PACK):
             nc.sync.dma_start(planes[d][:], dy_view[:, d, :])
@@ -119,9 +125,9 @@ def tile_moe_bds_lin_none_kernel(
             )
         load_bytes(w_first[:], words[:, 0:2, :])
         load_bytes(w_front[:], words[:, 2:E, 0:HALF_BYTES])
+        nc.sync.dma_start(late_rows[:], dy_view[:, :, EARLY_TOKENS:T])
         nc.sync.dma_start(pos1_sb[:], pos1)
         nc.sync.dma_start(pos2_sb[:], pos2)
-        nc.sync.dma_start(late_rows[:], dy_view[:, :, EARLY_TOKENS:T])
         load_bytes(w_shared[:], w_words[E, 0])
 
         def runs_out(dst):
@@ -141,9 +147,12 @@ def tile_moe_bds_lin_none_kernel(
                 dst.rearrange("p (c t) -> p c t", t=PACK), src.rearrange("p t c -> p c t"), 1.0, 0.0, op0=MULT, op1=ADD
             )
 
+        def gates_in_psum(s0, s1):
+            first = max(s for s in GATE_BANKS if s <= s0)
+            return banks[GATE_BANKS[first]][:, s0 - first : s1 - first]
+
         def gate_and_weave(dst, src, s0, s1):
-            bank, start = divmod(s0 - PLAIN[0], BANK)
-            gates = banks[GATE_BANKS[bank]][:, start : start + s1 - s0].rearrange("p (c i) -> p c i", i=RUN)
+            gates = gates_in_psum(s0, s1).rearrange("p (c i) -> p c i", i=RUN)
             nc.vector.tensor_tensor(
                 runs_out(dst), runs_in(src), gates.unsqueeze(2).to_broadcast([P, (s1 - s0) // RUN, PACK, RUN]), MULT
             )
@@ -171,7 +180,7 @@ def tile_moe_bds_lin_none_kernel(
             )
 
         def expert_sums(m, s0, s1, bank):
-            for j in range(s0, s1, C):
+            for j in sorted(range(s0, s1, C), reverse=s1 == S):
                 multiply(banks[bank][:, j - s0 : j - s0 + C], j // C, m, g_codes[:, j : j + C], g_scales[:, j : j + C])
             return banks[bank][:, 0 : s1 - s0]
 
@@ -191,9 +200,8 @@ def tile_moe_bds_lin_none_kernel(
         nc.tensor.transpose(banks[0][:, 0:P], gate_rows[:], ident[:])
         nc.vector.tensor_copy(gate_cols[:], banks[0][:, 0:GATE_BLOCKS])
         for j in range(GATE_BLOCKS):
-            bank, start = divmod(j * P, BANK)
             column = gate_cols[:, j : j + 1].to_broadcast([P, P])
-            nc.tensor.transpose(banks[GATE_BANKS[bank]][:, start : start + P], column, ident[:])
+            nc.tensor.transpose(gates_in_psum(GATES_FROM + j * P, GATES_FROM + (j + 1) * P), column, ident[:])
         short_rows = keep.tile([P, PACK, SHORT[1] - SHORT[0]], F32, name="short_rows", tag="short", align_bytes=64)
         for d in range(PACK):
             nc.scalar.activation(short_rows[:, d, :], window(d, SHORT), COPY)
@@ -205,17 +213,13 @@ def tile_moe_bds_lin_none_kernel(
         weave_on_gpsimd(slots_woven(0, GATED[1]), gated_rows[:])
         gate_slots(plain_rows, PLAIN[0], PLAIN[0], PLAIN[1])
         g_codes = keep.tile([P, S], U32, name="g_codes", tag="codes", align_bytes=64)
-        quantize(g_codes, g_scales, slots_woven, 0, GATED[1])
-        quantize(g_codes, g_scales, slots_woven, PLAIN[0], PLAIN[1])
-        weave_on_gpsimd(tokens_woven(0, LONG_RUN), early_rows[:, :, 0:LONG_RUN])
-        nc.scalar.copy(
-            out=runs_out(tokens_woven(LONG_RUN, EARLY_TOKENS)), in_=runs_in(early_rows[:, :, LONG_RUN:EARLY_TOKENS])
-        )
+        quantize(g_codes, g_scales, slots_woven, 0, FIRST_CUT)
+        quantize(g_codes, g_scales, slots_woven, FIRST_CUT, PLAIN[1])
+        weave_on_gpsimd(tokens_woven(0, EARLY_TOKENS), early_rows[:])
         for m in range(BLOCKS):
             pair_products(m, 0, bank=m)
         gate_slots(long_rows, LONG[0], LONG[0], 1024)
         gate_slots(long_rows, LONG[0], 1024, LONG[1])
-        gate_slots(short_rows, SHORT[0], SHORT[0], S - C)
         quantize(g_codes, g_scales, slots_woven, LONG[0], 1024)
         quantize(g_codes, g_scales, slots_woven, 1024, LONG[1])
         weave_on_gpsimd(tokens_woven(EARLY_TOKENS, T), late_rows[:])
@@ -223,13 +227,14 @@ def tile_moe_bds_lin_none_kernel(
         pair_products(1, 1, bank=5)
         pair_products(0, 2, bank=6)
         pair_products(1, 2, bank=0)
+        gate_slots(short_rows, SHORT[0], SHORT[0], S - C)
         gate_slots(short_rows, SHORT[0], S - C, S)
         quantize(g_codes, g_scales, slots_woven, SHORT[0], S - C)
         quantize(g_codes, g_scales, slots_woven, S - C, S)
         expert_products(0, SHORT[0], S - C, bank=1)
-        expert_products(0, S - C, S, bank=2)
-        for t0 in range(0, T, BANK):
-            quantize(y_codes, y_scales, tokens_woven, t0, t0 + BANK)
+        nc.vector.tensor_copy(dx[0][:, S - C : S], expert_sums(0, S - C, S, 2))
+        for a, b in ((0, BANK), (BANK, EARLY_TOKENS), (EARLY_TOKENS, T)):
+            quantize(y_codes, y_scales, tokens_woven, a, b)
         nc.vector.tensor_copy(dx[1][:, SHORT[0] : S], expert_sums(1, SHORT[0], S, 3))
         w_back = {2: keep.tile([P, E - 2, BLOCK_BYTES], U8, name="w_third", tag="woven", align_bytes=64)}
         load_bytes(w_back[2][:], words[:, 2:E, HALF_BYTES : HALF_BYTES + BLOCK_BYTES])
@@ -258,13 +263,12 @@ def tile_moe_bds_lin_none_kernel(
             return banks[ds_banks[m][a // BANK]][:, a % BANK : a % BANK + b - a]
 
         def finish(m, a, b, term):
-            total = ring.tile([P, b - a], F32, name="total")
+            total = ring.tile([P, b - a], F32, name="total", bufs=6)
             nc.vector.tensor_tensor(total[:], partial(m, a, b), term, ADD)
             nc.sync.dma_start(out[P * m : P * (m + 1), a:b], total[:])
 
-        cuts = [[0, FIRST_PIECE, BANK, T]] + [[0, BANK, T]] * (LAST - 1) + [[0, FIRST_PIECE, BANK]]
-        fetch(firsts[0][:, 0:FIRST_PIECE], pos1_sb, 0, 0, FIRST_PIECE)
-        fetch(firsts[0][:, FIRST_PIECE:BANK], pos1_sb, 0, FIRST_PIECE, BANK)
+        cuts = [[0, BANK, T]] * LAST + [[0, FIRST_PIECE, BANK]]
+        fetch(firsts[0][:, 0:BANK], pos1_sb, 0, 0, BANK)
         fetch(firsts[0][:, BANK:T], pos1_sb, 0, BANK, T)
         for m in range(BLOCKS):
             for h in range(T // BANK):

@@ -31,26 +31,14 @@ BYTES = 4 * N * T + (E + 1) * (N * K // 2 + N * K // 32) + 4 * S + 2 * (S + 2 * 
 PAIR = 2 * C
 PAIRS = S // PAIR
 LAST = BLOCKS - 1
-GATED = (0, 416)
-PLAIN = (416, 640)
+PLAIN = (0, 256)
+GATED = (256, 640)
 LONG = (640, 1536)
 SHORT = (1536, 2048)
-GATES_FROM = PLAIN[0] - PLAIN[0] % P
-GATE_BANKS = {GATES_FROM: 4, LONG[0]: 5, 1024: 6, SHORT[0]: 7}
-GATE_BLOCKS = (S - GATES_FROM) // P
-FIRST_CUT = 384
+GATE_BANKS = {0: 4, LONG[0]: 5, 1024: 6, SHORT[0]: 7}
+GATE_BLOCKS = S // P
 EARLY_TOKENS = 640
 LAP = 64
-TOKENS_AT = {EARLY_TOKENS: 0}
-AT = {LONG[0]: T - EARLY_TOKENS - LAP}
-AT[SHORT[0]] = AT[LONG[0]] + LAP
-AT[0] = AT[LONG[0]] + 1024 - LONG[0] - LAP
-AT[FIRST_CUT] = AT[0] + FIRST_CUT
-AT[PLAIN[0]] = AT[0] + PLAIN[0]
-AT[1024] = AT[0] + LAP
-AT[S - C] = AT[1024]
-TOKENS_AT[0] = AT[1024] + BANK
-WOVEN = TOKENS_AT[0] + EARLY_TOKENS
 RUN = 4
 FIRST_PIECE = 256
 LAST_PIECE = 128
@@ -64,6 +52,7 @@ def tile_moe_bds_lin_none_kernel(
     with ExitStack() as ctx:
         keep = ctx.enter_context(tc.tile_pool(name="keep", bufs=1))
         ring = ctx.enter_context(tc.tile_pool(name="ring", bufs=BLOCKS))
+        held = ctx.enter_context(tc.tile_pool(name="held", bufs=1))
         late = ctx.enter_context(tc.tile_pool(name="late", bufs=1))
         psum = ctx.enter_context(tc.psum_pool(name="psum", bufs=1))
 
@@ -73,8 +62,8 @@ def tile_moe_bds_lin_none_kernel(
         planes = [keep.tile([P, T], F32, name=f"plane{d}") for d in range(PACK)]
         plain_width = PLAIN[1] - PLAIN[0]
         plain_flat = keep.tile([P, PACK * plain_width], F32, name="plain_flat", align_bytes=64)
-        gate_at = 2 * plain_width - P
-        gate_first = plain_flat[:, gate_at : gate_at + GATED[1]]
+        gate_at = 2 * plain_width + 64
+        gate_first = plain_flat[:, gate_at : gate_at + GATED[1] - GATED[0]]
         gate_rows = keep.tile([P, P], F32, name="gate_rows")
         gate_cols = keep.tile([P, GATE_BLOCKS], F32, name="gate_cols", tag="short", align_bytes=64)
         ident = keep.tile([P, P], F32, name="ident")
@@ -89,14 +78,18 @@ def tile_moe_bds_lin_none_kernel(
         g_scales = keep.tile([P, S], U8, name="g_scales", align_bytes=64)
         y_codes = keep.tile([P, T], U32, name="y_codes", align_bytes=64)
         y_scales = keep.tile([P, T], U8, name="y_scales", align_bytes=64)
-        woven = keep.tile([P, PACK * WOVEN], BF16, name="woven", tag="woven", align_bytes=64)
+        woven = keep.tile([P, PACK * T], BF16, name="woven", tag="woven", align_bytes=64)
 
         def slots_woven(s0, s1):
-            return woven[:, PACK * AT[s0] : PACK * (AT[s0] + s1 - s0)]
+            if s0 < LONG[0]:
+                return woven[:, PACK * (LAP + s0) : PACK * (LAP + s1)]
+            if s0 < T:
+                return woven[:, PACK * s0 : PACK * s1]
+            at = BANK if s0 == SHORT[0] else 0
+            return back[:, PACK * at : PACK * (at + s1 - s0)]
 
         def tokens_woven(a, b):
-            first = 0 if a < EARLY_TOKENS else EARLY_TOKENS
-            return woven[:, PACK * (TOKENS_AT[first] + a - first) : PACK * (TOKENS_AT[first] + b - first)]
+            return woven[:, PACK * a : PACK * b]
 
         warm = keep.tile([P, 2], F32, name="warm")
         nc.gpsimd.memset(warm[:, 0:1], 0.0)
@@ -114,7 +107,7 @@ def tile_moe_bds_lin_none_kernel(
         nc.sync.dma_start(planes[0][:], dy_view[:, 0, :])
         nc.sync.dma_start(gate_first, gate[0:P, GATED[0] : GATED[1]])
         nc.sync.dma_start(planes[1][:], dy_view[:, 1, :])
-        flat = gate.rearrange("r s -> (r s)")[GATES_FROM : GATES_FROM + P * P]
+        flat = gate.rearrange("r s -> (r s)")[0 : P * P]
         nc.sync.dma_start(gate_rows[:], flat.rearrange("(j c) -> j c", c=P))
         for d in range(2, PACK):
             nc.sync.dma_start(planes[d][:], dy_view[:, d, :])
@@ -190,31 +183,35 @@ def tile_moe_bds_lin_none_kernel(
         def pair_products(m, c, bank):
             expert_products(m, c * PAIR, (c + 1) * PAIR, bank)
 
-        gated_rows = keep.tile([P, PACK, GATED[1]], F32, name="gated_rows", tag="codes", align_bytes=64)
+        back_bytes = 2 * PACK * (BANK + C)
+        gated_rows = held.tile([P, PACK, GATED[1] - GATED[0]], F32, name="gated_rows", offset=back_bytes // 2, align_bytes=64)
         plain_rows = plain_flat[:].rearrange("p (t c) -> p t c", t=PACK)
         long_rows = keep.tile([P, PACK, LONG[1] - LONG[0]], F32, name="long_rows", align_bytes=64)
         nc.vector.tensor_copy(plain_rows[:, 0, :], window(0, PLAIN))
         for d in range(PACK):
             nc.vector.tensor_tensor(gated_rows[:, d, :], window(d, GATED), gate_first, MULT)
             nc.scalar.activation(long_rows[:, d, :], window(d, LONG), COPY)
+            if d == 1:
+                nc.vector.tensor_copy(plain_rows[:, d, :], window(d, PLAIN))
         nc.tensor.transpose(banks[0][:, 0:P], gate_rows[:], ident[:])
         nc.vector.tensor_copy(gate_cols[:], banks[0][:, 0:GATE_BLOCKS])
-        for j in range(GATE_BLOCKS):
-            column = gate_cols[:, j : j + 1].to_broadcast([P, P])
-            nc.tensor.transpose(gates_in_psum(GATES_FROM + j * P, GATES_FROM + (j + 1) * P), column, ident[:])
+        for s0 in [*range(0, PLAIN[1], P), *range(LONG[0], S, P)]:
+            column = gate_cols[:, s0 // P : s0 // P + 1].to_broadcast([P, P])
+            nc.tensor.transpose(gates_in_psum(s0, s0 + P), column, ident[:])
         short_rows = keep.tile([P, PACK, SHORT[1] - SHORT[0]], F32, name="short_rows", tag="short", align_bytes=64)
         for d in range(PACK):
             nc.scalar.activation(short_rows[:, d, :], window(d, SHORT), COPY)
-        for d in range(1, PACK):
+        for d in range(2, PACK):
             nc.vector.tensor_copy(plain_rows[:, d, :], window(d, PLAIN))
         def gate_slots(rows, first, s0, s1):
             gate_and_weave(slots_woven(s0, s1), rows[:, :, s0 - first : s1 - first], s0, s1)
 
-        weave_on_gpsimd(slots_woven(0, GATED[1]), gated_rows[:])
+        weave_on_gpsimd(slots_woven(GATED[0], GATED[1]), gated_rows[:])
         gate_slots(plain_rows, PLAIN[0], PLAIN[0], PLAIN[1])
-        g_codes = keep.tile([P, S], U32, name="g_codes", tag="codes", align_bytes=64)
-        quantize(g_codes, g_scales, slots_woven, 0, FIRST_CUT)
-        quantize(g_codes, g_scales, slots_woven, FIRST_CUT, PLAIN[1])
+        g_codes = held.tile([P, S], U32, name="g_codes", offset=back_bytes, align_bytes=64)
+        quantize(g_codes, g_scales, slots_woven, C, LONG[0])
+        quantize(g_codes, g_scales, slots_woven, 0, C)
+        back = held.tile([P, PACK * (BANK + C)], BF16, name="back", offset=0, align_bytes=64)
         weave_on_gpsimd(tokens_woven(0, EARLY_TOKENS), early_rows[:])
         for m in range(BLOCKS):
             pair_products(m, 0, bank=m)
@@ -233,7 +230,7 @@ def tile_moe_bds_lin_none_kernel(
         quantize(g_codes, g_scales, slots_woven, S - C, S)
         expert_products(0, SHORT[0], S - C, bank=1)
         nc.vector.tensor_copy(dx[0][:, S - C : S], expert_sums(0, S - C, S, 2))
-        for a, b in ((0, BANK), (BANK, EARLY_TOKENS), (EARLY_TOKENS, T)):
+        for a, b in ((0, BANK), (BANK, T)):
             quantize(y_codes, y_scales, tokens_woven, a, b)
         nc.vector.tensor_copy(dx[1][:, SHORT[0] : S], expert_sums(1, SHORT[0], S, 3))
         w_back = {2: keep.tile([P, E - 2, BLOCK_BYTES], U8, name="w_third", tag="woven", align_bytes=64)}

@@ -71,6 +71,7 @@ def tile_moe_bds_lin_none_kernel(
         late_rows = late.tile([P, PACK, T - EARLY_TOKENS], F32, name="late_rows", offset=0, align_bytes=64)
         w_first = keep.tile([P, 2, 2 * K], U8, name="w_first", align_bytes=64)
         w_front = keep.tile([P, E - 2, HALF_BYTES], U8, name="w_front", align_bytes=64)
+        w_extra = keep.tile([P, 2, BLOCK_BYTES], U8, name="w_extra", align_bytes=64)
         w_shared = keep.tile([P, 2 * K], U8, name="w_shared", align_bytes=64)
         w_sc = keep.tile([P, E + 1, K], U8, name="w_sc", align_bytes=64)
         dx = [keep.tile([P, S], F32, name=f"dx{m}", tag=f"dx{m}", align_bytes=64) for m in range(BLOCKS)]
@@ -118,6 +119,7 @@ def tile_moe_bds_lin_none_kernel(
             )
         load_bytes(w_first[:], words[:, 0:2, :])
         load_bytes(w_front[:], words[:, 2:E, 0:HALF_BYTES])
+        load_bytes(w_extra[:], words[:, E - 2 : E, HALF_BYTES : HALF_BYTES + BLOCK_BYTES])
         nc.sync.dma_start(late_rows[:], dy_view[:, :, EARLY_TOKENS:T])
         nc.sync.dma_start(pos1_sb[:], pos1)
         nc.sync.dma_start(pos2_sb[:], pos2)
@@ -156,6 +158,8 @@ def tile_moe_bds_lin_none_kernel(
         def multiply(acc, e, m, codes, scales):
             if e == E:
                 weights = w_shared[:, BLOCK_BYTES * m : BLOCK_BYTES * (m + 1)]
+            elif e >= E - 2 and m == 2:
+                weights = w_extra[:, e - E + 2, :]
             elif e < 2:
                 weights = w_first[:, e, BLOCK_BYTES * m : BLOCK_BYTES * (m + 1)]
             elif m < 2:
@@ -233,8 +237,9 @@ def tile_moe_bds_lin_none_kernel(
         for a, b in ((0, BANK), (BANK, T)):
             quantize(y_codes, y_scales, tokens_woven, a, b)
         nc.vector.tensor_copy(dx[1][:, SHORT[0] : S], expert_sums(1, SHORT[0], S, 3))
-        w_back = {2: keep.tile([P, E - 2, BLOCK_BYTES], U8, name="w_third", tag="woven", align_bytes=64)}
-        load_bytes(w_back[2][:], words[:, 2:E, HALF_BYTES : HALF_BYTES + BLOCK_BYTES])
+        nc.vector.tensor_copy(dx[2][:, SHORT[0] : S], expert_sums(2, SHORT[0], S, 7))
+        w_back = {2: held.tile([P, E - 4, BLOCK_BYTES], U8, name="w_third", offset=0, align_bytes=64)}
+        load_bytes(w_back[2][:], words[:, 2 : E - 2, HALF_BYTES : HALF_BYTES + BLOCK_BYTES])
 
         firsts = [ring.tile([P, T], F32, name="first") for m in range(BLOCKS)]
         partials = {}
@@ -279,7 +284,7 @@ def tile_moe_bds_lin_none_kernel(
                 for a, b in zip(cuts[m + 1], cuts[m + 1][1:]):
                     fetch(firsts[m + 1][:, a:b], pos1_sb, m + 1, a, b)
                 if m + 2 < BLOCKS:
-                    for c in range(1, PAIRS):
+                    for c in range(1, PAIRS - 1 + m):
                         pair_products(m + 2, c, dx_banks[m + 2][c - 1])
                 for t0 in range(0, T, BANK):
                     finish(m, t0, t0 + BANK, shared_sums(m, t0, t0 + BANK))

@@ -53,6 +53,7 @@ def tile_moe_bds_lin_none_kernel(
         keep = ctx.enter_context(tc.tile_pool(name="keep", bufs=1))
         ring = ctx.enter_context(tc.tile_pool(name="ring", bufs=BLOCKS))
         held = ctx.enter_context(tc.tile_pool(name="held", bufs=1))
+        chain = ctx.enter_context(tc.tile_pool(name="chain", bufs=1))
         late = ctx.enter_context(tc.tile_pool(name="late", bufs=1))
         psum = ctx.enter_context(tc.psum_pool(name="psum", bufs=1))
 
@@ -68,16 +69,17 @@ def tile_moe_bds_lin_none_kernel(
         gate_cols = keep.tile([P, GATE_BLOCKS], F32, name="gate_cols", tag="short", align_bytes=64)
         ident = keep.tile([P, P], F32, name="ident")
         early_rows = keep.tile([P, PACK, EARLY_TOKENS], F32, name="early_rows", align_bytes=64)
-        late_rows = late.tile([P, PACK, T - EARLY_TOKENS], F32, name="late_rows", offset=0, align_bytes=64)
+        late_rows = keep.tile([P, PACK, T - EARLY_TOKENS], F32, name="late_rows", align_bytes=64)
         w_first = keep.tile([P, 2, 2 * K], U8, name="w_first", align_bytes=64)
-        w_front = keep.tile([P, E - 2, HALF_BYTES], U8, name="w_front", align_bytes=64)
-        w_extra = keep.tile([P, 2, BLOCK_BYTES], U8, name="w_extra", align_bytes=64)
+        w_front = keep.tile([P, E - 4, HALF_BYTES], U8, name="w_front", align_bytes=64)
+        w_key = chain.tile([P, 2, BLOCK_BYTES], U8, name="w_key", offset=4 * BANK - BLOCK_BYTES, align_bytes=64)
+        w_extra = late.tile([P, 2, HALF_BYTES], U8, name="w_extra", offset=4 * BANK - HALF_BYTES, align_bytes=64)
         w_shared = keep.tile([P, 2 * K], U8, name="w_shared", align_bytes=64)
         w_sc = keep.tile([P, E + 1, K], U8, name="w_sc", align_bytes=64)
         dx = [keep.tile([P, S], F32, name=f"dx{m}", tag=f"dx{m}", align_bytes=64) for m in range(BLOCKS)]
         banks = [psum.tile([P, BANK], F32, name=f"bank{b}") for b in range(8)]
         g_scales = keep.tile([P, S], U8, name="g_scales", align_bytes=64)
-        y_codes = keep.tile([P, T], U32, name="y_codes", align_bytes=64)
+        y_codes = [keep.tile([P, BANK], U32, name="y_codes0", align_bytes=64)]
         y_scales = keep.tile([P, T], U8, name="y_scales", align_bytes=64)
         woven = keep.tile([P, PACK * T], BF16, name="woven", tag="woven", align_bytes=64)
 
@@ -118,9 +120,10 @@ def tile_moe_bds_lin_none_kernel(
                 w_sc[32 * q : 32 * q + 4, :, :], w_scales[:, 0, 4 * q : 4 * q + 4, :].rearrange("e f k -> f e k")
             )
         load_bytes(w_first[:], words[:, 0:2, :])
-        load_bytes(w_front[:], words[:, 2:E, 0:HALF_BYTES])
-        load_bytes(w_extra[:], words[:, E - 2 : E, HALF_BYTES : HALF_BYTES + BLOCK_BYTES])
         nc.sync.dma_start(late_rows[:], dy_view[:, :, EARLY_TOKENS:T])
+        load_bytes(w_front[:], words[:, 2 : E - 2, 0:HALF_BYTES])
+        load_bytes(w_key[:], words[:, E - 2 : E, 0:BLOCK_BYTES])
+        load_bytes(w_extra[:], words[:, E - 2 : E, BLOCK_BYTES : LAST * BLOCK_BYTES])
         nc.sync.dma_start(pos1_sb[:], pos1)
         nc.sync.dma_start(pos2_sb[:], pos2)
         load_bytes(w_shared[:], w_words[E, 0])
@@ -158,8 +161,10 @@ def tile_moe_bds_lin_none_kernel(
         def multiply(acc, e, m, codes, scales):
             if e == E:
                 weights = w_shared[:, BLOCK_BYTES * m : BLOCK_BYTES * (m + 1)]
-            elif e >= E - 2 and m == 2:
-                weights = w_extra[:, e - E + 2, :]
+            elif e >= E - 2 and m == 0:
+                weights = w_key[:, e - E + 2, :]
+            elif e >= E - 2 and m < LAST:
+                weights = w_extra[:, e - E + 2, BLOCK_BYTES * (m - 1) : BLOCK_BYTES * m]
             elif e < 2:
                 weights = w_first[:, e, BLOCK_BYTES * m : BLOCK_BYTES * (m + 1)]
             elif m < 2:
@@ -234,11 +239,16 @@ def tile_moe_bds_lin_none_kernel(
         quantize(g_codes, g_scales, slots_woven, S - C, S)
         expert_products(0, SHORT[0], S - C, bank=1)
         nc.vector.tensor_copy(dx[0][:, S - C : S], expert_sums(0, S - C, S, 2))
-        for a, b in ((0, BANK), (BANK, T)):
-            quantize(y_codes, y_scales, tokens_woven, a, b)
+        y_codes.append(chain.tile([P, BANK], U32, name="y_codes1", offset=0, align_bytes=64))
+        for h in range(T // BANK):
+            nc.vector.quantize_mx(
+                out=y_codes[h][:].bitcast(FP8X4),
+                scales=y_scales[:, h * BANK : (h + 1) * BANK],
+                in_=tokens_woven(h * BANK, (h + 1) * BANK),
+            )
         nc.vector.tensor_copy(dx[1][:, SHORT[0] : S], expert_sums(1, SHORT[0], S, 3))
         nc.vector.tensor_copy(dx[2][:, SHORT[0] : S], expert_sums(2, SHORT[0], S, 7))
-        w_back = {2: held.tile([P, E - 4, BLOCK_BYTES], U8, name="w_third", offset=0, align_bytes=64)}
+        w_back = {2: chain.tile([P, E - 4, BLOCK_BYTES], U8, name="w_third", offset=4 * BANK, align_bytes=64)}
         load_bytes(w_back[2][:], words[:, 2 : E - 2, HALF_BYTES : HALF_BYTES + BLOCK_BYTES])
 
         firsts = [ring.tile([P, T], F32, name="first") for m in range(BLOCKS)]
@@ -247,7 +257,7 @@ def tile_moe_bds_lin_none_kernel(
         dx_banks = {2: [2, 1, 7], 3: [0, 4, 1]}
 
         def shared_product(m, t0, bank):
-            multiply(banks[bank][:], E, m, y_codes[:, t0 : t0 + BANK], y_scales[:, t0 : t0 + BANK])
+            multiply(banks[bank][:], E, m, y_codes[t0 // BANK][:], y_scales[:, t0 : t0 + BANK])
 
         def partial(m, a, b):
             t0 = a - a % BANK

@@ -40,7 +40,6 @@ GATE_BLOCKS = S // P
 EARLY_TOKENS = 640
 LAP = 64
 RUN = 4
-FIRST_PIECE = 256
 LAST_PIECE = 128
 HALF_BYTES = 2 * BLOCK_BYTES
 
@@ -115,12 +114,12 @@ def tile_moe_bds_lin_none_kernel(
         for d in range(2, PACK):
             nc.sync.dma_start(planes[d][:], dy_view[:, d, :])
         nc.sync.dma_start(early_rows[:], dy_view[:, :, 0:EARLY_TOKENS])
+        nc.sync.dma_start(late_rows[:], dy_view[:, :, EARLY_TOKENS:T])
         for q in range(4):
             load_bytes(
                 w_sc[32 * q : 32 * q + 4, :, :], w_scales[:, 0, 4 * q : 4 * q + 4, :].rearrange("e f k -> f e k")
             )
         load_bytes(w_first[:], words[:, 0:2, :])
-        nc.sync.dma_start(late_rows[:], dy_view[:, :, EARLY_TOKENS:T])
         load_bytes(w_front[:], words[:, 2 : E - 2, 0:HALF_BYTES])
         load_bytes(w_key[:], words[:, E - 2 : E, 0:BLOCK_BYTES])
         load_bytes(w_extra[:], words[:, E - 2 : E, BLOCK_BYTES : LAST * BLOCK_BYTES])
@@ -279,7 +278,7 @@ def tile_moe_bds_lin_none_kernel(
             nc.vector.tensor_tensor(total[:], partial(m, a, b), term, ADD)
             nc.sync.dma_start(out[P * m : P * (m + 1), a:b], total[:])
 
-        cuts = [[0, BANK, T]] * LAST + [[0, FIRST_PIECE, BANK]]
+        cuts = [[0, BANK, T]] * LAST + [[0, BANK]]
         fetch(firsts[0][:, 0:BANK], pos1_sb, 0, 0, BANK)
         fetch(firsts[0][:, BANK:T], pos1_sb, 0, BANK, T)
         for m in range(BLOCKS):
@@ -304,8 +303,7 @@ def tile_moe_bds_lin_none_kernel(
         ends = [BANK, T - LAST_PIECE, T]
         for a, b in zip(ends, ends[1:]):
             fetch(seconds[:, a - BANK : b - BANK], pos2_sb, LAST, a, b)
-        finish(LAST, 0, FIRST_PIECE, shared_sums(LAST, 0, FIRST_PIECE))
         nc.vector.tensor_tensor(partial(LAST, BANK, T), firsts[LAST][:, BANK:T], shared_sums(LAST, BANK, T), ADD)
-        finish(LAST, FIRST_PIECE, BANK, shared_sums(LAST, FIRST_PIECE, BANK))
+        finish(LAST, 0, BANK, shared_sums(LAST, 0, BANK))
         for a, b in zip(ends, ends[1:]):
             finish(LAST, a, b, seconds[:, a - BANK : b - BANK])

@@ -37,7 +37,8 @@ LONG = (640, 1536)
 SHORT = (1536, 2048)
 GATE_BANKS = {0: 4, LONG[0]: 5, 1024: 6, SHORT[0]: 7}
 GATE_BLOCKS = S // P
-EARLY_TOKENS = 640
+EARLY_TOKENS = 576
+LAST_RUN = 896
 LAP = 64
 RUN = 4
 LAST_PIECE = 128
@@ -72,22 +73,24 @@ def tile_moe_bds_lin_none_kernel(
         w_first = keep.tile([P, 2, 2 * K], U8, name="w_first", align_bytes=64)
         w_front = keep.tile([P, E - 4, HALF_BYTES], U8, name="w_front", align_bytes=64)
         w_key = chain.tile([P, 2, BLOCK_BYTES], U8, name="w_key", offset=4 * BANK - BLOCK_BYTES, align_bytes=64)
-        w_extra = late.tile([P, 2, HALF_BYTES], U8, name="w_extra", offset=4 * BANK - HALF_BYTES, align_bytes=64)
+        w_extra = late.tile([P, 2, HALF_BYTES], U8, name="w_extra", offset=4 * BANK - BLOCK_BYTES, align_bytes=64)
         w_shared = keep.tile([P, 2 * K], U8, name="w_shared", align_bytes=64)
         w_sc = keep.tile([P, E + 1, K], U8, name="w_sc", align_bytes=64)
         dx = [keep.tile([P, S], F32, name=f"dx{m}", tag=f"dx{m}", align_bytes=64) for m in range(BLOCKS)]
         banks = [psum.tile([P, BANK], F32, name=f"bank{b}") for b in range(8)]
         g_scales = keep.tile([P, S], U8, name="g_scales", align_bytes=64)
-        y_codes = [keep.tile([P, BANK], U32, name="y_codes0", align_bytes=64)]
-        y_scales = keep.tile([P, T], U8, name="y_scales", align_bytes=64)
-        woven = keep.tile([P, PACK * T], BF16, name="woven", tag="woven", align_bytes=64)
+        y_codes = keep.tile([P, T], U32, name="y_codes", align_bytes=64)
+        y_scales = [keep.tile([P, BANK], U8, name="y_scales0", align_bytes=64)]
+        woven = keep.tile([P, PACK * (LAST_RUN + C)], BF16, name="woven", tag="woven", align_bytes=64)
 
         def slots_woven(s0, s1):
             if s0 < LONG[0]:
                 return woven[:, PACK * (LAP + s0) : PACK * (LAP + s1)]
             if s0 < T:
                 return woven[:, PACK * s0 : PACK * s1]
-            at = BANK if s0 == SHORT[0] else 0
+            if s0 == S - C:
+                return woven[:, PACK * LAST_RUN :]
+            at = s0 - T
             return back[:, PACK * at : PACK * (at + s1 - s0)]
 
         def tokens_woven(a, b):
@@ -156,6 +159,13 @@ def tile_moe_bds_lin_none_kernel(
 
         def quantize(codes, scales, grouped, a, b):
             nc.vector.quantize_mx(out=codes[:, a:b].bitcast(FP8X4), scales=scales[:, a:b], in_=grouped(a, b))
+
+        def quantize_tokens(h):
+            nc.vector.quantize_mx(
+                out=y_codes[:, h * BANK : (h + 1) * BANK].bitcast(FP8X4),
+                scales=y_scales[h][:],
+                in_=tokens_woven(h * BANK, (h + 1) * BANK),
+            )
 
         def multiply(acc, e, m, codes, scales):
             if e == E:
@@ -227,7 +237,7 @@ def tile_moe_bds_lin_none_kernel(
         gate_slots(long_rows, LONG[0], 1024, LONG[1])
         quantize(g_codes, g_scales, slots_woven, LONG[0], 1024)
         quantize(g_codes, g_scales, slots_woven, 1024, LONG[1])
-        weave_on_gpsimd(tokens_woven(EARLY_TOKENS, T), late_rows[:])
+        weave_on_gpsimd(tokens_woven(EARLY_TOKENS, LAST_RUN), late_rows[:, :, 0 : LAST_RUN - EARLY_TOKENS])
         pair_products(0, 1, bank=4)
         pair_products(1, 1, bank=5)
         pair_products(0, 2, bank=6)
@@ -238,15 +248,12 @@ def tile_moe_bds_lin_none_kernel(
         quantize(g_codes, g_scales, slots_woven, S - C, S)
         expert_products(0, SHORT[0], S - C, bank=1)
         nc.vector.tensor_copy(dx[0][:, S - C : S], expert_sums(0, S - C, S, 2))
-        y_codes.append(chain.tile([P, BANK], U32, name="y_codes1", offset=0, align_bytes=64))
-        for h in range(T // BANK):
-            nc.vector.quantize_mx(
-                out=y_codes[h][:].bitcast(FP8X4),
-                scales=y_scales[:, h * BANK : (h + 1) * BANK],
-                in_=tokens_woven(h * BANK, (h + 1) * BANK),
-            )
+        weave_on_gpsimd(tokens_woven(LAST_RUN, T), late_rows[:, :, LAST_RUN - EARLY_TOKENS :])
+        quantize_tokens(0)
         nc.vector.tensor_copy(dx[1][:, SHORT[0] : S], expert_sums(1, SHORT[0], S, 3))
         nc.vector.tensor_copy(dx[2][:, SHORT[0] : S], expert_sums(2, SHORT[0], S, 7))
+        y_scales.append(late.tile([P, BANK], U8, name="y_scales1", offset=4 * BANK, align_bytes=64))
+        quantize_tokens(1)
         w_back = {2: chain.tile([P, E - 4, BLOCK_BYTES], U8, name="w_third", offset=4 * BANK, align_bytes=64)}
         load_bytes(w_back[2][:], words[:, 2 : E - 2, HALF_BYTES : HALF_BYTES + BLOCK_BYTES])
 
@@ -256,12 +263,12 @@ def tile_moe_bds_lin_none_kernel(
         dx_banks = {2: [2, 1, 7], 3: [0, 4, 1]}
 
         def shared_product(m, t0, bank):
-            multiply(banks[bank][:], E, m, y_codes[t0 // BANK][:], y_scales[:, t0 : t0 + BANK])
+            multiply(banks[bank][:], E, m, y_codes[:, t0 : t0 + BANK], y_scales[t0 // BANK][:])
 
         def partial(m, a, b):
             t0 = a - a % BANK
             if (m, t0) not in partials:
-                partials[m, t0] = late.tile([P, BANK], F32, name=f"partial{m}_{t0}", tag=f"half{t0}", offset=4 * t0)
+                partials[m, t0] = late.tile([P, BANK], F32, name=f"partial{m}_{t0}", tag=f"half{t0}", offset=5 * t0)
             return partials[m, t0][:, a - t0 : b - t0]
 
         def fetch(dst, pos_sb, m, a, b):
@@ -292,9 +299,9 @@ def tile_moe_bds_lin_none_kernel(
             if m < LAST:
                 for a, b in zip(cuts[m + 1], cuts[m + 1][1:]):
                     fetch(firsts[m + 1][:, a:b], pos1_sb, m + 1, a, b)
-                if m + 2 < BLOCKS:
-                    for c in range(1, PAIRS - 1 + m):
-                        pair_products(m + 2, c, dx_banks[m + 2][c - 1])
+                    if a == 0 and m + 2 < BLOCKS:
+                        for c in range(1, PAIRS - 1 + m):
+                            pair_products(m + 2, c, dx_banks[m + 2][c - 1])
                 for t0 in range(0, T, BANK):
                     finish(m, t0, t0 + BANK, shared_sums(m, t0, t0 + BANK))
 

@@ -37,9 +37,11 @@ LONG = (640, 1536)
 SHORT = (1536, 2048)
 GATE_BANKS = {0: 4, LONG[0]: 5, 1024: 6, SHORT[0]: 7}
 GATE_BLOCKS = S // P
-EARLY_TOKENS = 576
-LAST_RUN = 896
-LAP = 64
+EARLY_TOKENS = 384
+LAST_RUN = 768
+LENT = 96
+HANDED = 128
+LAP = 160
 RUN = 4
 LAST_PIECE = 128
 HALF_BYTES = 2 * BLOCK_BYTES
@@ -65,6 +67,7 @@ def tile_moe_bds_lin_none_kernel(
         plain_flat = keep.tile([P, PACK * plain_width], F32, name="plain_flat", align_bytes=64)
         gate_at = 2 * plain_width + 64
         gate_first = plain_flat[:, gate_at : gate_at + GATED[1] - GATED[0]]
+        gate_lent = keep.tile([P, LENT], F32, name="gate_lent")
         gate_rows = keep.tile([P, P], F32, name="gate_rows")
         gate_cols = keep.tile([P, GATE_BLOCKS], F32, name="gate_cols", tag="short", align_bytes=64)
         ident = keep.tile([P, P], F32, name="ident")
@@ -116,6 +119,7 @@ def tile_moe_bds_lin_none_kernel(
         nc.sync.dma_start(gate_rows[:], flat.rearrange("(j c) -> j c", c=P))
         for d in range(2, PACK):
             nc.sync.dma_start(planes[d][:], dy_view[:, d, :])
+        nc.sync.dma_start(gate_lent[:], gate[0:P, LONG[0] : LONG[0] + LENT])
         nc.sync.dma_start(early_rows[:], dy_view[:, :, 0:EARLY_TOKENS])
         nc.sync.dma_start(late_rows[:], dy_view[:, :, EARLY_TOKENS:T])
         for q in range(4):
@@ -217,7 +221,8 @@ def tile_moe_bds_lin_none_kernel(
             column = gate_cols[:, s0 // P : s0 // P + 1].to_broadcast([P, P])
             nc.tensor.transpose(gates_in_psum(s0, s0 + P), column, ident[:])
         short_rows = keep.tile([P, PACK, SHORT[1] - SHORT[0]], F32, name="short_rows", tag="short", align_bytes=64)
-        for d in range(PACK):
+        nc.scalar.activation(short_rows[:, 0, HANDED:], window(0, (SHORT[0] + HANDED, S)), COPY)
+        for d in range(1, PACK):
             nc.scalar.activation(short_rows[:, d, :], window(d, SHORT), COPY)
         for d in range(2, PACK):
             nc.vector.tensor_copy(plain_rows[:, d, :], window(d, PLAIN))
@@ -226,14 +231,21 @@ def tile_moe_bds_lin_none_kernel(
 
         weave_on_gpsimd(slots_woven(GATED[0], GATED[1]), gated_rows[:])
         gate_slots(plain_rows, PLAIN[0], PLAIN[0], PLAIN[1])
+        nc.vector.tensor_copy(short_rows[:, 0, 0:HANDED], window(0, (SHORT[0], SHORT[0] + HANDED)))
         g_codes = held.tile([P, S], U32, name="g_codes", offset=back_bytes, align_bytes=64)
         quantize(g_codes, g_scales, slots_woven, C, LONG[0])
         quantize(g_codes, g_scales, slots_woven, 0, C)
         back = held.tile([P, PACK * (BANK + C)], BF16, name="back", offset=0, align_bytes=64)
+        nc.gpsimd.tensor_tensor(
+            slots_woven(LONG[0], LONG[0] + LENT).rearrange("p (c t) -> p c t", t=PACK),
+            long_rows[:, :, 0:LENT].rearrange("p t c -> p c t"),
+            gate_lent[:].unsqueeze(2).to_broadcast([P, LENT, PACK]),
+            MULT,
+        )
         weave_on_gpsimd(tokens_woven(0, EARLY_TOKENS), early_rows[:])
         for m in range(BLOCKS):
             pair_products(m, 0, bank=m)
-        gate_slots(long_rows, LONG[0], LONG[0], 1024)
+        gate_slots(long_rows, LONG[0], LONG[0] + LENT, 1024)
         gate_slots(long_rows, LONG[0], 1024, LONG[1])
         quantize(g_codes, g_scales, slots_woven, LONG[0], 1024)
         quantize(g_codes, g_scales, slots_woven, 1024, LONG[1])

from contextlib import ExitStack

import concourse.mybir as mybir
from concourse.masks import make_identity

K, T, E, C, N = 512, 1024, 8, 256, 512
S = E * C

F32 = mybir.dt.float32
BF16 = mybir.dt.bfloat16
I32 = mybir.dt.int32
U32 = mybir.dt.uint32
U16 = mybir.dt.uint16
U8 = mybir.dt.uint8
FP8X4 = mybir.dt.float8_e4m3fn_x4
FP4X4 = mybir.dt.float4_e2m1fn_x4
MULT = mybir.AluOpType.mult
ADD = mybir.AluOpType.add
COPY = mybir.ActivationFunctionType.Copy

P = 128
PACK = 4
BANK = 512
PER_COL = 16
BLOCK_BYTES = 2 * P
BLOCKS = K // P

FLOPS = 2 * N * K * (S + T)
BYTES = 4 * N * T + (E + 1) * (N * K // 2 + N * K // 32) + 4 * S + 2 * (S + 2 * T) + 4 * K * T

PAIR = 2 * C
PAIRS = S // PAIR
LAST = BLOCKS - 1
PLAIN = (0, 256)
GATED = (256, 640)
LONG = (640, 1536)
SHORT = (1536, 2048)
GATE_BANKS = {0: 4, LONG[0]: 5, 1024: 6, SHORT[0]: 7}
GATE_BLOCKS = S // P
EARLY_TOKENS = 384
LAST_RUN = 768
LENT = 96
HANDED = 128
LAP = 160
RUN = 4
LAST_PIECE = 128
HALF_BYTES = 2 * BLOCK_BYTES


def tile_moe_bds_lin_none_kernel(
    tc, dyT, w_words, w_scales, gate, offs, pos1, pos2, out
):
    nc = tc.nc
    with ExitStack() as ctx:
        keep = ctx.enter_context(tc.tile_pool(name="keep", bufs=1))
        ring = ctx.enter_context(tc.tile_pool(name="ring", bufs=BLOCKS))
        held = ctx.enter_context(tc.tile_pool(name="held", bufs=1))
        chain = ctx.enter_context(tc.tile_pool(name="chain", bufs=1))
        late = ctx.enter_context(tc.tile_pool(name="late", bufs=1))
        psum = ctx.enter_context(tc.psum_pool(name="psum", bufs=1))

        offs_sb = keep.tile([P, S // PER_COL], U16, name="offs_sb")
        pos1_sb = keep.tile([P, T // PER_COL], U16, name="pos1_sb")
        pos2_sb = keep.tile([P, T // PER_COL], U16, name="pos2_sb")
        planes = [keep.tile([P, T], F32, name=f"plane{d}") for d in range(PACK)]
        plain_width = PLAIN[1] - PLAIN[0]
        plain_flat = keep.tile([P, PACK * plain_width], F32, name="plain_flat", align_bytes=64)
        gate_at = 2 * plain_width + 64
        gate_first = plain_flat[:, gate_at : gate_at + GATED[1] - GATED[0]]
        gate_lent = keep.tile([P, LENT], F32, name="gate_lent")
        gate_rows = keep.tile([P, P], F32, name="gate_rows")
        gate_cols = keep.tile([P, GATE_BLOCKS], F32, name="gate_cols", tag="short", align_bytes=64)
        ident = keep.tile([P, P], F32, name="ident")
        early_rows = keep.tile([P, PACK, EARLY_TOKENS], F32, name="early_rows", align_bytes=64)
        late_rows = keep.tile([P, PACK, T - EARLY_TOKENS], F32, name="late_rows", align_bytes=64)
        w_first = keep.tile([P, 2, 2 * K], U8, name="w_first", align_bytes=64)
        w_front = keep.tile([P, E - 4, HALF_BYTES], U8, name="w_front", align_bytes=64)
        w_key = chain.tile([P, 2, BLOCK_BYTES], U8, name="w_key", offset=4 * BANK - BLOCK_BYTES, align_bytes=64)
        w_extra = late.tile([P, 2, HALF_BYTES], U8, name="w_extra", offset=4 * BANK - BLOCK_BYTES, align_bytes=64)
        w_shared = keep.tile([P, 2 * K], U8, name="w_shared", align_bytes=64)
        w_sc = keep.tile([P, E + 1, K], U8, name="w_sc", align_bytes=64)
        dx = [keep.tile([P, S], F32, name=f"dx{m}", tag=f"dx{m}", align_bytes=64) for m in range(BLOCKS)]
        banks = [psum.tile([P, BANK], F32, name=f"bank{b}") for b in range(8)]
        g_scales = keep.tile([P, S], U8, name="g_scales", align_bytes=64)
        y_codes = keep.tile([P, T], U32, name="y_codes", align_bytes=64)
        y_scales = [keep.tile([P, BANK], U8, name="y_scales0", align_bytes=64)]
        woven = keep.tile([P, PACK * (LAST_RUN + C)], BF16, name="woven", tag="woven", align_bytes=64)

        def slots_woven(s0, s1):
            if s0 < LONG[0]:
                return woven[:, PACK * (LAP + s0) : PACK * (LAP + s1)]
            if s0 < T:
                return woven[:, PACK * s0 : PACK * s1]
            if s0 == S - C:
                return woven[:, PACK * LAST_RUN :]
            at = s0 - T
            return back[:, PACK * at : PACK * (at + s1 - s0)]

        def tokens_woven(a, b):
            return woven[:, PACK * a : PACK * b]

        warm = keep.tile([P, 2], F32, name="warm")
        nc.gpsimd.memset(warm[:, 0:1], 0.0)
        nc.scalar.activation(warm[:, 1:2], warm[:, 0:1], COPY)
        nc.vector.memset(w_sc[:].bitcast(I32), 0)
        make_identity(nc, ident[:])

        dy_view = dyT.rearrange("(p d) x -> p d x", d=PACK)
        words = w_words.rearrange("e a p b -> p (e a) b")

        def load_bytes(dst, src):
            nc.sync.dma_start(dst.bitcast(I32), src.bitcast(I32))

        nc.sync.dma_start(offs_sb[:], offs)
        nc.sync.dma_start(planes[0][:], dy_view[:, 0, :])
        nc.sync.dma_start(gate_first, gate[0:P, GATED[0] : GATED[1]])
        nc.sync.dma_start(planes[1][:], dy_view[:, 1, :])
        flat = gate.rearrange("r s -> (r s)")[0 : P * P]
        nc.sync.dma_start(gate_rows[:], flat.rearrange("(j c) -> j c", c=P))
        for d in range(2, PACK):
            nc.sync.dma_start(planes[d][:], dy_view[:, d, :])
        nc.sync.dma_start(gate_lent[:], gate[0:P, LONG[0] : LONG[0] + LENT])
        nc.sync.dma_start(early_rows[:], dy_view[:, :, 0:EARLY_TOKENS])
        nc.sync.dma_start(late_rows[:], dy_view[:, :, EARLY_TOKENS:T])
        for q in range(4):
            load_bytes(
                w_sc[32 * q : 32 * q + 4, :, :], w_scales[:, 0, 4 * q : 4 * q + 4, :].rearrange("e f k -> f e k")
            )
        load_bytes(w_first[:], words[:, 0:2, :])
        load_bytes(w_front[:], words[:, 2 : E - 2, 0:HALF_BYTES])
        load_bytes(w_key[:], words[:, E - 2 : E, 0:BLOCK_BYTES])
        load_bytes(w_extra[:], words[:, E - 2 : E, BLOCK_BYTES : LAST * BLOCK_BYTES])
        nc.sync.dma_start(pos1_sb[:], pos1)
        nc.sync.dma_start(pos2_sb[:], pos2)
        load_bytes(w_shared[:], w_words[E, 0])

        def runs_out(dst):
            return dst.rearrange("p (c i t) -> p c t i", i=RUN, t=PACK)

        def runs_in(src):
            return src.rearrange("p t (c i) -> p c t i", i=RUN)

        def offsets(lst, a, b):
            return lst[:, a // PER_COL : b // PER_COL]

        def window(d, chunk):
            return planes[d][:].indirect(offsets(offs_sb, chunk[0], chunk[1]))

        def weave_on_gpsimd(dst, src):
            nc.gpsimd.tensor_scalar(
                dst.rearrange("p (c t) -> p c t", t=PACK), src.rearrange("p t c -> p c t"), 1.0, 0.0, op0=MULT, op1=ADD
            )

        def gates_in_psum(s0, s1):
            first = max(s for s in GATE_BANKS if s <= s0)
            return banks[GATE_BANKS[first]][:, s0 - first : s1 - first]

        def gate_and_weave(dst, src, s0, s1):
            gates = gates_in_psum(s0, s1).rearrange("p (c i) -> p c i", i=RUN)
            nc.vector.tensor_tensor(
                runs_out(dst), runs_in(src), gates.unsqueeze(2).to_broadcast([P, (s1 - s0) // RUN, PACK, RUN]), MULT
            )

        def quantize(codes, scales, grouped, a, b):
            nc.vector.quantize_mx(out=codes[:, a:b].bitcast(FP8X4), scales=scales[:, a:b], in_=grouped(a, b))

        def quantize_tokens(h):
            nc.vector.quantize_mx(
                out=y_codes[:, h * BANK : (h + 1) * BANK].bitcast(FP8X4),
                scales=y_scales[h][:],
                in_=tokens_woven(h * BANK, (h + 1) * BANK),
            )

        def multiply(acc, e, m, codes, scales):
            if e == E:
                weights = w_shared[:, BLOCK_BYTES * m : BLOCK_BYTES * (m + 1)]
            elif e >= E - 2 and m == 0:
                weights = w_key[:, e - E + 2, :]
            elif e >= E - 2 and m < LAST:
                weights = w_extra[:, e - E + 2, BLOCK_BYTES * (m - 1) : BLOCK_BYTES * m]
            elif e < 2:
                weights = w_first[:, e, BLOCK_BYTES * m : BLOCK_BYTES * (m + 1)]
            elif m < 2:
                weights = w_front[:, e - 2, BLOCK_BYTES * m : BLOCK_BYTES * (m + 1)]
            else:
                weights = w_back[m][:, e - 2, :]
            nc.tensor.matmul_mx(
                out=acc,
                lhsT=weights.bitcast(FP4X4),
                lhsT_scale=w_sc[:, e, P * m : P * (m + 1)],
                rhs=codes.bitcast(FP8X4),
                rhs_scale=scales,
                start=True,
                stop=True,
            )

        def expert_sums(m, s0, s1, bank):
            for j in sorted(range(s0, s1, C), reverse=s1 == S):
                multiply(banks[bank][:, j - s0 : j - s0 + C], j // C, m, g_codes[:, j : j + C], g_scales[:, j : j + C])
            return banks[bank][:, 0 : s1 - s0]

        def expert_products(m, s0, s1, bank):
            nc.scalar.copy(out=dx[m][:, s0:s1], in_=expert_sums(m, s0, s1, bank))

        def pair_products(m, c, bank):
            expert_products(m, c * PAIR, (c + 1) * PAIR, bank)

        back_bytes = 2 * PACK * (BANK + C)
        gated_rows = held.tile([P, PACK, GATED[1] - GATED[0]], F32, name="gated_rows", offset=back_bytes // 2, align_bytes=64)
        plain_rows = plain_flat[:].rearrange("p (t c) -> p t c", t=PACK)
        long_rows = keep.tile([P, PACK, LONG[1] - LONG[0]], F32, name="long_rows", align_bytes=64)
        nc.vector.tensor_copy(plain_rows[:, 0, :], window(0, PLAIN))
        for d in range(PACK):
            nc.vector.tensor_tensor(gated_rows[:, d, :], window(d, GATED), gate_first, MULT)
            nc.scalar.activation(long_rows[:, d, :], window(d, LONG), COPY)
            if d == 1:
                nc.vector.tensor_copy(plain_rows[:, d, :], window(d, PLAIN))
        nc.tensor.transpose(banks[0][:, 0:P], gate_rows[:], ident[:])
        nc.vector.tensor_copy(gate_cols[:], banks[0][:, 0:GATE_BLOCKS])
        for s0 in [*range(0, PLAIN[1], P), *range(LONG[0], S, P)]:
            column = gate_cols[:, s0 // P : s0 // P + 1].to_broadcast([P, P])
            nc.tensor.transpose(gates_in_psum(s0, s0 + P), column, ident[:])
        short_rows = keep.tile([P, PACK, SHORT[1] - SHORT[0]], F32, name="short_rows", tag="short", align_bytes=64)
        nc.scalar.activation(short_rows[:, 0, HANDED:], window(0, (SHORT[0] + HANDED, S)), COPY)
        for d in range(1, PACK):
            nc.scalar.activation(short_rows[:, d, :], window(d, SHORT), COPY)
        for d in range(2, PACK):
            nc.vector.tensor_copy(plain_rows[:, d, :], window(d, PLAIN))
        def gate_slots(rows, first, s0, s1):
            gate_and_weave(slots_woven(s0, s1), rows[:, :, s0 - first : s1 - first], s0, s1)

        weave_on_gpsimd(slots_woven(GATED[0], GATED[1]), gated_rows[:])
        gate_slots(plain_rows, PLAIN[0], PLAIN[0], PLAIN[1])
        nc.vector.tensor_copy(short_rows[:, 0, 0:HANDED], window(0, (SHORT[0], SHORT[0] + HANDED)))
        g_codes = held.tile([P, S], U32, name="g_codes", offset=back_bytes, align_bytes=64)
        quantize(g_codes, g_scales, slots_woven, C, LONG[0])
        quantize(g_codes, g_scales, slots_woven, 0, C)
        back = held.tile([P, PACK * (BANK + C)], BF16, name="back", offset=0, align_bytes=64)
        nc.gpsimd.tensor_tensor(
            slots_woven(LONG[0], LONG[0] + LENT).rearrange("p (c t) -> p c t", t=PACK),
            long_rows[:, :, 0:LENT].rearrange("p t c -> p c t"),
            gate_lent[:].unsqueeze(2).to_broadcast([P, LENT, PACK]),
            MULT,
        )
        weave_on_gpsimd(tokens_woven(0, EARLY_TOKENS), early_rows[:])
        for m in range(BLOCKS):
            pair_products(m, 0, bank=m)
        gate_slots(long_rows, LONG[0], LONG[0] + LENT, 1024)
        gate_slots(long_rows, LONG[0], 1024, LONG[1])
        quantize(g_codes, g_scales, slots_woven, LONG[0], 1024)
        quantize(g_codes, g_scales, slots_woven, 1024, LONG[1])
        weave_on_gpsimd(tokens_woven(EARLY_TOKENS, LAST_RUN), late_rows[:, :, 0 : LAST_RUN - EARLY_TOKENS])
        pair_products(0, 1, bank=4)
        pair_products(1, 1, bank=5)
        pair_products(0, 2, bank=6)
        pair_products(1, 2, bank=0)
        gate_slots(short_rows, SHORT[0], SHORT[0], S - C)
        gate_slots(short_rows, SHORT[0], S - C, S)
        quantize(g_codes, g_scales, slots_woven, SHORT[0], S - C)
        quantize(g_codes, g_scales, slots_woven, S - C, S)
        expert_products(0, SHORT[0], S - C, bank=1)
        nc.vector.tensor_copy(dx[0][:, S - C : S], expert_sums(0, S - C, S, 2))
        weave_on_gpsimd(tokens_woven(LAST_RUN, T), late_rows[:, :, LAST_RUN - EARLY_TOKENS :])
        quantize_tokens(0)
        nc.vector.tensor_copy(dx[1][:, SHORT[0] : S], expert_sums(1, SHORT[0], S, 3))
        nc.vector.tensor_copy(dx[2][:, SHORT[0] : S], expert_sums(2, SHORT[0], S, 7))
        y_scales.append(late.tile([P, BANK], U8, name="y_scales1", offset=4 * BANK, align_bytes=64))
        quantize_tokens(1)
        w_back = {2: chain.tile([P, E - 4, BLOCK_BYTES], U8, name="w_third", offset=4 * BANK, align_bytes=64)}
        load_bytes(w_back[2][:], words[:, 2 : E - 2, HALF_BYTES : HALF_BYTES + BLOCK_BYTES])

        firsts = [ring.tile([P, T], F32, name="first") for m in range(BLOCKS)]
        partials = {}
        ds_banks = [[0, 4], [5, 6], [3, 2], [7, 0]]
        dx_banks = {2: [2, 1, 7], 3: [0, 4, 1]}

        def shared_product(m, t0, bank):
            multiply(banks[bank][:], E, m, y_codes[:, t0 : t0 + BANK], y_scales[t0 // BANK][:])

        def partial(m, a, b):
            t0 = a - a % BANK
            if (m, t0) not in partials:
                partials[m, t0] = late.tile([P, BANK], F32, name=f"partial{m}_{t0}", tag=f"half{t0}", offset=5 * t0)
            return partials[m, t0][:, a - t0 : b - t0]

        def fetch(dst, pos_sb, m, a, b):
            nc.scalar.activation(dst, dx[m][:].indirect(offsets(pos_sb, a, b)), COPY)

        def add_second(m, a, b):
            nc.vector.tensor_tensor(partial(m, a, b), dx[m][:].indirect(offsets(pos2_sb, a, b)), firsts[m][:, a:b], ADD)

        def shared_sums(m, a, b):
            return banks[ds_banks[m][a // BANK]][:, a % BANK : a % BANK + b - a]

        def finish(m, a, b, term):
            total = ring.tile([P, b - a], F32, name="total", bufs=6)
            nc.vector.tensor_tensor(total[:], partial(m, a, b), term, ADD)
            nc.sync.dma_start(out[P * m : P * (m + 1), a:b], total[:])

        cuts = [[0, BANK, T]] * LAST + [[0, BANK]]
        fetch(firsts[0][:, 0:BANK], pos1_sb, 0, 0, BANK)
        fetch(firsts[0][:, BANK:T], pos1_sb, 0, BANK, T)
        for m in range(BLOCKS):
            for h in range(T // BANK):
                shared_product(m, h * BANK, ds_banks[m][h])
            for a, b in zip(cuts[m], cuts[m][1:]):
                add_second(m, a, b)
            if m == 0:
                w_back[LAST] = keep.tile([P, E - 2, BLOCK_BYTES], U8, name="w_last", tag="dx0", align_bytes=64)
                load_bytes(w_back[LAST][:], words[:, 2:E, LAST * BLOCK_BYTES :])
            if m < LAST:
                for a, b in zip(cuts[m + 1], cuts[m + 1][1:]):
                    fetch(firsts[m + 1][:, a:b], pos1_sb, m + 1, a, b)
                    if a == 0 and m + 2 < BLOCKS:
                        for c in range(1, PAIRS - 1 + m):
                            pair_products(m + 2, c, dx_banks[m + 2][c - 1])
                for t0 in range(0, T, BANK):
                    finish(m, t0, t0 + BANK, shared_sums(m, t0, t0 + BANK))

        fetch(firsts[LAST][:, BANK:T], pos1_sb, LAST, BANK, T)
        seconds = keep.tile([P, T - BANK], F32, name="seconds")
        ends = [BANK, T - LAST_PIECE, T]
        for a, b in zip(ends, ends[1:]):
            fetch(seconds[:, a - BANK : b - BANK], pos2_sb, LAST, a, b)
        nc.vector.tensor_tensor(partial(LAST, BANK, T), firsts[LAST][:, BANK:T], shared_sums(LAST, BANK, T), ADD)
        finish(LAST, 0, BANK, shared_sums(LAST, 0, BANK))
        for a, b in zip(ends, ends[1:]):
            finish(LAST, a, b, seconds[:, a - BANK : b - BANK])
